import numpy as np, ml_dtypes
CORES = [2,3,42,43,82,83,122,123]
N = 8
BF = ml_dtypes.bfloat16
W, Q, CAP, ST, RO = 4096, 512, 192, 2, 2
R = np.arange(16)[:, None]
def hashes(path, node, w):
    u = np.add.accumulate(path * w[..., 0:1], axis=-2); v = np.add.accumulate(path * w[..., 1:2], axis=-2)
    return (((u * v) >> 5) + 37 * node[..., None, :]) & (W - 1)
def begin(node, path):
    return {"L": node, "G": node, "F": node, "P": path, "X": path, "O": path, "done": np.zeros(node.shape, bool), "Z": np.zeros_like(path), "V": np.zeros_like(node)}
def step(A, nk, w, s):
    h = hashes(s["P"], s["L"], w)
    key = (np.take_along_axis(A, h.reshape(N, 8, 1, 16 * Q), 3) & 15).reshape(N, 8, 16, 16, Q)
    differ = (key != s["P"][:, :, :, None, :]) & (R <= R.T)[:, :, None]
    m = R + 1; match = np.sum(differ, axis=2) <= (m >> 2)
    best = np.max(np.where(match, m, 0), axis=2)
    at = np.take_along_axis(h, np.maximum(best - 1, 0)[:, :, None, :], 2)
    Z = np.take_along_axis(A, at, 3) >> 4; x = np.take_along_axis(nk, at[:, :, 0], 2); node, kind = x >> 2, x & 3
    live = ~s["done"]; hit = live & (best > 0); miss = live & (best == 0)
    plain, quoted, nodal, value = hit & (kind == 0), hit & (kind == 1), hit & (kind == 2), hit & (kind == 3)
    q_, m_ = quoted[:, :, None], miss[:, :, None]
    new = np.where(R < best[:, :, None], Z, np.where(q_, s["X"], s["P"]))
    return {"P": np.where((plain | quoted | nodal)[:, :, None], new, np.where(m_, s["X"], s["P"])), "X": np.where((quoted | nodal)[:, :, None], new, s["X"]), "O": s["O"],
            "L": np.where(plain | nodal, node, np.where(quoted | miss, s["G"], s["L"])), "G": np.where(nodal, node, s["G"]), "F": s["F"],
            "done": s["done"] | value, "Z": np.where(value[:, :, None], Z, s["Z"]), "V": np.where(value, node, s["V"])}
def finish(A, nk, w, s, t):
    place = hashes(s["O"], s["F"], w)[:, :, 15]; done = s["done"]; d_ = done[:, :, None]
    for a in range(N):
        for g in range(8):
            v = np.flatnonzero(done[a, g]); c, k = np.unique(place[a, g, v], return_index=True); v = v[k]
            A[a, g][:, c] = s["O"][a, g][:, v] + 16 * s["Z"][a, g][:, v]; nk[a, g, c] = 4 * s["V"][a, g, v] + 3
    O = np.where(d_, (s["O"] + s["Z"]) & 15, s["O"]); F = np.where(done, s["V"], s["F"])
    old = {"P": np.where(d_, O, s["P"]), "X": np.where(d_, O, s["X"]), "O": O, "L": np.where(done, F, s["L"]), "G": np.where(done, F, s["G"]), "F": F}
    new = begin(F, O)
    for x in "PXOLGF": new[x] = np.array(old[x])
    for a in range(N):
        q = (a - 1 - t) % N
        for g in range(8):
            mine = np.flatnonzero(~done[a, g])[:CAP]; come = np.flatnonzero(~done[q, g])[:CAP][:len(mine)]
            here, spare = mine[:len(come)], mine[len(come):]
            for x in "PXOLGF": new[x][a, g][..., here] = old[x][q, g][..., come]
            for x, y in (("P", "O"), ("X", "O"), ("L", "F"), ("G", "F")): new[x][a, g][..., spare] = old[y][a, g][..., spare]
    return new
def sym(rng, *shape):
    return np.where(rng.random(shape) < 0.7, rng.integers(0, 3, shape), rng.integers(0, 16, shape))
def start(rng):
    A = (sym(rng, N, 8, 16, W) + 16 * sym(rng, N, 8, 16, W)).astype(np.int32)
    nk = 4 * rng.integers(0, 1024, (N, 8, W)) + rng.choice(np.array([0, 0, 0, 1, 1, 2, 2, 3, 3, 3]), (N, 8, W))
    return A, nk, rng.integers(1, 18, (N, 8, 16, 2)), rng.integers(0, 1024, (N, 8, Q)), sym(rng, N, 8, 16, Q)
def plant(rng, A, nk, w, s, used, share, lens, vals, fam, edge):
    h = hashes(s["P"], s["L"], w)
    for a in range(N):
        for g in range(8):
            lane = np.flatnonzero(~s["done"][a, g] & (rng.random(Q) < share[a, g])); m = rng.choice(lens, lane.size); c = h[a, g, m - 1, lane]
            keep = ~used[a, g, c]; lane, m, c = lane[keep], m[keep], c[keep]; used[a, g, c] = True; n = lane.size
            low = R < m; r = np.where(low, rng.random((16, n)), 2.0); order = np.argsort(np.argsort(r, axis=0), axis=0)
            ch = (m >> 2) + rng.integers(0, 2, n) if edge else (rng.random(n) * ((m >> 2) + 1)).astype(np.int64)
            p = s["P"][a, g][:, lane]; col = A[a, g][:, c]
            key = np.where(low, np.where(order < ch, (p + 1 + rng.integers(0, 15, (16, n))) & 15, p), col & 15)
            z = col >> 4; node = nk[a, g, c] >> 2; kind = np.where(rng.random(n) < vals, 3, nk[a, g, c] & 3)
            other = (lane + fam * rng.integers(0, Q // fam, n)) % Q if fam else rng.integers(0, Q, n)
            lead = (kind == 3) & (rng.random(n) < (0.9 if fam else 0.5)); O = s["O"][a, g]
            z = np.where(lead, (O[:, other] - O[:, lane]) & 15, z); node = np.where(lead, s["F"][a, g, other], node)
            A[a, g][:, c] = key + 16 * z; nk[a, g, c] = 4 * node + kind
def walk(rng, A, nk, w, qn, qp, share, lens, vals=0.0, fam=0, edge=False, used=None):
    s = begin(qn, qp); used = np.zeros((N, 8, W), bool) if used is None else used
    for k in range(ST):
        plant(rng, A, nk, w, s, used, share, lens, vals, fam, edge)
        if k < ST - 1: s = step(A, nk, w, s)
def pack(A, nk, w, qn, qp):
    return {"sen": A.reshape(N, 128, W).astype(np.float32).astype(BF), "nk": nk.astype(np.int32), "wt": np.ascontiguousarray(w.reshape(N, 128, 2)).astype(np.int32),
            "qn": qn.astype(np.int32), "qp": qp.reshape(N, 128, Q).astype(np.float32).astype(BF)}
def setup_inputs(rng):
    A, nk, w, qn, qp = start(rng)
    walk(rng, A, nk, w, qn, qp, rng.choice(np.array([0.3, 0.6, 0.9]), (N, 8)), np.arange(1, 17))
    return pack(A, nk, w, qn, qp)
def setup_inputs_alike(rng):
    A, nk, w, qn, qp = start(rng)
    for a in range(N):
        for g in range(8):
            o = rng.integers(0, 1 if g % 2 == 0 else 3, Q); qn[a, g] = qn[a, g, o]; qp[a, g] = qp[a, g][:, o]
            if g < 6:
                h = hashes(qp[a, g], qn[a, g], w[a, g])[15]; A[a, g][:, h] = qp[a, g] + 16 * (A[a, g][:, h] >> 4); nk[a, g, h] = 4 * (nk[a, g, h] >> 2) + (a + g) % 4
    J = Q // 8; O = rng.integers(0, 16, (N, 16, J)); F = rng.integers(0, 1024, (N, J)); Y = rng.integers(0, 16, (N, 16, J)); E = rng.integers(0, 1024, (N, J))
    for a in range(N):
        b = (a + 1) % N; o = rng.integers(0, J, Q); own = rng.permutation(Q) < Q // 2
        qp[a, 6] = np.where(own, O[a][:, o], O[b][:, o]); qn[a, 6] = np.where(own, F[a, o], F[b, o])
        for path, node, z, to, kind in ((O[b], F[b], Y[b], E[b], 2), (Y[b], E[b], Y[b], E[b], 2), (Y[a], E[a], rng.integers(0, 16, (16, J)), rng.integers(0, 1024, J), 3), (O[a], F[a], np.zeros_like(O[a]), F[a], 3)):
            c = hashes(path, node, w[a, 6])[15]; A[a, 6][:, c] = path + 16 * z; nk[a, 6, c] = 4 * to + kind
    return pack(A, nk, w, qn, qp)
def setup_inputs_ends(rng):
    A, nk, w, qn, qp = start(rng); w[:, 3] = 17; w[:, 4] = 1; used = np.zeros((N, 8, W), bool); used[:, :, 0] = True; used[:, :, W - 1] = True
    nk = np.where(rng.random(nk.shape) < 0.5, 4 * rng.choice(np.array([0, 1023]), nk.shape) + (nk & 3), nk)
    qn = np.where(rng.random(qn.shape) < 0.3, rng.choice(np.array([0, 1023]), qn.shape), qn)
    i3 = np.indices((16, 16, 16)).reshape(3, -1); inv = pow(37, -1, W)
    qn[:, :, 0] = 0; qp[:, :, :, 0] = 0; qn[:, :, 1] = 1023; qp[:, :, :, 1] = 15
    qp[:, :, :, 2:10] = 0; qp[:, 3, :, 10:34] = 15
    for a in range(N):
        for g in range(8):
            A[a, g, :, 0] = 16 * rng.integers(0, 16, 16); nk[a, g, 0] = 4 * (nk[a, g, 0] >> 2) + (a + g) % 4
            z = 1 + rng.permutation(64)[:8]; c = 37 * z; qn[a, g, 2:10] = z
            A[a, g][:, c] = 0; nk[a, g, c] = 4 * rng.integers(0, 1024, 8) + (np.arange(8) + a + g) % 4; used[a, g, c] = True
            if g == 3:
                qn[a, g, 10:34] = rng.permutation(np.arange(1000, 1024)); c = hashes(qp[a, g], qn[a, g], w[a, g])[15, 10:34]
                A[a, g][:, c] = 15 + 16 * rng.integers(0, 16, (16, 24)); nk[a, g, c] = 4 * rng.integers(0, 1024, 24) + 2 + np.arange(24) % 2; used[a, g, c] = True
            u = np.sum(w[a, g, :3, 0:1] * i3, axis=0); v = np.sum(w[a, g, :3, 1:2] * i3, axis=0)
            node = ((W - 1 - ((u * v) >> 5)) * inv) & (W - 1); ok = np.flatnonzero(node < 1024)
            if ok.size:
                k = rng.choice(ok); qp[a, g, :, Q - 1] = 0; qp[a, g, :3, Q - 1] = i3[:, k]; qn[a, g, Q - 1] = node[k]
                A[a, g, :, W - 1] = qp[a, g, :, Q - 1] + 16 * rng.integers(0, 16, 16); nk[a, g, W - 1] = 4 * (nk[a, g, W - 1] >> 2) + (a + g + 1) % 4
    walk(rng, A, nk, w, qn, qp, np.full((N, 8), 0.9), np.array([1, 3, 4, 7, 8, 11, 12, 15, 16]), edge=True, used=used)
    return pack(A, nk, w, qn, qp)
def setup_inputs_room(rng):
    A, nk, w, qn, qp = start(rng); few = rng.random(A.shape) < 0.7
    A = (np.where(few, rng.integers(0, 3, A.shape), rng.integers(0, 8, A.shape)) + 16 * rng.integers(0, 8, A.shape)).astype(np.int32)
    nk = 4 * (nk >> 2) + rng.integers(0, 3, nk.shape); qp = np.where(rng.random(qp.shape) < 0.7, rng.integers(0, 3, qp.shape), rng.integers(0, 8, qp.shape))
    want = rng.choice(np.array([0, 1, CAP - 1, CAP, CAP + 1, Q - 256, Q]), (N, 8)); want[0] = (CAP, CAP + 1, Q, CAP - 1, 1, 0, CAP, CAP); want[1] = (CAP, CAP, 0, CAP + 1, Q, CAP, 1, CAP - 1)
    want[2, 3] = Q - 256; want[2, 5] = 0
    for a in range(N):
        for g in range(8):
            n = Q - int(want[a, g])
            if n == 0: continue
            w[a, g] = rng.integers(5, 18, (1, 2))
            p = rng.integers(8, 16, (16, 4 * Q)); i = rng.integers(0, 15, 4 * Q)
            p[i, np.arange(4 * Q)] = 8 + (p[15] + rng.integers(1, 8, 4 * Q)) % 8; node = rng.integers(0, 1024, 4 * Q); h = hashes(p, node, w[a, g])
            k = np.unique(h[14], return_index=True)[1]; k = k[np.unique(h[15, k], return_index=True)[1]]
            k = np.resize(rng.permutation(k), n); up = rng.permutation(Q)[:n]; c = h[14, k]
            z = np.zeros((16, n), np.int64); gap = p[i[k], k] - p[15, k]; z[15] = gap & 15; z[i[k], np.arange(n)] = (-gap) & 15
            qp[a, g][:, up] = p[:, k]; qn[a, g, up] = node[k]; A[a, g][:, c] = p[:, k] + 16 * z; nk[a, g, c] = 4 * node[k] + 3
    return pack(A, nk, w, qn, qp)
def setup_inputs_spread(rng):
    A, nk, w, qn, qp = start(rng); A = rng.integers(0, 256, A.shape).astype(np.int32); nk = rng.integers(0, 4096, nk.shape)
    w = np.minimum(np.exp2(4.2 * rng.random(w.shape)).astype(np.int64), 17); qn = np.minimum(np.exp2(10 * rng.random(qn.shape)).astype(np.int64) - 1, 1023)
    qp = np.minimum((np.exp2(4.5 * rng.random((N, 8, 1, Q))) * rng.random(qp.shape)).astype(np.int64), 15)
    walk(rng, A, nk, w, qn, qp, np.full((N, 8), 0.7), np.arange(1, 17))
    return pack(A, nk, w, qn, qp)
def setup_inputs_ties(rng):
    A, nk, w, qn, qp = start(rng); fam = Q // 16; w = np.ascontiguousarray(np.broadcast_to(rng.integers(1, 18, (N, 8, 1, 2)), w.shape))
    qn = np.tile(rng.integers(0, 1024, (N, 8, fam)), (1, 1, 16)); base = np.tile(rng.integers(0, 16, (N, 8, 16, fam)), (1, 1, 1, 16))
    i = rng.integers(0, 16, (N, 8, 1, Q)); j = (i + 1 + rng.integers(0, 15, i.shape)) % 16
    qp = np.take_along_axis(base, np.where(R == i, j, np.where(R == j, i, R)), 2)
    walk(rng, A, nk, w, qn, qp, np.full((N, 8), 0.9), np.arange(4, 16), vals=0.8, fam=fam)
    o = np.arange(Q).reshape(16, fam).T.reshape(-1); qn[:, 1::2] = qn[:, 1::2][..., o]; qp[:, 1::2] = qp[:, 1::2][..., o]
    return pack(A, nk, w, qn, qp)
def check_inputs(d):
    bad = []
    for k, hi, lo in (("sen", 255, 0), ("nk", 4095, 0), ("wt", 17, 1), ("qn", 1023, 0), ("qp", 15, 0)):
        x = np.asarray(d[k]).astype(np.float64)
        if not (np.all(x >= lo) and np.all(x <= hi) and np.all(x == np.floor(x))): bad.append("range of " + k)
    return bad
def reference(sen, nk, wt, qn, qp):
    A = sen.astype(np.float32).astype(np.int32).reshape(N, 8, 16, W); kn = nk.astype(np.int64); w = wt.astype(np.int64).reshape(N, 8, 16, 2)
    s = begin(qn.astype(np.int64), qp.astype(np.float32).astype(np.int64).reshape(N, 8, 16, Q))
    for t in range(RO):
        for k in range(ST): s = step(A, kn, w, s)
        s = finish(A, kn, w, s, t)
    return {"yp": np.concatenate([s["P"], s["X"]], axis=3).reshape(N, 128, 2 * Q).astype(np.float32).astype(BF), "yn": np.concatenate([s["L"], s["G"]], axis=2).astype(np.float32)}

@@ -1,0 +1,833 @@
+from concourse.mybir import AluOpType, ActivationFunctionType
+
+AL = AluOpType
+AF = ActivationFunctionType
+W, Q, CAP, NRANK = 4096, 512, 192, 8
+CUTS = [0, 160, 352, 512]
+SUB = 2
+SCH = 32
+SQ = 24
+PACKS = [(12, 4), (11, 5), (10, 6), (9, 7)]
+PLAIN = [16, 15, 14, 13, 8]
+TAB, EXT, DUM = 256, 4352, 4608
+BIG = 8192.0
+CY, PECY, GATH, SCAT, LAT, FIX = 1.0, 0.5, 1.5, 3.5, 120.0, 60.0
+LEAD, STRETCH, WIN, SHY, LOW, TURNS, BWIN = 128, 0.5, 40.0, 100.0, 5000.0, 6, 40.0
+
+MATS = ["I", "NI", "I16", "IM16", "IM9", "IC", "IH", "I2K", "J", "BD", "TRI", "TRI2", "SEL", "TRK", "WU", "WV", "T1"]
+for _x in "ABPC":
+    MATS += [_x + str(_a) for _a, _b in PACKS]
+WIDE = ["E"] + ["CW%d" % _m for _m in range(1, 17)]
+GM = ["QH", "NL0", "D1", "D2", "D3", "DP", "NS1", "PLA", "NL1", "NS2", "NDR", "NDF", "NRS", "YO"]
+GW = ["WB", "WHV", "WXS", "WL", "WX", "WPL", "W8"]
+MOFF = {}
+GMW = VMW = 0
+for _n in GM + GW:
+    MOFF[_n] = ("gm", GMW)
+    GMW += 128 if _n in GM else 144
+for _n in MATS + WIDE:
+    MOFF[_n] = ("vm", VMW)
+    VMW += 128 if _n in MATS else 144
+
+SCRATCH = {}
+for _d, _l in (("bfloat16", (("gm", GMW), ("vm", VMW), ("row", 768), ("iow", 176), ("iog", 128), ("i256", 256), ("iq", 1024),
+                             ("ones", Q), ("q16", 32), ("raw", W), ("kt", 5120), ("zt", 4864), ("nt", 5376), ("ft", 2560),
+                             ("qpi", Q), ("qh", 2 * Q), ("sw0", 2624), ("sw1", 3456), ("nd0", Q), ("nd1", Q), ("nd2", Q),
+                             ("nw0", 1232), ("nw1", 1232), ("sb0", 1616), ("sb1", 1616), ("ns", 2 * Q), ("rr", 2 * Q),
+                             ("gk", 16 * Q), ("ne", 9 * Q), ("mt", Q), ("lt", Q), ("ab", 2 * Q), ("ee", W), ("du", Q),
+                             ("wn", Q), ("lv", 256), ("ld", Q), ("un", 64), ("zv", 2 * Q), ("re2", Q), ("ys", 2 * Q))),
+               ("float32", (("qfm", 128), ("cc", 64), ("mk", 32), ("iof", 32), ("st", Q), ("qf", Q), ("ue", Q), ("xf", Q),
+                            ("pa", Q), ("pb", 128), ("kp", 128), ("sm", 256), ("w4", 256), ("pr", 256), ("t4", 384), ("yq", Q))),
+               ("int32", (("pi", 8), ("nki", 1024), ("wti", 8), ("qni", Q), ("xi", 2 * Q))),
+               ("uint16", (("hu", Q), ("hb", 32), ("ob", 32), ("ov", 32), ("po", 32), ("ol", 32), ("ow", 32), ("of", 128))),
+               ("float16", (("hs", 2 * Q), ("tm", Q)))):
+    for _n, _c in _l:
+        SCRATCH[_n] = ("sbuf", [128, _c], _d)
+for _b in range(8):
+    SCRATCH["ps%d" % _b] = ("psum", [128, 512], "float32")
+SEMAPHORES = ["cV", "cS", "cP", "cG", "l_qp", "l_wt", "l_qn", "l_nk", "l_s0", "l_s1", "l_s2", "l_s3", "l_nt", "z_a", "z_b",
+              "o_p", "o_n", "in00", "in01", "in10", "in11", "out00", "out01", "out10", "out11"]
+SIZE = {"bfloat16": 2, "float16": 2, "uint16": 2, "float32": 4, "int32": 4}
+
+
+def A(name, c0, c1, st=1, p0=0, p1=128, ps=1):
+    return (name, c0, c1, st, p0, p1, ps)
+
+
+def IND(win, off):
+    return ("#", win, off)
+
+
+def M(name, rows=128, cols=128):
+    b, c = MOFF[name]
+    return A(b, c, c + cols, 1, 0, rows)
+
+
+def MW(name, r, rows=128):
+    b, c = MOFF[name]
+    return A(b, c + 15 - r, c + 143 - r, 1, 0, rows)
+
+
+def cols(ap):
+    if ap[0] == "#":
+        return 16 * cols(ap[2])
+    return len(range(ap[1], ap[2], ap[3]))
+
+
+def is_ap(x):
+    return isinstance(x, tuple)
+
+
+def width(ap):
+    if ap[0][0] in "#@":
+        return 4
+    return SIZE[SCRATCH[ap[0]][2]]
+
+
+def graph():
+    ops = []
+
+    def add(eng, kind, outs, ins, args, cost, sem=None, lat=0.0):
+        ops.append({"eng": eng, "kind": kind, "outs": outs, "ins": ins, "args": args, "cost": cost, "sem": sem, "lat": lat})
+
+    def vcost(out, in0, per):
+        if out[0] == "#":
+            return FIX + cols(out) * SCAT * CY
+        if in0[0] == "#":
+            return FIX + cols(out) * GATH * CY
+        return FIX + max(64, cols(out) * per) * CY
+
+    def ts(out, in0, s1, s2, op0, op1=None):
+        per = 0.5 if width(out) == 2 and width(in0) == 2 else 1
+        add("V", "ts", [out], [in0] + [s for s in (s1, s2) if is_ap(s)], (out, in0, s1, s2, op0, op1), vcost(out, in0, per))
+
+    def tt(out, in0, in1, op):
+        per = 1 if "@" in (in0[0][0], in1[0][0]) else 2
+        add("V", "tt", [out], [in0, in1], (out, in0, in1, op), vcost(out, in0, per))
+
+    def cp(out, in0):
+        per = 0.5 if width(out) == 2 and width(in0) == 2 else 1
+        add("V", "cp", [out], [in0], (out, in0), vcost(out, in0, per))
+
+    def ms(out, val):
+        add("V", "ms", [out], [], (out, val), FIX + max(64, cols(out) * width(out) / 4) * CY)
+
+    def act(out, in0, func=AF.Identity, bias=0.0, scale=1.0):
+        add("S", "act", [out], [in0] + [s for s in (bias, scale) if is_ap(s)], (out, in0, func, bias, scale), vcost(out, in0, 1))
+
+    def either(out, in0, bias=0.0, scale=1.0, sign=False):
+        act(out, in0, AF.Sign if sign else AF.Identity, bias, scale)
+        a = ops.pop()
+        if sign:
+            ts(out, in0, 0.5, None, AL.is_ge)
+        elif scale != 1.0:
+            ts(out, in0, scale, None, AL.mult)
+        elif bias != 0.0:
+            ts(out, in0, bias, None, AL.add)
+        else:
+            cp(out, in0)
+        b = ops.pop()
+        a["alt"] = [(x["eng"], x["kind"], x["args"], x["cost"]) for x in (a, b)]
+        a["eng"] = "?"
+        ops.append(a)
+
+    def mm(out, terms, first=True, last=True, after=()):
+        for i, (l, r) in enumerate(terms):
+            o = out[i] if isinstance(out, list) else out
+            c = max(min(64, cols(l)), cols(r)) * PECY * (4 if width(r) == 4 else 1) + 10
+            add("P", "mm", [o], [l, r] + list(after), (o, l, r, first and i == 0, last and i == len(terms) - 1), c)
+
+    def iota(out, pat, base, cm):
+        add("G", "iota", [out], [], (out, pat, base, cm), 160 + 2 * cols(out) * CY)
+
+    def put(ap, pat, base, val):
+        add("G", "put", [ap], [ap], (ap, pat, base, val), 210 + 2 * cols(ap) * CY)
+
+    def keep(out, in0, pat, cm):
+        add("G", "keep", [out], [in0], (out, in0, pat, cm), 210 + 2 * cols(out) * CY)
+
+    def ent(name, k, c, val):
+        b, o = MOFF[name]
+        put(A(b, o + c, o + 128, 16), [[-16, 8]], -k, val)
+
+    def entrow(name, k, val):
+        put(M(name), [[-16, 8], [0, 16]], -k, val)
+
+    def dma(eng, out, in0, sem, ns):
+        add(eng, "dma", [out] if is_ap(out) else [], [in0] if is_ap(in0) else [], (out, in0), 60.0, sem, ns)
+
+    nps = [0]
+
+    def tile():
+        nps[0] += 1
+        return "@%d" % nps[0]
+
+    def narrow(out, wide, src, c0, c1, more=(), rows=128):
+        mm(out, [(MW(wide, r, rows), A(src, c0 + r, c1, 16, 0, rows)) for r in range(16)] + list(more))
+
+    col = lambda i: A("cc", i, i + 1)
+    mkc = lambda m: A("mk", m, m + 1)
+    PC, KC, GB, JC, G15, THR, S1, BH, SC1, DUMC = [col(i) for i in range(10)]
+    W0, W1 = col(12), col(13)
+    io = A("iow", 16, 144)
+
+    dma("Y", A("qpi", 0, Q), "qp", "l_qp", 2200)
+    dma("S", A("raw", 0, 1024), ["sen", 0, 1024], "l_s0", 2600)
+    dma("Y", A("wti", 0, 2), "wt", "l_wt", 2000)
+    dma("S", A("raw", 1024, 2048), ["sen", 1024, 2048], "l_s1", 3300)
+    dma("Y", A("qni", 0, Q, 1, 0, 8), "qn", "l_qn", 2200)
+    dma("Y", A("raw", 2048, 3072), ["sen", 2048, 3072], "l_s2", 4000)
+    dma("Y", A("raw", 3072, 4096), ["sen", 3072, 4096], "l_s3", 4700)
+    dma("Y", A("nki", 0, 256), "nk", "l_nk", 5000)
+
+    iota(A("pi", 0, 1), [[0, 1]], 0, 1)
+    iota(A("iow", 0, 176), [[1, 176]], -16, 0)
+    iota(A("iog", 0, 128), [[16, 8], [0, 16]], 0, 0)
+    iota(A("iof", 0, 32), [[1, 32]], 0, 0)
+    ms(A("gm", 0, 256), 0.0)
+    ms(A("qfm", 0, 128, 1, 0, 8), 0.0)
+    ms(A("ee", 0, 1152), 0.0)
+    b, o = MOFF["CW1"]
+    for x in (A("gm", 256, 1280), A(b, o, o + 1152), A(b, o + 1152, o + 2304), A("gm", 1792, GMW), A("gm", 1280, 1792)):
+        dma("Y", x, A("ee", 0, cols(x)), "z_a", 2500)
+    ms(A("ones", 0, Q), 1.0)
+    ts(A("pi", 1, 2), A("pi", 0, 1), 15, None, AL.bitwise_and)
+    cp(A("cc", 0, 2), A("pi", 0, 2))
+    act(GB, KC, AF.Identity, PC, -1.0)
+    ts(A("mk", 0, 17), A("iof", 0, 17), KC, None, AL.is_gt)
+    ts(M("I"), io, PC, None, AL.is_equal)
+    ts(M("BD"), A("iog", 0, 128), GB, None, AL.is_equal)
+    keep(M("TRI"), M("BD"), [[1, 128]], -1)
+    cp(A("cc", 12, 14), A("wti", 0, 2))
+    ts(M("WU"), M("TRI"), W0, 16.0, AL.mult, AL.mult)
+    ts(M("WV"), M("TRI"), W1, 16.0, AL.mult, AL.mult)
+    for nm, v in (("I16", 1 / 16), ("IM16", -16.0), ("NI", -1.0), ("IM9", -10.0), ("IC", BIG), ("IH", -0.5), ("I2K", -2048.0), ("T1", -BIG)):
+        act(M(nm), M("I"), AF.Identity, 0.0, v)
+    act(G15, GB, AF.Identity, 15.0)
+    act(JC, KC, AF.Identity, G15, -1.0)
+    ts(M("J"), io, JC, None, AL.is_equal)
+    b, o = MOFF["E"]
+    ts(A(b, o, o + 144), A("iow", 16, 160), G15, None, AL.is_equal)
+    b, o = MOFF["CW1"]
+    x = A(b, o + 15, o + 2304, 16)
+    iota(x, [[0, 144]], 1, 0)
+    keep(x, x, [[0, 16], [-16, 9]], 1)
+    keep(x, x, [[1, 16], [16, 9]], -1)
+    for i, (a, s) in enumerate(PACKS):
+        act(M("A%d" % a), M("I"), AF.Identity, 0.0, mkc(a))
+        act(M("B%d" % a), M("J"), AF.Identity, 0.0, mkc(s))
+        act(col(20 + i), mkc(a), AF.Identity, GB, float(a - s))
+        ts(M("C%d" % a), A("iow", 17 - s, 145 - s), col(20 + i), None, AL.is_equal)
+    p = tile()
+    for i, (a, s) in enumerate(PACKS):
+        mm(A(p, 128 * i, 128 * i + 128), [(M("I"), M("A%d" % a)), (M("I"), M("B%d" % a))])
+    act(M("P%d" % PACKS[0][0], 128, 512), A(p, 0, 512))
+    p = tile()
+    mm(A(p, 0, 128), [(M("I"), M("BD")), (M("I"), M("I")), (M("NI"), M("TRI"))])
+    mm(A(p, 128, 256), [(M("IC"), M("I")), (M("IC"), M("TRI")), (M("T1"), M("BD"))])
+    mm(A(p, 256, 384), [(M("I"), M("TRI")), (M("NI"), M("BD")), (M("I"), M("I2K"))])
+    act(M("TRI2", 128, 384), A(p, 0, 384))
+    ts(A("pi", 2, 3), A("pi", 1, 2), 1, None, AL.add)
+    ts(A("pi", 3, 4), A("pi", 2, 3), 2, None, AL.arith_shift_right)
+    cp(THR, A("pi", 3, 4))
+    act(S1, mkc(3), AF.Identity, THR, -BIG)
+    act(BH, mkc(8), AF.Identity, 1.0, -1.0)
+    act(SC1, KC, AF.Identity, 1.0)
+    ts(DUMC, KC, 14.0, mkc(8), AL.is_equal, AL.add)
+    act(A("q16", 0, 32), A("iof", 0, 32), AF.Identity, 0.0, 16.0)
+    ts(A("cc", 32, 40), A("q16", 0, 8), GB, None, AL.is_equal)
+    act(A("cc", 40, 48), A("cc", 32, 40), AF.Identity, 0.0, -1.0)
+    act(A("st", 0, 32), A("q16", 0, 32), AF.Identity, KC)
+    act(A("st", 32, 64), A("st", 0, 32), AF.Identity, float(DUM))
+    act(A("st", 64, 96), A("st", 0, 32), AF.Identity, 512.0 - 2047.0)
+    for x in (A("row", 128, 768), A("kt", W, 5120), A("nt", EXT + Q, 5376), A("sb0", 576, 1616), A("sb1", 576, 1616)):
+        dma("Y", x, A("ee", 0, cols(x)), "z_b", 2500)
+    for o, c, v in ((128, 10, 1.0), (256, 11, 1.0), (384, 12, 0.125), (512, 13, 1.0), (640, 12, 17.0), (640, 4, 1.0), (640, 5, 1.0), (640, 15, 1.0)):
+        put(A("row", o + c, o + 128, 16, 0, 1), [[0, 8]], 0, v)
+    R1 = lambda o: A("row", o, o + 128, 1, 0, 1)
+    b, o = MOFF["QH"]
+    for c in (0, 2, 4):
+        put(A("qfm", c + 1, 128, 16, 0, 8), [[-1, 8]], 0, 1.0)
+        put(A(b, o + c, o + 128, 16, 0, 8), [[-1, 8]], 0, 1.0)
+        put(A(b, o + c + 1, o + 128, 16, 0, 8), [[-1, 8]], 0, -32.0)
+    entrow("NL0", 4, -93184.0)
+    entrow("NL0", 5, 1184.0)
+    for m in (1, 2, 3):
+        for k in range(m):
+            ent("D%d" % m, k, m - 1, float(32 ** k))
+            ent("DP", k, m - 1, float(32 ** k))
+    iota(A("i256", 0, 256), [[1, 256]], 0, 0)
+    for k, c, v in ((2, 0, 1), (3, 1, 1), (2, 2, 1), (3, 3, 1), (8, 6, -1)):
+        ent("NS1", k, c, float(v))
+    ent("WPL", 15, 15, 1.0)
+    entrow("PLA", 15, 1.0)
+    for k, c, v in ((2, 0, 1), (10, 0, 1), (3, 1, 1), (11, 1, 1), (2, 2, 1), (10, 2, 1), (3, 3, 1), (11, 3, 1), (12, 4, 1), (13, 5, 1),
+                    (14, 6, 1), (14, 7, 1), (15, 12, -1), (15, 13, -1)):
+        ent("NS2", k, c, float(v))
+    for k, v in ((0, -93184.0), (8, -93184.0), (1, 1184.0), (9, 1184.0)):
+        entrow("NL1", k, v)
+    ent("WB", 6, 15, 512.0)
+    iota(A("iq", 0, Q, 1, 0, 1), [[1, 16], [0, 32]], 0, 0)
+    iota(A("iq", Q, 2 * Q, 1, 0, 1), [[0, 16], [1, 32]], 0, 0)
+    for k, c in ((0, 4), (8, 4), (1, 5), (9, 5), (2, 2), (10, 2), (3, 3), (11, 3), (14, 6), (7, 6)):
+        ent("NDR", k, c, 1.0)
+    b, o = MOFF["W8"]
+    put(A(b, o + 15, o + 128, 16, 0, 8), [[-1, 8]], 0, 1.0)
+    ent("NDF", 0, 0, 1.0)
+    ent("NDF", 1, 1, 1.0)
+    for k, v in ((4, 256.0), (5, 1.0), (12, 256.0), (13, 1.0)):
+        ent("WHV", k, 15, v)
+    for nm, k, v in (("WL", 10, 32.0), ("WL", 11, 1.0), ("WX", 10, 32.0), ("WX", 11, 1.0), ("WX", 6, 512.0), ("WXS", 14, 512.0), ("WXS", 7, 512.0)):
+        ent(nm, k, 15, v)
+    for c in (0, 2, 4):
+        for k in (0, 8):
+            ent("NRS", k, c, 1.0)
+            ent("NRS", k + 1, c + 1, 1.0)
+    b, o = MOFF["YO"]
+    for j, k, v in ((0, 4, 32.0), (0, 5, 1.0), (1, 2, 32.0), (1, 3, 1.0)):
+        put(A(b, o + j, o + 16, 2), [[-16, 8]], -k, v)
+
+    ts(A("sw0", 1600, 2112), A("qpi", 0, Q), 1 / 16, None, AL.mult)
+    cp(A("qf", 0, Q, 1, 0, 8), A("qni", 0, Q, 1, 0, 8))
+    act(A("qh", 0, Q, 1, 0, 8), A("qf", 0, Q, 1, 0, 8), AF.Identity, 129 - 15.5 / 32, 1 / 32)
+    ts(A("qh", Q, 2 * Q, 1, 0, 8), A("qh", 0, Q, 1, 0, 8), -129.0, None, AL.add)
+    p = tile()
+    mm(A(p, 0, Q), [(A("qfm", 0, 128, 1, 0, 8), A("qf", 0, Q, 1, 0, 8)), (M("QH", 8), A("qh", Q, 2 * Q, 1, 0, 8))])
+    act(A("nd0", 0, Q), A(p, 0, Q), AF.Identity, BH)
+
+    for j in range(8):
+        c0, c1 = 512 * j, 512 * j + 512
+        ts(A("zt", TAB + c0, TAB + c1), A("raw", c0, c1), 1 / 256, 9 - 7.5 / 256, AL.mult, AL.add)
+        p = tile()
+        mm(A(p, 0, Q), [(M("I16"), A("raw", c0, c1)), (M("IM16"), A("zt", TAB + c0, TAB + c1))])
+        either(A("kt", c0, c1), A(p, 0, Q), 144.0)
+    ms(A("zt", 0, TAB), 9.0)
+    ts(A("nt", 0, TAB), A("ones", 0, TAB), DUMC, None, AL.mult)
+    F = lambda i: A("ft", 256 * i, 256 * i + 256)
+    raw, kind, hi, lo = [A("nki", 256 * i, 256 * i + 256) for i in range(4)]
+    ts(kind, raw, 3, None, AL.bitwise_and)
+    ts(hi, raw, 7, None, AL.arith_shift_right)
+    ts(lo, raw, 2, 31, AL.arith_shift_right, AL.bitwise_and)
+    ts(F(0), kind, 1.0, None, AL.is_equal)
+    ts(F(1), kind, 2.0, None, AL.not_equal)
+    ts(F(2), kind, 0.0, None, AL.is_equal)
+    ts(F(3), kind, 3.0, None, AL.is_equal)
+    act(F(8), F(3), AF.Identity, 0.0, SC1)
+    p = tile()
+    mm(A(p, 0, 256), [(M("I"), F(3))])
+    tt(F(9), A("i256", 0, 256), A(p, 0, 256), AL.mult)
+    for f, o in ((0, 4), (1, 6)):
+        p = tile()
+        for j in (0, 256):
+            mm(A(p, j, j + 256), [(M("NI"), F(f)), (M("I"), A("ones", 0, 256))])
+        tt(A("ft", 256 * o, 256 * o + 512), A("nki", 512, 1024), A(p, 0, 512), AL.mult)
+    one = A("ones", 0, 256)
+    rows = [F(0), F(0), F(1), F(1), one, one, F(0), F(2), F(4), F(5), F(6), F(7), F(8), F(9), F(2), F(3)]
+    for j in (4, 5, 0, 1, 6, 2, 3, 7, 14, 15, 12, 13, 8, 9, 10, 11):
+        dma("Y", A("nt", TAB, TAB + W, 1, j, 128, 16), rows[j], "l_nt", 2500)
+    p = tile()
+    mm(A(p, 0, Q), [(R1(384), A("iq", 0, Q, 1, 0, 1)), (R1(512), A("iq", Q, 2 * Q, 1, 0, 1)), (R1(640), A("ones", 0, Q, 1, 0, 1))])
+    act(A("wn", 0, Q), A(p, 0, Q))
+    p = tile()
+    mm(A(p, 0, Q), [(R1(128), A("iq", 0, Q, 1, 0, 1)), (R1(256), A("iq", Q, 2 * Q, 1, 0, 1))])
+    act(A("ld", 0, Q), A(p, 0, Q))
+
+    SEG = [{"aO": 0, "aP": 192, "aX": 384, "P2": 576, "P1": 1088, "X0": 1600, "P0": 1600, "O": 1600, "On": 2112, "end": 2624},
+           {"aP": 0, "aX": 192, "P2": 384, "P1": 896, "X0": 1408, "P0": 1920, "O": 2432, "On": 2944, "end": 3456}]
+    for t in (0, 1):
+        for i, a in enumerate((192 + Q, SEG[t]["On"] - SEG[t]["aP"], SEG[t]["On"] - SEG[t]["aX"], SEG[t]["On"])[:4 - t]):
+            iota(A("w4", 128 * t + 32 * i, 128 * t + 32 * i + 32), [[16, 32]], a, 0)
+    act(A("st", 128, 352), A("w4", 0, 224), AF.Identity, KC)
+    iota(A("pr", 96, 128), [[0, 32]], 0, 0)
+
+    def step(t, s, c0, c1):
+        n, sw, seg, nd = c1 - c0, "sw%d" % t, SEG[t], "nd%d" % t
+        q0, q1 = c0 // 16, c1 // 16
+        top = EXT if t == 0 else EXT + Q
+        pin = seg["P0"] if s == 0 else seg["P1"]
+        P = A(sw, pin + c0, pin + c1)
+        C = lambda nm, o=0: A(nm, o + c0, o + c1)
+        if s == 0:
+            p = tile()
+            mm(A(p, 0, n), [(M("NS1"), C(nd))])
+            either(C("ns"), A(p, 0, n), BH)
+        p = tile()
+        mm(A(p, 0, n), [(M("WU"), P)])
+        mm(A(p, 256, 256 + n), [(M("WV"), P)])
+        either(C("ue"), A(p, 0, n))
+        tt(C("xf"), A(p, 256, 256 + n), C("ue"), AL.mult)
+        p = tile()
+        mm(A(p, 0, n), [(M("NL0"), C(nd)) if s == 0 else (M("NL1"), C("rr"))], after=[C("ue")])
+        tt(C("xi"), A(p, 0, n), C("xf"), AL.add)
+        ts(C("xi", Q), C("xi"), 5, W - 1, AL.arith_shift_right, AL.bitwise_and)
+        cp(C("hu"), C("xi", Q))
+        ho = Q if (t, s) == (0, 0) else 0
+        ts(C("hs", ho), C("hu"), -2048.0, None, AL.add)
+        if (t, s, c0) == (1, 0, 0):
+            for j in (3, 2, 1, 0):
+                cp(IND(A("nt", TAB, TAB + 5120), A("ow", 8 * j, 8 * j + 8)), A("wn", 128 * j, 128 * j + 128))
+                ops[-1]["ins"].append(C("hu"))
+        for a in range(c0, c1, SCH):
+            e = min(a + SCH, c1)
+            either(A("gk", 16 * a, 16 * e), IND(A("kt", 0, W), A("hu", a, e)), 0.0, -1.0)
+        pc = tile()
+        cut = [c0 + (n * i // SUB) // 16 * 16 for i in range(SUB)] + [c1]
+        for d0, d1 in zip(cut, cut[1:]):
+            compare(pc, A(sw, pin + d0, pin + d1), c0, c1, d0, d1)
+        ts(C("mt"), A(pc, 0, n), S1, THR, AL.max, AL.is_equal)
+        p = tile()
+        mm(A(p, 0, n), [(M("TRI2"), C("mt"))])
+        either(C("lt"), A(p, 0, n), sign=True)
+        p = tile()
+        mm(A(p, 0, n), [(M("SEL"), C("mt")), (M("I"), C("hs", ho))])
+        ts(C("tm"), A(p, 0, n), BIG - 2049.0, 1.0 - BIG, AL.max, AL.add)
+        p = tile()
+        narrow(A(p, 0, q1 - q0), "E", "tm", c0, c1)
+        hb = A("hb", q0, q1)
+        ts(hb, A(p, 0, q1 - q0), 16 * 2048.0 - 1 + TAB, None, AL.add)
+        tt(C("rr", s * Q), IND(A("nt", 0, top), hb), C("ns", s * Q), AL.mult)
+        tt(C("ab"), IND(A("zt", 0, top), hb), C("lt"), AL.mult)
+        if (t, s) == (0, 0):
+            tt(C("ab", Q), P, C("lt"), AL.max)
+        else:
+            p = tile()
+            narrow(A(p, 0, q1 - q0), "WB", "rr", s * Q + c0, s * Q + c1, [(M("I"), A("q16", q0, q1))])
+            ob = A("ob", q0, q1)
+            ts(ob, A(p, 0, q1 - q0), KC, 512.0 if s == 0 else 0.0, AL.add, AL.add)
+            w0 = seg["X0"] if s == 0 else seg["P1"]
+            tt(C("ab", Q), IND(A(sw, w0, w0 + 1024), ob), C("lt"), AL.max)
+        p = tile()
+        mm(A(p, 0, n), [(M("I"), C("ab")), (M("IM9"), C("lt")), (M("I"), C("ab", Q))])
+        either(C(sw, seg["P1"] if s == 0 else seg["P2"]), A(p, 0, n))
+        p = tile()
+        if s == 0:
+            mm(A(p, 0, n), [(M("NS2"), C("rr"))])
+            either(C("ns", Q), A(p, 0, n), BH)
+        else:
+            mm(A(p, 0, n), [(M("NDR"), C("rr", Q)), (M("NDF"), C(nd)), (M("I"), C("ld"))])
+            either(C("nw%d" % t, 208), A(p, 0, n), BH)
+        if (t, s) == (0, 0):
+            p = tile()
+            mm(A(p, 0, n), [(M("PLA"), C("hs", Q))])
+            act(C("pa"), A(p, 0, n))
+            p = tile()
+            narrow(A(p, 0, q1 - q0), "WPL", "hs", Q + c0, Q + c1)
+            act(A("pb", q0, q1), A(p, 0, q1 - q0))
+
+    def compare(pc, P, b0, b1, c0, c1):
+        n = c1 - c0
+        K = lambda m: A("gk", 16 * c0 + m - 1, 16 * c1, 16)
+        NE = lambda i: A("ne", 9 * c0 + i * n, 9 * c0 + (i + 1) * n)
+        out = A(pc, c0 - b0, c1 - b0)
+        mm(out, [(M("D1"), K(1)), (M("D2"), K(2)), (M("D3"), K(3)), (M("DP"), P)], c0 == b0, False)
+        pp = tile()
+        late = 16 * max(c0, c1 - LEAD)
+        mm(A(pp, 0, n), [(M("NI"), P)], after=[A("gk", late, late + 1)])
+        per = min(4, 512 // n)
+        for i in range(0, 4, per):
+            p = tile()
+            k = min(per, 4 - i)
+            for j in range(k):
+                a, e = PACKS[i + j]
+                mm(A(p, j * n, j * n + n), [(M("A%d" % a), K(a)), (M("B%d" % a), K(e)), (M("P%d" % a), P)])
+            ts(A("ne", 9 * c0 + i * n, 9 * c0 + (i + k) * n), A(p, 0, k * n), 0.0, None, AL.not_equal)
+        for i, m in enumerate(PLAIN):
+            tt(NE(4 + i), K(m), A(pp, 0, n), AL.not_equal)
+        mm(out, [(MW("CW%d" % m, m - 1), NE(4 + i)) for i, m in enumerate(PLAIN[:2])]
+           + [(M("C%d" % a), NE(i)) for i, (a, e) in enumerate(PACKS)]
+           + [(MW("CW%d" % m, m - 1), NE(6 + i)) for i, m in enumerate(PLAIN[2:])], False, c1 == b1)
+
+    def send(t, j, src, dst, ns):
+        add("G", "send", [], [src], (t, j, src, dst), 1500.0)
+        add("R", "recv", [dst], [], (t, j, len(ops) - 1), 0.0, "in%d%d" % (t, j), ns)
+
+    def finish(t):
+        sw, seg, nd, nw, sb = "sw%d" % t, SEG[t], "nd%d" % t, "nw%d" % t, "sb%d" % t
+        top = EXT if t == 0 else EXT + Q
+        ns = 4 if t == 0 else 3
+        un, sc, kp, ov = A("un", 0, 32), A("un", 32, 64), A("kp", 0, 32), A("ov", 0, 32)
+        S = lambda i: A("sm", 32 * i, 32 * i + 32)
+        O = A(sw, seg["O"], seg["O"] + Q)
+        p = tile()
+        narrow(A(p, 0, 32), "WHV", "rr", Q, 2 * Q)
+        ts(un, A(p, 0, 32), 0.0, None, AL.is_equal)
+        cp(ov, A(p, 0, 32))
+        add("V", "scan", [sc], [A("ones", 0, 32), un], (sc, A("ones", 0, 32), un), FIX + 64 * CY)
+        p = tile()
+        mm(A(p, 0, 32), [(M("BD"), sc), (M("TRK"), un)])
+        tt(S(0), A(p, 0, 32), A("st", 64, 96), AL.min)
+        ts(A("po", 0, 32), S(0), 2047.0, None, AL.add)
+        cp(IND(A(sb, 592, 1616), A("po", 0, 32)), A(nw, 208, 208 + Q))
+        p = tile()
+        mm(A(p, 128, 130), [(M("BD"), A("un", 62, 64))])
+        for i in range(ns):
+            mm(A(p, 32 * i, 32 * i + 32), [(M("BD"), sc), (M("TRK"), un)])
+        ts(A(sb, 576, 578), A(p, 128, 130), float(CAP), None, AL.min)
+        either(A("kp", 0, 32 * ns), A(p, 0, 32 * ns), 2047.0)
+        send(t, 0, A(sb, 576, 784), A(nw, 0, 208), 2500)
+        for j, wide in ((0, "WL"), (12, "WX")):
+            p = tile()
+            narrow(A(p, 0, 12), wide, sb, 592, 784)
+            ts(A("ol", j, j + 12), A(p, 0, 12), -33.0, None, AL.add)
+        either(A(sb, 192, 384), IND(A(sw, seg["P2"], seg["P2"] + Q), A("ol", 0, 12)))
+        either(A(sb, 384, 576), IND(A(sw, seg["P2"], seg["P2"] + 1536), A("ol", 12, 24)))
+        if t == 0:
+            either(A(sb, 0, 192), IND(O, A("ol", 0, 12)))
+            send(t, 1, A(sb, 0, 576), A(sw, 0, seg["P2"]), 3500)
+        else:
+            send(t, 1, A(sb, 192, 576), A(sw, 0, seg["P2"]), 3000)
+        zv = A("zt", EXT, EXT + Q) if t == 0 else A("zv", 0, Q)
+        act(zv, IND(A("zt", 0, top), ov))
+        p = tile()
+        mm(A(p, 0, Q), [(M("I"), zv), (M("I"), O)])
+        act(A("zv", Q, 2 * Q), A(p, 0, Q), AF.Sign, -9.96875)
+        p = tile()
+        mm(A(p, 0, Q), [(M("IH"), A("zv", Q, 2 * Q)), (M("I"), zv), (M("I"), O)])
+        act(A(sw, seg["On"], seg["On"] + Q), A(p, 0, Q), AF.Identity, -9.5)
+        rv = A("nt", EXT, EXT + Q) if t == 0 else A("re2", 0, Q)
+        tt(rv, IND(A("nt", 0, top), ov), A(nd, 0, Q), AL.mult)
+        p = tile()
+        mm(A(p, 0, Q), [(M("NRS"), rv)])
+        act(A(nw, 208 + Q, 208 + 2 * Q), A(p, 0, Q), AF.Identity, BH)
+        if t == 0:
+            act(A("pb", 96, 128), A("pb", 0, 32), AF.Identity, 0.0, -1.0)
+            for q in range(32):
+                e = 128 * (q // 8 + 1)
+                eq = A("ee", 128 * q, 128 * q + e - 16 * q)
+                if q < SQ:
+                    d = A("du", 128 * (q % 4), 128 * (q % 4) + e - 16 * q)
+                    act(d, A("pa", 16 * q, e), AF.Abs, A("pb", 96 + q, 97 + q))
+                    act(eq, d, AF.Relu, BIG, -BIG)
+                else:
+                    ts(eq, A("pa", 16 * q, e), A("pb", q, q + 1), BIG, AL.is_equal, AL.mult)
+            for r in range(16):
+                either(A("ee", r, W, 128), A("ee", r, W, 128), 0.0, mkc(r))
+            for j in range(8):
+                x = A("lv", j, 256, 8)
+                if j % 2:
+                    act(x, un, AF.Identity, col(32 + j), col(40 + j))
+                else:
+                    ts(x, un, col(40 + j), col(32 + j), AL.mult, AL.add)
+            p = tile()
+            mm([A(p, 16 * q, 128 * (q // 8 + 1), 1, 0, 8) for q in range(32)],
+               [(A("lv", 8 * q, 8 * q + 8), A("ee", 128 * q, 128 * q + 128 - 16 * (q % 8))) for q in range(32)])
+            either(A("du", 0, Q, 1, 0, 8), A(p, 0, Q, 1, 0, 8))
+            p = tile()
+            narrow(A(p, 0, 32), "W8", "du", 0, Q, [(M("IC"), un)], 8)
+            act(A("pb", 64, 96), A("pb", 0, 32), AF.Identity, 2048.0)
+            tt(S(6), A(p, 0, 32), A("pb", 64, 96), AL.add)
+            tt(S(7), S(6), A("st", 32, 64), AL.min)
+            cp(A("ow", 0, 32), S(7))
+            for j in (3, 2, 1, 0):
+                cp(IND(A("kt", 0, 5120), A("ow", 8 * j, 8 * j + 8)), A(sw, seg["O"] + 128 * j, seg["O"] + 128 * j + 128))
+        B = lambda nm, i: A(nm, 32 * i, 32 * i + 32)
+        back = float(seg["P2"] - seg["On"])
+        act(S(1), kp, AF.Abs, -608.0)
+        p = tile()
+        narrow(A(p, 0, 32), "WXS", "rr", Q, 2 * Q)
+        act(S(4), A(p, 0, 32), AF.Identity, -back / 512, -1 / 512)
+        ts(B("pr", 0), S(1), 416.5, -512.0, AL.is_lt, AL.mult)
+        ts(B("pr", 1), S(1), 416.5, back, AL.is_lt, AL.mult)
+        tt(B("pr", 2), B("pr", 0), S(4), AL.mult)
+        n = 32 * ns
+        tt(A("pr", 128, 128 + n), A("pr", 0, n), A("st", 128 + 128 * t, 128 + 128 * t + n), AL.add)
+        ts(A("t4", 0, n), A("kp", 0, n), A(nw, 1, 2), BIG, AL.is_ge, AL.mult)
+        tt(A("t4", 128, 128 + n), A("t4", 0, n), A("kp", 0, n), AL.max)
+        tt(A("t4", 256, 256 + n), A("t4", 128, 128 + n), A("pr", 128, 128 + n), AL.min)
+        cp(A("of", 0, n), A("t4", 256, 256 + n))
+        nwin = A(nw, 16, 1232)
+        win = lambda a: A(sw, seg[a], seg["end"])
+        if t == 0:
+            for c0, c1 in zip(CUTS, CUTS[1:]):
+                off = lambda i: A("of", 32 * i + c0 // 16, 32 * i + c1 // 16)
+                either(A("nd1", c0, c1), IND(nwin, off(0)))
+                for i, a, x in ((1, "aP", "P0"), (2, "aX", "X0"), (3, "aO", "O")):
+                    either(A("sw1", SEG[1][x] + c0, SEG[1][x] + c1), IND(win(a), off(i)))
+        else:
+            either(A("nd2", 0, Q), IND(nwin, B("of", 0)))
+            p = tile()
+            mm(A(p, 0, Q, 1, 0, 16), [(M("YO", 128, 16), A("nd2", 0, Q))])
+            either(A("yq", 0, Q, 1, 0, 16), A(p, 0, Q, 1, 0, 16))
+            dma("Y", "yn", A("yq", 0, Q, 1, 0, 16), "o_n", 2000)
+            for j, a in ((0, "aP"), (1, "aX")):
+                for h in (0, 256):
+                    either(A("ys", j * Q + h, j * Q + h + 256), IND(win(a), A("of", 32 + 32 * j + h // 16, 48 + 32 * j + h // 16)), 0.0, 16.0)
+            for h in (0, 512, 256, 768):
+                dma("Y", ["yp", h, h + 256], A("ys", h, h + 256), "o_p", 2200)
+
+    for t in (0, 1):
+        for s in (0, 1):
+            for c0, c1 in zip(CUTS, CUTS[1:]):
+                step(t, s, c0, c1)
+        finish(t)
+    return ops
+
+
+def plan():
+    best = p = forward(None)
+    for _ in range(TURNS):
+        p = forward(backward(p))
+        if p[5] < best[5]:
+            best = p
+    return best
+
+
+def backward(p):
+    ops = p[0]
+    n = len(ops)
+    succ = [[] for _ in range(n)]
+    for i in range(n):
+        for j in ops[i]["all"]:
+            succ[j].append(i)
+    left = [len(s) for s in succ]
+    ready = set(i for i in range(n) if not left[i])
+    done, free = [0.0] * n, {}
+    while ready:
+        c = []
+        for i in ready:
+            o = ops[i]
+            st = max([done[j] + (0.0 if o["eng"] == ops[j]["eng"] == "P" else LAT) for j in succ[i]] + [0.0]) + o["lat"]
+            c.append((max(st, free.get(o["eng"], 0.0) if o["eng"] != "R" else 0.0), -o["t"], i))
+        t0 = min(c)[0]
+        st, _, i = min((x for x in c if x[0] <= t0 + BWIN), key=lambda x: x[1:])
+        done[i] = free[ops[i]["eng"]] = st + ops[i]["cost"]
+        ready.discard(i)
+        for j in ops[i]["all"]:
+            left[j] -= 1
+            if not left[j]:
+                ready.add(j)
+    return done
+
+
+def forward(given):
+    ops = graph()
+    n = len(ops)
+    hist, group, tiles = {}, {}, {}
+    for i, o in enumerate(ops):
+        if o["kind"] == "dma":
+            group.setdefault(o["sem"], []).append(i)
+    for i, o in enumerate(ops):
+        hard, soft = set(), set()
+        acc = [(x[1] if x[0] == "#" else x, True) for x in o["outs"]] + [(x[1] if x[0] == "#" else x, False) for x in o["ins"]]
+        acc += [(x[2], False) for x in o["outs"] + o["ins"] if x[0] == "#"]
+        for a, wr in acc:
+            nm, c0, c1 = a[0], a[1], a[2]
+            h = hist.setdefault(nm, [])
+            if nm[0] == "@":
+                tiles.setdefault(nm, []).append(i)
+                for j, _, _, w2 in h:
+                    if j == i:
+                        continue
+                    if ops[j]["eng"] != o["eng"] or o["eng"] == "?":
+                        hard.add(j)
+                    elif o["eng"] == "P":
+                        soft.add(j)
+                    elif wr or w2:
+                        hard.add(j)
+            else:
+                for j, d0, d1, w2 in h:
+                    if j != i and (wr or w2) and d0 < c1 and c0 < d1:
+                        if ops[j]["kind"] == "dma" and o["kind"] == "dma" and ops[j]["sem"] == o["sem"]:
+                            continue
+                        hard.update(group[ops[j]["sem"]] if ops[j]["kind"] == "dma" else [j])
+            h.append((i, c0, c1, wr))
+        if o["kind"] == "recv":
+            soft.add(o["args"][2])
+        o["hard"], o["soft"], o["all"] = hard, soft, hard | soft
+    opens = {v[0]: k for k, v in tiles.items()}
+    succ = [[] for _ in range(n)]
+    for i, o in enumerate(ops):
+        for j in o["all"]:
+            succ[j].append(i)
+    prio = [0.0] * n
+    chain = [i for i, o in enumerate(ops) if o["outs"] and o["outs"][0][0] == "gk"]
+    nxt = dict(zip(chain, chain[1:]))
+    for i in range(n - 1, -1, -1):
+        prio[i] = ops[i]["cost"] + ops[i]["lat"] + max([prio[j] + LAT for j in succ[i]] + [prio[nxt[i]] + STRETCH * ops[i]["cost"] if i in nxt else 0.0])
+    prio = given or prio
+    left = [len(o["all"]) for o in ops]
+    ready = set(i for i in range(n) if left[i] == 0)
+    fin, issue = [None] * n, [None] * n
+    free = {e: 0.0 for e in "VSPGYR"}
+    bank, held = {}, [None] * 8
+    order = []
+    while ready:
+        best = []
+        for i in sorted(ready):
+            o = ops[i]
+            st = 0.0
+            for j in o["hard"]:
+                st = max(st, fin[j] + LAT)
+            for j in o["soft"]:
+                st = max(st, issue[j] if o["eng"] == "P" else fin[j])
+            bk = None
+            if i in opens:
+                cand = []
+                for b in range(8):
+                    if held[b] is None:
+                        cand.append((0.0, b))
+                    elif all(fin[j] is not None for j in tiles[held[b]]):
+                        cand.append((max(fin[j] for j in tiles[held[b]]) + LAT, b))
+                if not cand:
+                    continue
+                tb, bk = min(cand)
+                st = max(st, tb)
+            if o["eng"] == "?":
+                best.append((max(st, free["S"]), i, bk, 0, prio[i]))
+                best.append((max(st, free["V"]) + SHY, i, bk, 1, prio[i] - LOW))
+            else:
+                best.append((max(st, free[o["eng"]]) if o["eng"] != "R" else st, i, bk, None, prio[i]))
+        t0 = min(x[0] for x in best)
+        st, i, bk, alt = max((x for x in best if x[0] <= t0 + WIN), key=lambda x: x[4])[:4]
+        o = ops[i]
+        if alt is not None:
+            o["eng"], o["kind"], o["args"], o["cost"] = o["alt"][alt]
+            o["pick"] = alt
+            st -= SHY * alt
+        if bk is not None:
+            if held[bk] is not None:
+                o["hard"] = o["hard"] | set(tiles[held[bk]])
+            held[bk] = opens[i]
+            bank[opens[i]] = bk
+        issue[i] = st + o["cost"]
+        fin[i] = issue[i] + o["lat"]
+        o["t"] = st
+        free[o["eng"]] = issue[i]
+        order.append(i)
+        ready.discard(i)
+        for j in succ[i]:
+            left[j] -= 1
+            if left[j] == 0:
+                ready.add(j)
+    assert len(order) == n
+    place = {i: k for k, i in enumerate(order)}
+    needed = set()
+    for o in ops:
+        last = {}
+        for j in o["hard"]:
+            e = ops[j]["eng"]
+            if e not in last or place[j] > place[last[e]]:
+                last[e] = j
+        needed.update(last.values())
+        o["hard"] = set(j for j in o["hard"] if ops[j]["kind"] in ("dma", "recv", "send") or j in last.values())
+    count = {e: 0 for e in "VSPG"}
+    for i in order:
+        o = ops[i]
+        if o["kind"] == "dma":
+            o["sig"] = (o["sem"], 16 * len(group[o["sem"]]))
+        elif o["kind"] == "recv":
+            o["sig"] = (o["sem"], None)
+        elif o["kind"] == "send":
+            o["sig"] = ("out%d%d" % o["args"][:2], None)
+        elif i in needed:
+            count[o["eng"]] += 1
+            o["sig"] = ("c" + o["eng"], count[o["eng"]])
+        else:
+            o["sig"] = None
+    return ops, order, bank, count, group, max(fin)
+
+
+PLAN = []
+
+
+def rank_program(g, core, T, topo):
+    rank = T.rank_of(core)
+    if rank is None:
+        return
+    if not PLAN:
+        PLAN.append(plan())
+    ops, order, bank, count, group = PLAN[0][:5]
+    queue = {"V": g.vector, "S": g.scalar, "P": g.tensor, "G": g, "Y": g.sync}
+
+    def lanes(src, dst):
+        return topo.engines(src, dst)[:8]
+
+    to = [T.cores[(rank + 1 + t) % NRANK] for t in (0, 1)]
+    frm = [T.cores[(rank - 1 - t) % NRANK] for t in (0, 1)]
+    n_out = [len(lanes(core, c)) for c in to]
+    n_in = [len(lanes(c, core)) for c in frm]
+
+    def R(x):
+        if isinstance(x, str):
+            return T[x][:]
+        if isinstance(x, list):
+            return T[x[0]][:, x[1]:x[2]]
+        if not is_ap(x):
+            return x
+        if x[0] == "#":
+            return R(x[1]).indirect(R(x[2]))
+        nm = "ps%d" % bank[x[0]] if x[0][0] == "@" else x[0]
+        ps = slice(x[4], x[5], x[6]) if x[6] != 1 else slice(x[4], x[5])
+        cs = slice(x[1], x[2], x[3]) if x[3] != 1 else slice(x[1], x[2])
+        return T[nm][ps, cs]
+
+    def sig(j):
+        s, v = ops[j]["sig"]
+        if ops[j]["kind"] == "recv":
+            v = n_in[ops[j]["args"][0]]
+        elif ops[j]["kind"] == "send":
+            v = n_out[ops[j]["args"][0]]
+        return s, v
+
+    seen = {}
+    for i in order:
+        o = ops[i]
+        k, a, e = o["kind"], o["args"], o["eng"]
+        if k == "recv":
+            continue
+        q = queue[e]
+        want = {}
+        for j in o["hard"]:
+            s, v = sig(j)
+            want[s] = max(want.get(s, 0), v)
+        for s in sorted(want):
+            if seen.get((e, s), 0) < want[s]:
+                q.wait_ge(T.sem[s], want[s])
+                seen[(e, s)] = want[s]
+        if k == "ts":
+            if a[5] is None:
+                ins = q.tensor_scalar(R(a[0]), R(a[1]), R(a[2]), None, a[4])
+            else:
+                ins = q.tensor_scalar(R(a[0]), R(a[1]), R(a[2]), R(a[3]), a[4], a[5])
+        elif k == "tt":
+            ins = q.tensor_tensor(R(a[0]), R(a[1]), R(a[2]), a[3])
+        elif k == "cp":
+            ins = q.tensor_copy(R(a[0]), R(a[1]))
+        elif k == "ms":
+            ins = q.memset(R(a[0]), a[1])
+        elif k == "scan":
+            ins = q.tensor_tensor_scan(R(a[0]), R(a[1]), R(a[2]), 0.0, AL.mult, AL.add)
+        elif k == "act":
+            ins = q.activation(R(a[0]), R(a[1]), a[2], bias=R(a[3]), scale=R(a[4]))
+        elif k == "mm":
+            ins = q.matmul(R(a[0]), R(a[1]), R(a[2]), a[3], a[4])
+        elif k == "iota":
+            if SCRATCH[a[0][0]][2] == "int32":
+                ins = q.iota(R(a[0]), a[1], a[2], a[3])
+            else:
+                ins = q.iota(R(a[0]), a[1], a[2], a[3], allow_small_or_imprecise_dtypes=True)
+        elif k == "put":
+            ins = q.affine_select(R(a[0]), R(a[0]), a[1], AL.not_equal, a[3], a[2], 1)
+        elif k == "keep":
+            ins = q.affine_select(R(a[0]), R(a[1]), a[2], AL.is_ge, 0.0, 0, a[3])
+        elif k == "dma":
+            q.dma_start(R(a[0]), R(a[1])).then_inc(T.sem[o["sem"]], 16)
+            continue
+        else:
+            t, j = a[0], a[1]
+            rid, pid = topo.addr(to[t])[:2]
+            mask = sum(1 << x for x in lanes(core, to[t]))
+            q.remote_dma(R(a[3]), R(a[2]), T.sem["in%d%d" % (t, j)], T.sem["out%d%d" % (t, j)], pid, rid, mask)
+            continue
+        if o["sig"] is not None:
+            ins.then_inc(T.sem[o["sig"][0]], 1)
+    last = {"c" + e: count[e] for e in count}
+    for s in group:
+        last[s] = 16 * len(group[s])
+    for t in (0, 1):
+        for j in (0, 1):
+            last["in%d%d" % (t, j)] = n_in[t]
+            last["out%d%d" % (t, j)] = n_out[t]
+    for s in sorted(last):
+        if not any(v >= last[s] for (e, s2), v in seen.items() if s2 == s):
+            g.sync.wait_ge(T.sem[s], last[s])

@@ -1,57 +1,70 @@
+import numpy as np
 from concourse.mybir import AluOpType, ActivationFunctionType
 
 AL = AluOpType
 AF = ActivationFunctionType
 W, Q, CAP, NRANK = 4096, 512, 192, 8
-CUTS = [0, 160, 352, 512]
-SUB = 2
-SCH = 32
-SQ = 24
-PACKS = [(12, 4), (11, 5), (10, 6), (9, 7)]
-PLAIN = [16, 15, 14, 13, 8]
-TAB, EXT, DUM = 256, 4352, 4608
+HASH = [[0, 96, 320, 512], [0, 224, 416, 512]]
+KEYS = [list(range(0, Q + 1, 32))] * 2
+PARTS = [[0, 112, 224, 320, 416, 512]] * 2
+TAIL = [[0, 224, 416, 512]] * 2
+SHUT = [0, 416, 512]
+SOFT = 320
+CH = 32
+PACKS = [[(10, 0), (6, 16)], [(9, 0), (7, 16)], [(8, 0), (5, 16), (1, 8), (2, 9), (3, 10)]]
+PLAIN = [16, 15, 14, 13, 12, 11, 4]
+NP, NT = len(PACKS), len(PACKS) + len(PLAIN)
+TAB, EXT = 256, 4352
 BIG = 8192.0
-CY, PECY, GATH, SCAT, LAT, FIX = 1.0, 0.5, 1.5, 3.5, 120.0, 60.0
-LEAD, STRETCH, WIN, SHY, LOW, TURNS, BWIN = 128, 0.5, 40.0, 100.0, 5000.0, 6, 40.0
+SEG = [{"aO": 0, "aP": 512, "aX": 704, "P2": 896, "P1": 1408, "X0": 1920, "P0": 1920, "O": 1920, "On": 2432, "end": 2944},
+       {"aP": 0, "aX": 192, "P2": 384, "P1": 896, "X0": 1408, "P0": 1920, "O": 2432, "On": 2944, "end": 3456}]
+PECY, PEFIX, LAT, FIX, SFIX = 0.5, 10.0, 120.0, 60.0, 78.0
+CASES = [(1.0, 1.56, 3.8), (1.3, 1.9, 5.0), (1.3, 1.2, 2.5)]
+LOAD, SEND, FLY = 1.0, 1500.0, 1.0
+LEAD, STRETCH, WIN, SHY, GSHY, NSHY, TURNS, BWIN = 128, 0.5, 40.0, 600.0, 1000.0, 1e6, 3, 40.0
+MOVES, HEAT, FLIP, MARK, SEED = 30000, 60.0, 0.2, 64, 2
 
-MATS = ["I", "NI", "I16", "IM16", "IM9", "IC", "IH", "I2K", "J", "BD", "TRI", "TRI2", "SEL", "TRK", "WU", "WV", "T1"]
-for _x in "ABPC":
-    MATS += [_x + str(_a) for _a, _b in PACKS]
-WIDE = ["E"] + ["CW%d" % _m for _m in range(1, 17)]
-GM = ["QH", "NL0", "D1", "D2", "D3", "DP", "NS1", "PLA", "NL1", "NS2", "NDR", "NDF", "NRS", "YO"]
-GW = ["WB", "WHV", "WXS", "WL", "WX", "WPL", "W8"]
+MATS = ["I", "NI", "IM", "J", "BD", "TRI", "TRI2", "NTRI", "SEL", "TRK", "WU", "WV",
+        "DJ0", "DJ1", "DJ2", "DJ3", "DQ0", "DQ1", "DQ2", "DQ3", "DQ4", "DQ5", "DQ6", "DQ7", "MK0", "MK1"]
+MATS += ["K%d" % _m for _t in PACKS for _m, _r in _t if _m > 3] + ["P%d" % _i for _i in range(NP)]
+EARLY = ["NL0", "K1", "K2", "K3"] + ["CW%d" % _m for _m in sorted(PLAIN)] + ["C%d" % _i for _i in range(NP)] + ["NS2", "NL1"]
+LATE = ["IO", "IC", "NC", "IH", "QN", "QP", "VAL", "NDR", "WNM", "LD6", "NRS", "PLA", "SG", "WHV", "WL", "WPL"]
 MOFF = {}
 GMW = VMW = 0
-for _n in GM + GW:
+for _n in EARLY + LATE:
     MOFF[_n] = ("gm", GMW)
-    GMW += 128 if _n in GM else 144
-for _n in MATS + WIDE:
+    GMW += 144 if _n[0] == "W" and _n != "WNM" or _n[:2] == "CW" else 128
+for _n in MATS:
     MOFF[_n] = ("vm", VMW)
-    VMW += 128 if _n in MATS else 144
+    VMW += 128
 
 SCRATCH = {}
-for _d, _l in (("bfloat16", (("gm", GMW), ("vm", VMW), ("row", 768), ("iow", 176), ("iog", 128), ("i256", 256), ("iq", 1024),
-                             ("ones", Q), ("q16", 32), ("raw", W), ("kt", 5120), ("zt", 4864), ("nt", 5376), ("ft", 2560),
-                             ("qpi", Q), ("qh", 2 * Q), ("sw0", 2624), ("sw1", 3456), ("nd0", Q), ("nd1", Q), ("nd2", Q),
-                             ("nw0", 1232), ("nw1", 1232), ("sb0", 1616), ("sb1", 1616), ("ns", 2 * Q), ("rr", 2 * Q),
-                             ("gk", 16 * Q), ("ne", 9 * Q), ("mt", Q), ("lt", Q), ("ab", 2 * Q), ("ee", W), ("du", Q),
-                             ("wn", Q), ("lv", 256), ("ld", Q), ("un", 64), ("zv", 2 * Q), ("re2", Q), ("ys", 2 * Q))),
-               ("float32", (("qfm", 128), ("cc", 64), ("mk", 32), ("iof", 32), ("st", Q), ("qf", Q), ("ue", Q), ("xf", Q),
-                            ("pa", Q), ("pb", 128), ("kp", 128), ("sm", 256), ("w4", 256), ("pr", 256), ("t4", 384), ("yq", Q))),
-               ("int32", (("pi", 8), ("nki", 1024), ("wti", 8), ("qni", Q), ("xi", 2 * Q))),
-               ("uint16", (("hu", Q), ("hb", 32), ("ob", 32), ("ov", 32), ("po", 32), ("ol", 32), ("ow", 32), ("of", 128))),
-               ("float16", (("hs", 2 * Q), ("tm", Q)))):
+for _d, _l in (("bfloat16", (("gm", GMW), ("vm", VMW), ("iow", 176), ("iog", 128), ("ones", Q), ("raw", W), ("kt", W + CH), ("zt", EXT + Q),
+                             ("qpi", Q), ("sw0", 2944), ("sw1", 3456), ("sb0", 384), ("sb1", 384), ("gk", 16 * Q), ("ne", NT * Q),
+                             ("mt", Q), ("lt", Q), ("ab", 2 * Q), ("ee", 2 * Q), ("un", 288), ("zv", 2 * Q), ("ys", 2 * Q))),
+               ("float32", (("I32", 128), ("cc", 32), ("mk", 64), ("iof", Q), ("nt", TAB + W + CH), ("ft", 2560), ("ns", Q), ("ue", Q),
+                            ("xf", Q), ("wn", Q), ("pk", Q), ("nw0", 912), ("nw1", 912), ("nd2", Q), ("kp", 32), ("w4", 288),
+                            ("st", 288), ("dc", 128), ("sm", 32), ("t4", 256))),
+               ("int32", (("pi", 8), ("nki", 768), ("wti", 8), ("qni", Q), ("xi", 2 * Q))),
+               ("uint16", (("hu", Q), ("hb", 32), ("ov", 32), ("po", 32), ("ol", 32), ("ow", 32), ("of", 96), ("oo", 32))),
+               ("float16", (("hs", 2 * Q), ("tm", Q), ("nd0", Q), ("nd1", Q), ("rr", 2 * Q), ("ld", Q), ("sn0", 400), ("sn1", 400),
+                            ("sh", 192), ("ar0", 208), ("ar1", 208), ("pt", 128), ("xv", 32)))):
     for _n, _c in _l:
         SCRATCH[_n] = ("sbuf", [128, _c], _d)
 for _b in range(8):
     SCRATCH["ps%d" % _b] = ("psum", [128, 512], "float32")
-SEMAPHORES = ["cV", "cS", "cP", "cG", "l_qp", "l_wt", "l_qn", "l_nk", "l_s0", "l_s1", "l_s2", "l_s3", "l_nt", "z_a", "z_b",
-              "o_p", "o_n", "in00", "in01", "in10", "in11", "out00", "out01", "out10", "out11"]
+WRITES = ["00", "01", "02", "10", "11"]
+SEMAPHORES = ["cV", "cS", "cP", "cG", "c2", "l_qp", "l_wt", "l_qn", "l_nk", "l_s0", "l_s1", "l_s2", "l_s3", "l_nt", "z_a", "z_b",
+              "o_p", "o_n"] + ["in" + _w for _w in WRITES] + ["out" + _w for _w in WRITES]
 SIZE = {"bfloat16": 2, "float16": 2, "uint16": 2, "float32": 4, "int32": 4}
 
 
 def A(name, c0, c1, st=1, p0=0, p1=128, ps=1):
     return (name, c0, c1, st, p0, p1, ps)
+
+
+def B(name, i, k=1):
+    return A(name, 32 * i, 32 * (i + k))
 
 
 def IND(win, off):
@@ -63,9 +76,14 @@ def M(name, rows=128, cols=128):
     return A(b, c, c + cols, 1, 0, rows)
 
 
-def MW(name, r, rows=128):
+def MW(name, r):
     b, c = MOFF[name]
-    return A(b, c + 15 - r, c + 143 - r, 1, 0, rows)
+    return A(b, c + 15 - r, c + 143 - r)
+
+
+def MC(name, c):
+    b, o = MOFF[name]
+    return A(b, o + c, o + 128, 16)
 
 
 def cols(ap):
@@ -84,18 +102,25 @@ def width(ap):
     return SIZE[SCRATCH[ap[0]][2]]
 
 
+def spans(cuts):
+    return list(zip(cuts, cuts[1:]))
+
+
 def graph():
     ops = []
 
     def add(eng, kind, outs, ins, args, cost, sem=None, lat=0.0):
         ops.append({"eng": eng, "kind": kind, "outs": outs, "ins": ins, "args": args, "cost": cost, "sem": sem, "lat": lat})
 
-    def vcost(out, in0, per):
+    def price(fix, n, kind=0):
+        return [fix + n * c[0] * (c[kind] if kind else 1.0) for c in CASES]
+
+    def vcost(out, in0, per, fix=FIX):
         if out[0] == "#":
-            return FIX + cols(out) * SCAT * CY
+            return price(fix, cols(out), 2)
         if in0[0] == "#":
-            return FIX + cols(out) * GATH * CY
-        return FIX + max(64, cols(out) * per) * CY
+            return price(fix, cols(out), 1)
+        return price(fix, max(64, cols(out) * per))
 
     def ts(out, in0, s1, s2, op0, op1=None):
         per = 0.5 if width(out) == 2 and width(in0) == 2 else 1
@@ -110,16 +135,25 @@ def graph():
         add("V", "cp", [out], [in0], (out, in0), vcost(out, in0, per))
 
     def ms(out, val):
-        add("V", "ms", [out], [], (out, val), FIX + max(64, cols(out) * width(out) / 4) * CY)
+        add("V", "ms", [out], [], (out, val), price(FIX, max(64, cols(out) * width(out) / 4)))
 
     def act(out, in0, func=AF.Identity, bias=0.0, scale=1.0):
-        add("S", "act", [out], [in0] + [s for s in (bias, scale) if is_ap(s)], (out, in0, func, bias, scale), vcost(out, in0, 1))
+        add("S", "act", [out], [in0] + [s for s in (bias, scale) if is_ap(s)], (out, in0, func, bias, scale), vcost(out, in0, 1, SFIX))
 
-    def either(out, in0, bias=0.0, scale=1.0, sign=False):
-        act(out, in0, AF.Sign if sign else AF.Identity, bias, scale)
+    def either(out, in0, bias=0.0, scale=1.0, func=AF.Identity, shy=None):
+        act(out, in0, func, bias, scale)
         a = ops.pop()
-        if sign:
-            ts(out, in0, 0.5, None, AL.is_ge)
+        if func == AF.Abs:
+            a["kind"], a["cost"] = "act2", [2 * c + LAT for c in a["cost"]]
+            ts(out, in0, 0.0, None, AL.not_equal)
+        elif func == AF.Sign:
+            ts(out, in0, bias, 0.5, AL.add, AL.is_ge)
+        elif func == AF.Relu and scale == -1.0:
+            ts(out, in0, -1.0, 0.0, AL.mult, AL.max)
+        elif func == AF.Relu:
+            ts(out, in0, bias, 0.0, AL.add, AL.max)
+        elif scale != 1.0 and bias != 0.0:
+            ts(out, in0, scale, bias, AL.mult, AL.add)
         elif scale != 1.0:
             ts(out, in0, scale, None, AL.mult)
         elif bias != 0.0:
@@ -129,32 +163,47 @@ def graph():
         b = ops.pop()
         a["alt"] = [(x["eng"], x["kind"], x["args"], x["cost"]) for x in (a, b)]
         a["eng"] = "?"
+        a["shy"] = SHY if shy is None else shy
         ops.append(a)
 
     def mm(out, terms, first=True, last=True, after=()):
         for i, (l, r) in enumerate(terms):
             o = out[i] if isinstance(out, list) else out
-            c = max(min(64, cols(l)), cols(r)) * PECY * (4 if width(r) == 4 else 1) + 10
-            add("P", "mm", [o], [l, r] + list(after), (o, l, r, first and i == 0, last and i == len(terms) - 1), c)
+            c = price(PEFIX, max(min(64, cols(l)), cols(r)) * PECY * (4 if width(r) == 4 else 1))
+            add("P", "mm", [o], [l, r] + list(after), [(o, l, r, first and i == 0, last and i == len(terms) - 1)], c)
+
+    def mmx(out, terms, first=True, last=True, after=()):
+        k = len(ops)
+        mm(out, terms, first, last, after)
+        part = ops[k:]
+        del ops[k:]
+        add("P", "mm", [x for o in part for x in o["outs"]], [x for o in part for x in o["ins"]], [o["args"][0] for o in part],
+            [sum(c) for c in zip(*[o["cost"] for o in part])])
 
     def iota(out, pat, base, cm):
-        add("G", "iota", [out], [], (out, pat, base, cm), 160 + 2 * cols(out) * CY)
+        add("G", "iota", [out], [], (out, pat, base, cm), price(0, 160 + 2 * cols(out)))
+
+    def sel(out, in0, pat, cmp, fill, base, cm):
+        add("G", "sel", [out], [in0], (out, in0, pat, cmp, fill, base, cm), price(0, 210 + 2 * cols(out)))
 
     def put(ap, pat, base, val):
-        add("G", "put", [ap], [ap], (ap, pat, base, val), 210 + 2 * cols(ap) * CY)
+        sel(ap, ap, pat, AL.not_equal, float(val), base, 1)
 
-    def keep(out, in0, pat, cm):
-        add("G", "keep", [out], [in0], (out, in0, pat, cm), 210 + 2 * cols(out) * CY)
+    def keep(out, in0, pat, cm, base=0):
+        sel(out, in0, pat, AL.is_ge, 0.0, base, cm)
 
     def ent(name, k, c, val):
-        b, o = MOFF[name]
-        put(A(b, o + c, o + 128, 16), [[-16, 8]], -k, val)
+        put(MC(name, c), [[-16, 8]], -k, val)
 
     def entrow(name, k, val):
         put(M(name), [[-16, 8], [0, 16]], -k, val)
 
-    def dma(eng, out, in0, sem, ns):
-        add(eng, "dma", [out] if is_ap(out) else [], [in0] if is_ap(in0) else [], (out, in0), 60.0, sem, ns)
+    def dma(eng, out, in0, sem, ns, after=(), busy=60.0):
+        add(eng, "dma", [out] if is_ap(out) else [], ([in0] if is_ap(in0) else []) + list(after), (out, in0), price(busy, 0), sem, ns * LOAD)
+
+    def send(w, src, dst, ns):
+        add("G", "send", [], [src], (w, src, dst), price(SEND, 0))
+        add("R", "recv", [dst], [], (w, len(ops) - 1), price(0.0, 0), "in" + w, ns * FLY)
 
     nps = [0]
 
@@ -162,446 +211,406 @@ def graph():
         nps[0] += 1
         return "@%d" % nps[0]
 
-    def narrow(out, wide, src, c0, c1, more=(), rows=128):
-        mm(out, [(MW(wide, r, rows), A(src, c0 + r, c1, 16, 0, rows)) for r in range(16)] + list(more))
+    def rows16(wide, src, c0, c1):
+        return [(MW(wide, r), A(src, c0 + r, c1, 16)) for r in range(16)]
 
     col = lambda i: A("cc", i, i + 1)
     mkc = lambda m: A("mk", m, m + 1)
-    PC, KC, GB, JC, G15, THR, S1, BH, SC1, DUMC = [col(i) for i in range(10)]
-    W0, W1 = col(12), col(13)
-    io = A("iow", 16, 144)
+    nmk = lambda m: A("mk", 32 + m, 33 + m)
+    PC, KC, GB, JC, THR, LTB, TA, DUMC, LDM, IXB = [col(i) for i in range(10)]
+    W0, W1 = col(14), col(15)
+    I32 = A("I32", 0, 128)
 
     dma("Y", A("qpi", 0, Q), "qp", "l_qp", 2200)
     dma("S", A("raw", 0, 1024), ["sen", 0, 1024], "l_s0", 2600)
     dma("Y", A("wti", 0, 2), "wt", "l_wt", 2000)
     dma("S", A("raw", 1024, 2048), ["sen", 1024, 2048], "l_s1", 3300)
-    dma("Y", A("qni", 0, Q, 1, 0, 8), "qn", "l_qn", 2200)
     dma("Y", A("raw", 2048, 3072), ["sen", 2048, 3072], "l_s2", 4000)
     dma("Y", A("raw", 3072, 4096), ["sen", 3072, 4096], "l_s3", 4700)
-    dma("Y", A("nki", 0, 256), "nk", "l_nk", 5000)
+    dma("Y", A("nki", 0, 256), "nk", "l_nk", 3000)
+    for j in range(16):
+        dma("YS"[j % 2], A("qni", 0, Q, 1, j, 128, 16), "qn", "l_qn", 2200)
 
     iota(A("pi", 0, 1), [[0, 1]], 0, 1)
     iota(A("iow", 0, 176), [[1, 176]], -16, 0)
     iota(A("iog", 0, 128), [[16, 8], [0, 16]], 0, 0)
     iota(A("iof", 0, 32), [[1, 32]], 0, 0)
-    ms(A("gm", 0, 256), 0.0)
-    ms(A("qfm", 0, 128, 1, 0, 8), 0.0)
-    ms(A("ee", 0, 1152), 0.0)
-    b, o = MOFF["CW1"]
-    for x in (A("gm", 256, 1280), A(b, o, o + 1152), A(b, o + 1152, o + 2304), A("gm", 1792, GMW), A("gm", 1280, 1792)):
-        dma("Y", x, A("ee", 0, cols(x)), "z_a", 2500)
+    late = MOFF[LATE[0]][1]
+    ms(A("gm", 0, 512), 0.0)
+    ms(A("gm", 512, late), 0.0)
+    ms(A("ee", 0, 384), 0.0)
+    for a in range(late, GMW, 384):
+        e = min(GMW, a + 384)
+        dma("Y", A("gm", a, e), A("ee", 0, e - a), "z_a", 2200, [A("raw", 1024, 1025)], 600.0)
     ms(A("ones", 0, Q), 1.0)
     ts(A("pi", 1, 2), A("pi", 0, 1), 15, None, AL.bitwise_and)
     cp(A("cc", 0, 2), A("pi", 0, 2))
     act(GB, KC, AF.Identity, PC, -1.0)
     ts(A("mk", 0, 17), A("iof", 0, 17), KC, None, AL.is_gt)
-    ts(M("I"), io, PC, None, AL.is_equal)
+    ts(A("mk", 32, 49), A("iof", 0, 17), KC, None, AL.is_le)
+    ts(M("I"), A("iow", 16, 144), PC, None, AL.is_equal)
     ts(M("BD"), A("iog", 0, 128), GB, None, AL.is_equal)
     keep(M("TRI"), M("BD"), [[1, 128]], -1)
-    cp(A("cc", 12, 14), A("wti", 0, 2))
-    ts(M("WU"), M("TRI"), W0, 16.0, AL.mult, AL.mult)
-    ts(M("WV"), M("TRI"), W1, 16.0, AL.mult, AL.mult)
-    for nm, v in (("I16", 1 / 16), ("IM16", -16.0), ("NI", -1.0), ("IM9", -10.0), ("IC", BIG), ("IH", -0.5), ("I2K", -2048.0), ("T1", -BIG)):
-        act(M(nm), M("I"), AF.Identity, 0.0, v)
-    act(G15, GB, AF.Identity, 15.0)
-    act(JC, KC, AF.Identity, G15, -1.0)
-    ts(M("J"), io, JC, None, AL.is_equal)
-    b, o = MOFF["E"]
-    ts(A(b, o, o + 144), A("iow", 16, 160), G15, None, AL.is_equal)
-    b, o = MOFF["CW1"]
-    x = A(b, o + 15, o + 2304, 16)
-    iota(x, [[0, 144]], 1, 0)
-    keep(x, x, [[0, 16], [-16, 9]], 1)
-    keep(x, x, [[1, 16], [16, 9]], -1)
-    for i, (a, s) in enumerate(PACKS):
-        act(M("A%d" % a), M("I"), AF.Identity, 0.0, mkc(a))
-        act(M("B%d" % a), M("J"), AF.Identity, 0.0, mkc(s))
-        act(col(20 + i), mkc(a), AF.Identity, GB, float(a - s))
-        ts(M("C%d" % a), A("iow", 17 - s, 145 - s), col(20 + i), None, AL.is_equal)
-    p = tile()
-    for i, (a, s) in enumerate(PACKS):
-        mm(A(p, 128 * i, 128 * i + 128), [(M("I"), M("A%d" % a)), (M("I"), M("B%d" % a))])
-    act(M("P%d" % PACKS[0][0], 128, 512), A(p, 0, 512))
-    p = tile()
-    mm(A(p, 0, 128), [(M("I"), M("BD")), (M("I"), M("I")), (M("NI"), M("TRI"))])
-    mm(A(p, 128, 256), [(M("IC"), M("I")), (M("IC"), M("TRI")), (M("T1"), M("BD"))])
-    mm(A(p, 256, 384), [(M("I"), M("TRI")), (M("NI"), M("BD")), (M("I"), M("I2K"))])
-    act(M("TRI2", 128, 384), A(p, 0, 384))
+    keep(M("TRI2"), M("BD"), [[-1, 128]], 1)
+    cp(A("cc", 14, 16), A("wti", 0, 2))
+    ts(M("WU"), M("TRI"), W0, 256.0, AL.mult, AL.mult)
+    ts(M("WV"), M("TRI"), W1, 256.0, AL.mult, AL.mult)
+    for nm, v in (("IM", -4096.0), ("NI", -1.0)):
+        either(M(nm), M("I"), 0.0, v)
+    for nm, v in (("IC", BIG), ("IH", -1 / 32), ("NC", -BIG), ("IO", SEG[0]["On"] / BIG)):
+        put(M(nm), [[-1, 128]], 0, v)
+    either(I32, M("I"))
+    either(M("SEL"), M("TRI2"), 0.0, -BIG / 2)
+    put(M("SEL"), [[-1, 128]], 0, BIG / 2)
+    either(M("NTRI"), M("TRI2"), 0.0, -1.0)
+    either(M("TRK"), M("TRI2"), 0.0, -1.0)
+    put(M("TRK"), [[-1, 128]], 0, -2048.0)
+    act(JC, KC, AF.Identity, GB, -1.0)
+    ts(M("J"), A("iow", 1, 129), JC, None, AL.is_equal)
+    run = [m for m in PLAIN if m > 7]
+    b, o = MOFF["CW%d" % min(run)]
+    x = A(b, o + 15, o + 144 * len(run), 16)
+    iota(x, [[0, 9 * len(run)]], 1, 0)
+    keep(x, x, [[0, len(run)], [-16, 9]], 1)
+    keep(x, x, [[1, len(run)], [16, 9]], -1, min(run) - 1)
+    for m in PLAIN:
+        if m not in run:
+            b, o = MOFF["CW%d" % m]
+            keep(A(b, o + 15, o + 143, 16), MC("BD", 0), [[16, 8]], -1, m - 1)
+    for i, t in enumerate(PACKS):
+        for m, r in t:
+            x = MC("C%d" % i, m - 1)
+            if m < 4:
+                for k in range(m):
+                    ent("K%d" % m, k, r, float(32 ** k))
+                put(x, [[-16, 8]], -r, 1.0)
+            elif r == 16:
+                either(M("K%d" % m), M("J"), 0.0, mkc(m))
+                keep(x, MC("BD", 0), [[-16, 8]], 1, m - 16)
+            elif r == 0:
+                either(M("K%d" % m), M("I"), 0.0, mkc(m))
+                keep(x, MC("BD", 0), [[16, 8]], -1, m - 1)
+            else:
+                ts(M("K%d" % m), A("iow", 16 - r, 144 - r), PC, mkc(m), AL.is_equal, AL.mult)
+                keep(x, MC("BD", 0), [[16, 8]], -1, r + m - 1)
+                keep(x, x, [[-16, 8]], 1, -r)
+    entrow("NL0", 4, 1184.0)
+    entrow("NL0", 9, -2.0 ** 21)
+    for i0 in range(0, NP, 4):
+        p, k = tile(), min(4, NP - i0)
+        for i in range(k):
+            mm(A(p, 128 * i, 128 * i + 128), [(M("I"), M("K%d" % m)) for m, r in PACKS[i0 + i]])
+        either(M("P%d" % i0, 128, 128 * k), A(p, 0, 128 * k))
     ts(A("pi", 2, 3), A("pi", 1, 2), 1, None, AL.add)
     ts(A("pi", 3, 4), A("pi", 2, 3), 2, None, AL.arith_shift_right)
-    cp(THR, A("pi", 3, 4))
-    act(S1, mkc(3), AF.Identity, THR, -BIG)
-    act(BH, mkc(8), AF.Identity, 1.0, -1.0)
-    act(SC1, KC, AF.Identity, 1.0)
-    ts(DUMC, KC, 14.0, mkc(8), AL.is_equal, AL.add)
-    act(A("q16", 0, 32), A("iof", 0, 32), AF.Identity, 0.0, 16.0)
-    ts(A("cc", 32, 40), A("q16", 0, 8), GB, None, AL.is_equal)
-    act(A("cc", 40, 48), A("cc", 32, 40), AF.Identity, 0.0, -1.0)
-    act(A("st", 0, 32), A("q16", 0, 32), AF.Identity, KC)
-    act(A("st", 32, 64), A("st", 0, 32), AF.Identity, float(DUM))
-    act(A("st", 64, 96), A("st", 0, 32), AF.Identity, 512.0 - 2047.0)
-    for x in (A("row", 128, 768), A("kt", W, 5120), A("nt", EXT + Q, 5376), A("sb0", 576, 1616), A("sb1", 576, 1616)):
-        dma("Y", x, A("ee", 0, cols(x)), "z_b", 2500)
-    for o, c, v in ((128, 10, 1.0), (256, 11, 1.0), (384, 12, 0.125), (512, 13, 1.0), (640, 12, 17.0), (640, 4, 1.0), (640, 5, 1.0), (640, 15, 1.0)):
-        put(A("row", o + c, o + 128, 16, 0, 1), [[0, 8]], 0, v)
-    R1 = lambda o: A("row", o, o + 128, 1, 0, 1)
-    b, o = MOFF["QH"]
-    for c in (0, 2, 4):
-        put(A("qfm", c + 1, 128, 16, 0, 8), [[-1, 8]], 0, 1.0)
-        put(A(b, o + c, o + 128, 16, 0, 8), [[-1, 8]], 0, 1.0)
-        put(A(b, o + c + 1, o + 128, 16, 0, 8), [[-1, 8]], 0, -32.0)
-    entrow("NL0", 4, -93184.0)
-    entrow("NL0", 5, 1184.0)
-    for m in (1, 2, 3):
-        for k in range(m):
-            ent("D%d" % m, k, m - 1, float(32 ** k))
-            ent("DP", k, m - 1, float(32 ** k))
-    iota(A("i256", 0, 256), [[1, 256]], 0, 0)
-    for k, c, v in ((2, 0, 1), (3, 1, 1), (2, 2, 1), (3, 3, 1), (8, 6, -1)):
-        ent("NS1", k, c, float(v))
+    ts(THR, A("pi", 3, 4), 0.5, None, AL.add)
+    act(LTB, KC, AF.Identity, 16.0, -1.0)
+    act(TA, KC, AF.Identity, -8 * BIG, BIG / 2)
+    ts(col(16), KC, 7.0, mkc(10), AL.is_equal, AL.add)
+    act(DUMC, mkc(1), AF.Identity, col(16), -1.0)
+    act(LDM, mkc(5), AF.Identity, mkc(6), -1.0)
+    act(IXB, KC, AF.Identity, -2048.0, 256.0)
+    iota(A("iof", 32, Q), [[1, Q - 32]], 32, 0)
+    NEWF, NEWG, NEWL = ((1, 1), (0, -1), (13, 1)), ((3, 1), (10, 1), (12, -1)), ((2, 1), (10, 1), (11, -1))
+    for c, terms in ((0, NEWF), (1, NEWF), (2, NEWG), (3, NEWG)):
+        for k, v in terms:
+            ent("NS2", k, c, v)
+    either(M("NDR"), M("NS2"))
+    for k, c, v in ((15, 4, 1), (14, 5, 1), (7, 6, 1), (6, 6, -1), (7, 7, 1), (6, 7, -1)):
+        ent("NS2", k, c, v)
+    for k, v in NEWL:
+        entrow("NL1", k, 1184.0 * v)
+    entrow("NL1", 9, -2.0 ** 21)
+    entrow("QN", 6, -1 / 8)
+    entrow("QP", 6, 1.0)
+    entrow("VAL", 15, 64.0)
+    for k, v in NEWL:
+        ent("NDR", k, 4, v)
+    for k, v in ((7, 512.0), (6, -512.0), (8, -512.0)):
+        ent("NDR", k, 6, v)
+        ent("WHV", k, 15, -v)
+    for k, v in ((14, 1.0), (5, 1.0), (15, 2304.0), (4, 2816.0)):
+        ent("WHV", k, 15, v)
+    ent("WL", 5, 15, 1.0)
+    ent("WL", 6, 15, 1.0)
+    for k, c in ((0, 0), (0, 1), (0, 2), (0, 3), (0, 4), (5, 5)):
+        ent("NRS", k, c, 1.0)
     ent("WPL", 15, 15, 1.0)
     entrow("PLA", 15, 1.0)
-    for k, c, v in ((2, 0, 1), (10, 0, 1), (3, 1, 1), (11, 1, 1), (2, 2, 1), (10, 2, 1), (3, 3, 1), (11, 3, 1), (12, 4, 1), (13, 5, 1),
-                    (14, 6, 1), (14, 7, 1), (15, 12, -1), (15, 13, -1)):
-        ent("NS2", k, c, float(v))
-    for k, v in ((0, -93184.0), (8, -93184.0), (1, 1184.0), (9, 1184.0)):
-        entrow("NL1", k, v)
-    ent("WB", 6, 15, 512.0)
-    iota(A("iq", 0, Q, 1, 0, 1), [[1, 16], [0, 32]], 0, 0)
-    iota(A("iq", Q, 2 * Q, 1, 0, 1), [[0, 16], [1, 32]], 0, 0)
-    for k, c in ((0, 4), (8, 4), (1, 5), (9, 5), (2, 2), (10, 2), (3, 3), (11, 3), (14, 6), (7, 6)):
-        ent("NDR", k, c, 1.0)
-    b, o = MOFF["W8"]
-    put(A(b, o + 15, o + 128, 16, 0, 8), [[-1, 8]], 0, 1.0)
-    ent("NDF", 0, 0, 1.0)
-    ent("NDF", 1, 1, 1.0)
-    for k, v in ((4, 256.0), (5, 1.0), (12, 256.0), (13, 1.0)):
-        ent("WHV", k, 15, v)
-    for nm, k, v in (("WL", 10, 32.0), ("WL", 11, 1.0), ("WX", 10, 32.0), ("WX", 11, 1.0), ("WX", 6, 512.0), ("WXS", 14, 512.0), ("WXS", 7, 512.0)):
-        ent(nm, k, 15, v)
-    for c in (0, 2, 4):
-        for k in (0, 8):
-            ent("NRS", k, c, 1.0)
-            ent("NRS", k + 1, c + 1, 1.0)
-    b, o = MOFF["YO"]
-    for j, k, v in ((0, 4, 32.0), (0, 5, 1.0), (1, 2, 32.0), (1, 3, 1.0)):
-        put(A(b, o + j, o + 16, 2), [[-16, 8]], -k, v)
+    b, o = MOFF["SG"]
+    SELG, SELV = A(b, o, o + 8), A(b, o + 8, o + 16)
+    put(SELG, [[-16, 8]], -15, -1.0)
+    put(SELV, [[-16, 8]], -15, -BIG)
+    put(SELV, [[-16, 8]], -4, -BIG)
+    for c in (10, 13):
+        for k, v in NEWG:
+            ent("WNM", k, c, v)
+    for c, v in ((0, 1), (1, 1), (4, 1), (5, 1), (8, 1), (9, 1), (14, -768), (15, 2)):
+        ent("WNM", 9, c, v)
+    ent("LD6", 5, 14, 1.0)
+    ts(A("ld", 0, Q), A("iof", 0, Q), LDM, None, AL.mult)
+    one32 = A("ones", 0, Q, 1, 0, 32)
+    DJ, DQ = M("DJ0", 32, Q), [M("DQ0", 32, Q), M("DQ4", 32, Q)]
+    sel(DJ, one32, [[0, 16], [-1, 32]], AL.is_equal, 0.0, 0, 1)
+    for e in (0, 1):
+        sel(DQ[e], one32, [[-2, 16], [0, 32]], AL.is_equal, 0.0, -e, 1)
+        iota(M("MK%d" % e, 32), [[0, 128]], int(BIG), 0)
+        keep(M("MK%d" % e, 32), M("MK%d" % e, 32), [[0, 8], [1, 16]], -1, 16 * e)
 
-    ts(A("sw0", 1600, 2112), A("qpi", 0, Q), 1 / 16, None, AL.mult)
-    cp(A("qf", 0, Q, 1, 0, 8), A("qni", 0, Q, 1, 0, 8))
-    act(A("qh", 0, Q, 1, 0, 8), A("qf", 0, Q, 1, 0, 8), AF.Identity, 129 - 15.5 / 32, 1 / 32)
-    ts(A("qh", Q, 2 * Q, 1, 0, 8), A("qh", 0, Q, 1, 0, 8), -129.0, None, AL.add)
-    p = tile()
-    mm(A(p, 0, Q), [(A("qfm", 0, 128, 1, 0, 8), A("qf", 0, Q, 1, 0, 8)), (M("QH", 8), A("qh", Q, 2 * Q, 1, 0, 8))])
-    act(A("nd0", 0, Q), A(p, 0, Q), AF.Identity, BH)
+    s0, s1 = SEG
+    ts(A("sw0", s0["O"], s0["On"]), A("qpi", 0, Q), 1 / 256, None, AL.mult)
+    ts(A("nd0", 0, Q), A("qni", 0, Q), mkc(5), nmk(5), AL.mult, AL.add)
+    send("02", A("sw0", s0["O"], s0["On"]), A("sw0", 0, Q), 4000)
 
     for j in range(8):
         c0, c1 = 512 * j, 512 * j + 512
-        ts(A("zt", TAB + c0, TAB + c1), A("raw", c0, c1), 1 / 256, 9 - 7.5 / 256, AL.mult, AL.add)
+        ts(A("zt", TAB + c0, TAB + c1), A("raw", c0, c1), 1 / 4096, -1 - 7.5 / 4096, AL.mult, AL.add)
         p = tile()
-        mm(A(p, 0, Q), [(M("I16"), A("raw", c0, c1)), (M("IM16"), A("zt", TAB + c0, TAB + c1))])
-        either(A("kt", c0, c1), A(p, 0, Q), 144.0)
-    ms(A("zt", 0, TAB), 9.0)
-    ts(A("nt", 0, TAB), A("ones", 0, TAB), DUMC, None, AL.mult)
+        mm(A(p, 0, Q), [(M("I"), A("raw", c0, c1)), (M("IM"), A("zt", TAB + c0, TAB + c1))])
+        either(A("kt", c0, c1), A(p, 0, Q), -16.0, 1 / 256)
+    ms(A("zt", 0, TAB), -1.0)
+    ms(A("kt", W, W + CH), 0.0)
+    ms(A("nt", TAB + W, TAB + W + CH), 0.0)
+    dma("Y", A("pk", 0, Q), A("iof", 0, Q), "z_b", 2500)
+    either(A("nt", 0, TAB), A("ones", 0, TAB), 0.0, DUMC)
     F = lambda i: A("ft", 256 * i, 256 * i + 256)
-    raw, kind, hi, lo = [A("nki", 256 * i, 256 * i + 256) for i in range(4)]
+    raw, kind, node = [A("nki", 256 * i, 256 * i + 256) for i in range(3)]
+    val, quo, low, nof, nq, nl, nv, vc, ix, one = [F(i) for i in range(10)]
     ts(kind, raw, 3, None, AL.bitwise_and)
-    ts(hi, raw, 7, None, AL.arith_shift_right)
-    ts(lo, raw, 2, 31, AL.arith_shift_right, AL.bitwise_and)
-    ts(F(0), kind, 1.0, None, AL.is_equal)
-    ts(F(1), kind, 2.0, None, AL.not_equal)
-    ts(F(2), kind, 0.0, None, AL.is_equal)
-    ts(F(3), kind, 3.0, None, AL.is_equal)
-    act(F(8), F(3), AF.Identity, 0.0, SC1)
+    ts(node, raw, 2, None, AL.arith_shift_right)
+    ts(val, kind, 3.0, None, AL.is_equal)
+    ts(quo, kind, 1.0, None, AL.is_equal)
+    ts(low, kind, 2.0, None, AL.is_lt)
+    cp(nof, node)
+    either(ix, A("iof", 0, 256), IXB)
+    iota(one, [[0, 256]], 1, 0)
     p = tile()
-    mm(A(p, 0, 256), [(M("I"), F(3))])
-    tt(F(9), A("i256", 0, 256), A(p, 0, 256), AL.mult)
-    for f, o in ((0, 4), (1, 6)):
-        p = tile()
-        for j in (0, 256):
-            mm(A(p, j, j + 256), [(M("NI"), F(f)), (M("I"), A("ones", 0, 256))])
-        tt(A("ft", 256 * o, 256 * o + 512), A("nki", 512, 1024), A(p, 0, 512), AL.mult)
-    one = A("ones", 0, 256)
-    rows = [F(0), F(0), F(1), F(1), one, one, F(0), F(2), F(4), F(5), F(6), F(7), F(8), F(9), F(2), F(3)]
-    for j in (4, 5, 0, 1, 6, 2, 3, 7, 14, 15, 12, 13, 8, 9, 10, 11):
-        dma("Y", A("nt", TAB, TAB + W, 1, j, 128, 16), rows[j], "l_nt", 2500)
-    p = tile()
-    mm(A(p, 0, Q), [(R1(384), A("iq", 0, Q, 1, 0, 1)), (R1(512), A("iq", Q, 2 * Q, 1, 0, 1)), (R1(640), A("ones", 0, Q, 1, 0, 1))])
-    act(A("wn", 0, Q), A(p, 0, Q))
-    p = tile()
-    mm(A(p, 0, Q), [(R1(128), A("iq", 0, Q, 1, 0, 1)), (R1(256), A("iq", Q, 2 * Q, 1, 0, 1))])
-    act(A("ld", 0, Q), A(p, 0, Q))
+    mm(A(p, 0, 256), [(I32, nof)])
+    mm(A(p, 256, 512), [(I32, ix)])
+    for o, f in ((nq, quo), (nl, low), (nv, val)):
+        tt(o, f, A(p, 0, 256), AL.mult)
+    tt(vc, val, A(p, 256, 512), AL.mult)
+    rows = [val, one, quo, low, one, one, quo, low, quo, one, nof, nq, nl, nv, vc, val]
+    for j in (1, 4, 5, 9, 0, 15, 2, 6, 8, 3, 7, 10, 11, 12, 13, 14):
+        dma("Y", A("nt", TAB, TAB + W, 1, j, 128, 16), rows[j], "l_nt", 2200, [A("raw", 1024, 1025)], 700.0)
 
-    SEG = [{"aO": 0, "aP": 192, "aX": 384, "P2": 576, "P1": 1088, "X0": 1600, "P0": 1600, "O": 1600, "On": 2112, "end": 2624},
-           {"aP": 0, "aX": 192, "P2": 384, "P1": 896, "X0": 1408, "P0": 1920, "O": 2432, "On": 2944, "end": 3456}]
-    for t in (0, 1):
-        for i, a in enumerate((192 + Q, SEG[t]["On"] - SEG[t]["aP"], SEG[t]["On"] - SEG[t]["aX"], SEG[t]["On"])[:4 - t]):
-            iota(A("w4", 128 * t + 32 * i, 128 * t + 32 * i + 32), [[16, 32]], a, 0)
-    act(A("st", 128, 352), A("w4", 0, 224), AF.Identity, KC)
-    iota(A("pr", 96, 128), [[0, 32]], 0, 0)
+    for i, a in enumerate((384, s0["On"] - s0["aP"], s0["On"] - s0["aX"], 384, s1["On"], s1["On"] - s1["aX"], 2 * CAP, CAP)):
+        iota(B("w4", i), [[16, 32]], a, 0)
+    iota(B("w4", 8), [[0, 16], [16, 2]], W - 2048, 0)
+    either(B("st", 0, 9), B("w4", 0, 9), KC)
+    cp(B("sh", 0, 2), B("st", 6, 2))
+    ts(B("sh", 4), B("st", 7), -1.0, Q - 1.0 + CAP, AL.mult, AL.add)
+    iota(B("un", 5), [[0, 32]], CAP, 0)
+    iota(B("un", 6), [[0, 32]], 2, 0)
 
-    def step(t, s, c0, c1):
-        n, sw, seg, nd = c1 - c0, "sw%d" % t, SEG[t], "nd%d" % t
-        q0, q1 = c0 // 16, c1 // 16
-        top = EXT if t == 0 else EXT + Q
-        pin = seg["P0"] if s == 0 else seg["P1"]
-        P = A(sw, pin + c0, pin + c1)
-        C = lambda nm, o=0: A(nm, o + c0, o + c1)
-        if s == 0:
-            p = tile()
-            mm(A(p, 0, n), [(M("NS1"), C(nd))])
-            either(C("ns"), A(p, 0, n), BH)
+    def hashes(t, s, c0, c1):
+        n, C = c1 - c0, lambda nm, o=0: A(nm, o + c0, o + c1)
+        P = C("sw%d" % t, SEG[t]["P1" if s else "P0"])
         p = tile()
         mm(A(p, 0, n), [(M("WU"), P)])
         mm(A(p, 256, 256 + n), [(M("WV"), P)])
         either(C("ue"), A(p, 0, n))
         tt(C("xf"), A(p, 256, 256 + n), C("ue"), AL.mult)
         p = tile()
-        mm(A(p, 0, n), [(M("NL0"), C(nd)) if s == 0 else (M("NL1"), C("rr"))], after=[C("ue")])
+        mm(A(p, 0, n), [(M("NL1"), C("rr")) if s else (M("NL0"), C("nd%d" % t))], after=[C("ue")])
         tt(C("xi"), A(p, 0, n), C("xf"), AL.add)
         ts(C("xi", Q), C("xi"), 5, W - 1, AL.arith_shift_right, AL.bitwise_and)
         cp(C("hu"), C("xi", Q))
-        ho = Q if (t, s) == (0, 0) else 0
-        ts(C("hs", ho), C("hu"), -2048.0, None, AL.add)
-        if (t, s, c0) == (1, 0, 0):
-            for j in (3, 2, 1, 0):
-                cp(IND(A("nt", TAB, TAB + 5120), A("ow", 8 * j, 8 * j + 8)), A("wn", 128 * j, 128 * j + 128))
-                ops[-1]["ins"].append(C("hu"))
-        for a in range(c0, c1, SCH):
-            e = min(a + SCH, c1)
-            either(A("gk", 16 * a, 16 * e), IND(A("kt", 0, W), A("hu", a, e)), 0.0, -1.0)
+        ts(C("hs", Q if (t, s) == (0, 0) else 0), C("hu"), -2048.0, None, AL.add)
+
+    def step(t, s, c0, c1):
+        n, sw, seg, nd = c1 - c0, "sw%d" % t, SEG[t], "nd%d" % t
+        q0, q1 = c0 // 16, c1 // 16
+        pin = seg["P1" if s else "P0"]
+        C = lambda nm, o=0: A(nm, o + c0, o + c1)
+        P, X, R = C(sw, pin), C(sw, seg["X0"]), C("rr", s * Q)
         pc = tile()
-        cut = [c0 + (n * i // SUB) // 16 * 16 for i in range(SUB)] + [c1]
-        for d0, d1 in zip(cut, cut[1:]):
-            compare(pc, A(sw, pin + d0, pin + d1), c0, c1, d0, d1)
-        ts(C("mt"), A(pc, 0, n), S1, THR, AL.max, AL.is_equal)
+        for d0, d1 in spans([c for c in PARTS[s] if c0 <= c <= c1]):
+            compare(pc, A(sw, pin + d0, pin + d1), c0, c1, d0, d1, [(M("VAL"), A("rr", d0, d1))] if s else [])
+        act(C("mt"), A(pc, 0, n), AF.Sign, THR, -1.0)
         p = tile()
         mm(A(p, 0, n), [(M("TRI2"), C("mt"))])
-        either(C("lt"), A(p, 0, n), sign=True)
+        either(C("lt"), A(p, 0, n), LTB, func=AF.Sign)
         p = tile()
-        mm(A(p, 0, n), [(M("SEL"), C("mt")), (M("I"), C("hs", ho))])
-        ts(C("tm"), A(p, 0, n), BIG - 2049.0, 1.0 - BIG, AL.max, AL.add)
+        mm(A(p, 0, n), [(M("SEL"), C("mt")), (M("I"), C("hs", Q if (t, s) == (0, 0) else 0))])
+        ts(C("tm"), A(p, 0, n), TA, -2050.0, AL.add, AL.max)
         p = tile()
-        narrow(A(p, 0, q1 - q0), "E", "tm", c0, c1)
+        mmx(A(p, 0, q1 - q0), rows16("CW16", "tm", c0, c1))
         hb = A("hb", q0, q1)
-        ts(hb, A(p, 0, q1 - q0), 16 * 2048.0 - 1 + TAB, None, AL.add)
-        tt(C("rr", s * Q), IND(A("nt", 0, top), hb), C("ns", s * Q), AL.mult)
-        tt(C("ab"), IND(A("zt", 0, top), hb), C("lt"), AL.mult)
-        if (t, s) == (0, 0):
-            tt(C("ab", Q), P, C("lt"), AL.max)
-        else:
-            p = tile()
-            narrow(A(p, 0, q1 - q0), "WB", "rr", s * Q + c0, s * Q + c1, [(M("I"), A("q16", q0, q1))])
-            ob = A("ob", q0, q1)
-            ts(ob, A(p, 0, q1 - q0), KC, 512.0 if s == 0 else 0.0, AL.add, AL.add)
-            w0 = seg["X0"] if s == 0 else seg["P1"]
-            tt(C("ab", Q), IND(A(sw, w0, w0 + 1024), ob), C("lt"), AL.max)
+        ts(hb, A(p, 0, q1 - q0), 15 * 2050.0 + 2048 + TAB, None, AL.add)
+        tt(R, IND(A("nt", 0, TAB + W), hb), C("ns") if s else C(nd), AL.mult)
+        tt(C("ab"), IND(A("zt", 0, TAB + W), hb), C("lt"), AL.add)
         p = tile()
-        mm(A(p, 0, n), [(M("I"), C("ab")), (M("IM9"), C("lt")), (M("I"), C("ab", Q))])
-        either(C(sw, seg["P1"] if s == 0 else seg["P2"]), A(p, 0, n))
+        if (t, s) == (0, 0):
+            mm(A(p, 0, n), [(M("NI"), C("lt")), (M("I"), P)])
+        else:
+            mm(A(p, 0, n), [(M("I"), X), (M("NI"), P), (M("QP"), R)], after=[C("lt")])
+            either(C("ab", Q), A(p, 0, n), -7 / 8, func=AF.Relu)
+            p = tile()
+            mm(A(p, 0, n), [(M("NI"), C("lt")), (M("I"), P), (M("QN"), R), (M("I"), C("ab", Q))], after=[R])
+        tt(C(sw, seg["P2" if s else "P1"]), A(p, 0, n), C("ab"), AL.max)
         p = tile()
         if s == 0:
-            mm(A(p, 0, n), [(M("NS2"), C("rr"))])
-            either(C("ns", Q), A(p, 0, n), BH)
+            mm(A(p, 0, n), [(M("NS2"), R)])
+            either(C("ns"), A(p, 0, n), nmk(7))
         else:
-            mm(A(p, 0, n), [(M("NDR"), C("rr", Q)), (M("NDF"), C(nd)), (M("I"), C("ld"))])
-            either(C("nw%d" % t, 208), A(p, 0, n), BH)
-        if (t, s) == (0, 0):
-            p = tile()
-            mm(A(p, 0, n), [(M("PLA"), C("hs", Q))])
-            act(C("pa"), A(p, 0, n))
-            p = tile()
-            narrow(A(p, 0, q1 - q0), "WPL", "hs", Q + c0, Q + c1)
-            act(A("pb", q0, q1), A(p, 0, q1 - q0))
+            mm(A(p, 0, n), [(M("NDR"), R), (M("I"), C("ld"))], after=[R])
+            either(C("nw%d" % t, 400), A(p, 0, n))
 
-    def compare(pc, P, b0, b1, c0, c1):
+    def compare(pc, P, b0, b1, c0, c1, more):
         n = c1 - c0
         K = lambda m: A("gk", 16 * c0 + m - 1, 16 * c1, 16)
-        NE = lambda i: A("ne", 9 * c0 + i * n, 9 * c0 + (i + 1) * n)
-        out = A(pc, c0 - b0, c1 - b0)
-        mm(out, [(M("D1"), K(1)), (M("D2"), K(2)), (M("D3"), K(3)), (M("DP"), P)], c0 == b0, False)
-        pp = tile()
+        NE = lambda i, k=1: A("ne", NT * c0 + i * n, NT * c0 + (i + k) * n)
         late = 16 * max(c0, c1 - LEAD)
+        pp = tile()
         mm(A(pp, 0, n), [(M("NI"), P)], after=[A("gk", late, late + 1)])
-        per = min(4, 512 // n)
-        for i in range(0, 4, per):
-            p = tile()
-            k = min(per, 4 - i)
-            for j in range(k):
-                a, e = PACKS[i + j]
-                mm(A(p, j * n, j * n + n), [(M("A%d" % a), K(a)), (M("B%d" % a), K(e)), (M("P%d" % a), P)])
-            ts(A("ne", 9 * c0 + i * n, 9 * c0 + (i + k) * n), A(p, 0, k * n), 0.0, None, AL.not_equal)
         for i, m in enumerate(PLAIN):
-            tt(NE(4 + i), K(m), A(pp, 0, n), AL.not_equal)
-        mm(out, [(MW("CW%d" % m, m - 1), NE(4 + i)) for i, m in enumerate(PLAIN[:2])]
-           + [(M("C%d" % a), NE(i)) for i, (a, e) in enumerate(PACKS)]
-           + [(MW("CW%d" % m, m - 1), NE(6 + i)) for i, m in enumerate(PLAIN[2:])], False, c1 == b1)
+            tt(NE(NP + i), K(m), A(pp, 0, n), AL.not_equal)
+        per = -(-NP // -(-NP * n // 512))
+        per = min(per, 512 // n)
+        for i in range(0, NP, per):
+            p, k = tile(), min(per, NP - i)
+            for j in range(k):
+                mmx(A(p, j * n, j * n + n), [(M("K%d" % m), K(m)) for m, r in PACKS[i + j]] + [(M("P%d" % (i + j)), P)])
+            either(NE(i, k), A(p, 0, k * n), func=AF.Abs, shy=0.0 if more and c0 >= SOFT else -NSHY)
+        mm(A(pc, c0 - b0, c1 - b0), [(MW("CW%d" % m, m - 1), NE(NP + i)) for i, m in enumerate(PLAIN)] + more
+           + [(M("C%d" % i), NE(i)) for i in range(NP)], c0 == b0, c1 == b1)
 
-    def send(t, j, src, dst, ns):
-        add("G", "send", [], [src], (t, j, src, dst), 1500.0)
-        add("R", "recv", [dst], [], (t, j, len(ops) - 1), 0.0, "in%d%d" % (t, j), ns)
+    def close(t, c0, c1):
+        sw, seg, nw = "sw%d" % t, SEG[t], "nw%d" % t
+        n, q0, q1 = c1 - c0, c0 // 16, c1 // 16
+        k = q1 - q0
+        N = lambda nm, o=0: A(nm, o + q0, o + q1)
+        p = tile()
+        mmx(A(p, 0, k), rows16("WHV", "rr", Q + c0, Q + c1))
+        ts(N("un"), A(p, 0, k), 0.0, None, AL.is_le)
+        cp(N("ov"), A(p, 0, k))
+        either(N("un", 128), A(p, 0, k), 0.0, -1.0, AF.Relu)
+        init = A("un", 31 + q0, 32 + q0) if q0 else 0.0
+        add("V", "scan", [N("un", 32)], [N("ones"), N("un")] + ([init] if q0 else []), (N("un", 32), N("ones"), N("un"), init), price(FIX, 64))
+        tt(N("xv"), N("un"), N("sh", 128), AL.mult)
+        p = tile()
+        mm(A(p, 0, k), [(M("I"), N("sh", 128)), (M("NTRI"), N("un")), (M("NI"), N("xv")), (M("BD"), N("un", 32))], after=[N("un")])
+        cp(N("po"), A(p, 0, k))
+        cp(IND(A("pk", 0, Q), N("po")), A(nw, 400 + c0, 400 + c1))
+        zv = A("zt", EXT + c0, EXT + c1) if t == 0 else A("zv", c0, c1)
+        O = A(sw, seg["O"] + c0, seg["O"] + c1)
+        either(zv, IND(A("zt", 0, EXT if t == 0 else EXT + Q), N("ov")))
+        p = tile()
+        mm(A(p, 0, n), [(M("I"), zv), (M("I"), O)])
+        act(A("zv", Q + c0, Q + c1), A(p, 0, n), AF.Sign, 1 - 15.5 / 256)
+        p = tile()
+        mm(A(p, 0, n), [(M("IH"), A("zv", Q + c0, Q + c1)), (M("I"), zv), (M("I"), O)])
+        either(A(sw, seg["On"] + c0, seg["On"] + c1), A(p, 0, n), 1 - 1 / 32)
+
+    def places():
+        p = tile()
+        mmx(A(p, 0, 32), rows16("WPL", "hs", Q, 2 * Q))
+        cp(B("sh", 5), A(p, 0, 32))
+        p = tile()
+        mmx([A(p, r, 128, 16, 0, 32) for r in range(16)], [(A("hs", Q + r, 2 * Q, 16), SELG) for r in range(16)])
+        act(A("dc", 0, 128, 1, 0, 32), A(p, 0, 128, 1, 0, 32), AF.Identity, BIG)
+
+    def write():
+        O, un = SEG[0]["O"], B("un", 0)
+        p = tile()
+        mm(A(p, 0, Q), [(M("WNM"), A("rr", Q, 2 * Q)), (M("LD6"), A("ld", 0, Q))])
+        either(A("wn", 0, Q), A(p, 0, Q))
+        p = tile()
+        mmx([A(p, r, 128, 16, 0, 32) for r in range(16)], [(A("rr", Q + r, 2 * Q, 16), SELV) for r in range(16)])
+        pt = A("pt", 0, 128, 1, 0, 32)
+        tt(pt, A(p, 0, 128, 1, 0, 32), A("dc", 0, 128, 1, 0, 32), AL.add)
+        for e in (0, 1):
+            p = tile()
+            mm(A(p, 0, Q), [(M("PLA"), A("hs", Q, 2 * Q)), (M("MK%d" % e, 32), DJ), (pt, DQ[e])], after=[A("hb", 30, 32)])
+            either(A("ee", e * Q, e * Q + Q), A(p, 0, Q), func=AF.Abs, shy=1e6 * e)
+        p = tile()
+        mmx(A(p, 0, 64), rows16("CW16", "ee", 0, 2 * Q))
+        either(B("un", 7, 2), A(p, 0, 64), 16 * BIG, -BIG)
+        p = tile()
+        mm(A(p, 0, 32), [(M("I"), B("sh", 5)), (M("IC"), un), (M("I"), B("un", 7)), (M("I"), B("un", 8))], after=[B("un", 7)])
+        tt(B("sm", 0), A(p, 0, 32), B("st", 8), AL.min)
+        ts(A("ow", 0, 32), B("sm", 0), 2048.0, None, AL.add)
+        for a in range(Q - CH, -1, -CH):
+            off = A("ow", a // 16, (a + CH) // 16)
+            cp(IND(A("kt", 0, W + CH), off), A("sw0", O + a, O + a + CH))
+            cp(IND(A("nt", TAB, TAB + W + CH), off), A("wn", a, a + CH))
 
     def finish(t):
-        sw, seg, nd, nw, sb = "sw%d" % t, SEG[t], "nd%d" % t, "nw%d" % t, "sb%d" % t
-        top = EXT if t == 0 else EXT + Q
-        ns = 4 if t == 0 else 3
-        un, sc, kp, ov = A("un", 0, 32), A("un", 32, 64), A("kp", 0, 32), A("ov", 0, 32)
-        S = lambda i: A("sm", 32 * i, 32 * i + 32)
-        O = A(sw, seg["O"], seg["O"] + Q)
+        sw, seg, nw, sb, sn, ar = "sw%d" % t, SEG[t], "nw%d" % t, "sb%d" % t, "sn%d" % t, "ar%d" % t
+        un, sc, nl, gone = B("un", 0), B("un", 1), B("un", 2), B("un", 3)
         p = tile()
-        narrow(A(p, 0, 32), "WHV", "rr", Q, 2 * Q)
-        ts(un, A(p, 0, 32), 0.0, None, AL.is_equal)
-        cp(ov, A(p, 0, 32))
-        add("V", "scan", [sc], [A("ones", 0, 32), un], (sc, A("ones", 0, 32), un), FIX + 64 * CY)
+        mm(A(p, 128, 144), [(M("BD"), A("un", 48, 64))])
+        mm(B(p, 0), [(M("BD"), sc), (M("TRK"), un)])
+        ts(A(sn, 0, 16), A(p, 128, 144), float(CAP), None, AL.min)
+        either(B("kp", 0), B(p, 0), 2047.0)
+        ts(A(sn, 16, 208), A("pk", 0, CAP), mkc(6), None, AL.mult)
+        cp(A(sn, 208, 400), A("pk", 0, CAP))
+        send("%d0" % t, A(sn, 0, 208), A(ar, 0, 208), 2500)
         p = tile()
-        mm(A(p, 0, 32), [(M("BD"), sc), (M("TRK"), un)])
-        tt(S(0), A(p, 0, 32), A("st", 64, 96), AL.min)
-        ts(A("po", 0, 32), S(0), 2047.0, None, AL.add)
-        cp(IND(A(sb, 592, 1616), A("po", 0, 32)), A(nw, 208, 208 + Q))
+        mmx(A(p, 0, 24), rows16("WL", sn, 16, 400))
+        cp(A("ol", 0, 24), A(p, 0, 24))
+        either(A(sb, 0, 192), IND(A(sw, seg["P2"], seg["P2"] + Q), A("ol", 0, 12)))
+        either(A(sb, 192, 384), IND(A(sw, seg["P2"], seg["P2"] + 1536), A("ol", 12, 24)))
+        send("%d1" % t, A(sb, 0, 384), A(sw, seg["aP"], seg["P2"]), 3000)
         p = tile()
-        mm(A(p, 128, 130), [(M("BD"), A("un", 62, 64))])
-        for i in range(ns):
-            mm(A(p, 32 * i, 32 * i + 32), [(M("BD"), sc), (M("TRK"), un)])
-        ts(A(sb, 576, 578), A(p, 128, 130), float(CAP), None, AL.min)
-        either(A("kp", 0, 32 * ns), A(p, 0, 32 * ns), 2047.0)
-        send(t, 0, A(sb, 576, 784), A(nw, 0, 208), 2500)
-        for j, wide in ((0, "WL"), (12, "WX")):
-            p = tile()
-            narrow(A(p, 0, 12), wide, sb, 592, 784)
-            ts(A("ol", j, j + 12), A(p, 0, 12), -33.0, None, AL.add)
-        either(A(sb, 192, 384), IND(A(sw, seg["P2"], seg["P2"] + Q), A("ol", 0, 12)))
-        either(A(sb, 384, 576), IND(A(sw, seg["P2"], seg["P2"] + 1536), A("ol", 12, 24)))
+        mm(A(p, 0, CAP), [(M("NRS"), A(sn, 16, 208))])
+        either(A(nw, 208, 400), A(p, 0, CAP))
         if t == 0:
-            either(A(sb, 0, 192), IND(O, A("ol", 0, 12)))
-            send(t, 1, A(sb, 0, 576), A(sw, 0, seg["P2"]), 3500)
-        else:
-            send(t, 1, A(sb, 192, 576), A(sw, 0, seg["P2"]), 3000)
-        zv = A("zt", EXT, EXT + Q) if t == 0 else A("zv", 0, Q)
-        act(zv, IND(A("zt", 0, top), ov))
+            write()
+        ts(nl, B("kp", 0), float(CAP), None, AL.is_ge)
         p = tile()
-        mm(A(p, 0, Q), [(M("I"), zv), (M("I"), O)])
-        act(A("zv", Q, 2 * Q), A(p, 0, Q), AF.Sign, -9.96875)
+        mm(B(p, 0), [(M("I"), B("un", 5)), (M("BD"), sc), (M("NTRI"), un), (M("IC"), nl)], True, False, [nl])
+        for i in (1, 2):
+            mm(B(p, i), [(M("I"), B("sh", i - 1)), (M("IC"), B("un", 6)), (M("NC"), un), (M("NC"), nl)], False, False)
+        mm(B(p, 2), [(M("I"), B("un", 4))], False, True)
+        tt(A("t4", 0, 96), A(p, 0, 96), B("st", 3 * t, 3), AL.min)
+        cp(A(nw, 0, 208), A(ar, 0, 208))
+        ts(gone, B("kp", 0), A(nw, 15, 16), BIG, AL.is_ge, AL.mult)
         p = tile()
-        mm(A(p, 0, Q), [(M("IH"), A("zv", Q, 2 * Q)), (M("I"), zv), (M("I"), O)])
-        act(A(sw, seg["On"], seg["On"] + Q), A(p, 0, Q), AF.Identity, -9.5)
-        rv = A("nt", EXT, EXT + Q) if t == 0 else A("re2", 0, Q)
-        tt(rv, IND(A("nt", 0, top), ov), A(nd, 0, Q), AL.mult)
-        p = tile()
-        mm(A(p, 0, Q), [(M("NRS"), rv)])
-        act(A(nw, 208 + Q, 208 + 2 * Q), A(p, 0, Q), AF.Identity, BH)
-        if t == 0:
-            act(A("pb", 96, 128), A("pb", 0, 32), AF.Identity, 0.0, -1.0)
-            for q in range(32):
-                e = 128 * (q // 8 + 1)
-                eq = A("ee", 128 * q, 128 * q + e - 16 * q)
-                if q < SQ:
-                    d = A("du", 128 * (q % 4), 128 * (q % 4) + e - 16 * q)
-                    act(d, A("pa", 16 * q, e), AF.Abs, A("pb", 96 + q, 97 + q))
-                    act(eq, d, AF.Relu, BIG, -BIG)
-                else:
-                    ts(eq, A("pa", 16 * q, e), A("pb", q, q + 1), BIG, AL.is_equal, AL.mult)
-            for r in range(16):
-                either(A("ee", r, W, 128), A("ee", r, W, 128), 0.0, mkc(r))
-            for j in range(8):
-                x = A("lv", j, 256, 8)
-                if j % 2:
-                    act(x, un, AF.Identity, col(32 + j), col(40 + j))
-                else:
-                    ts(x, un, col(40 + j), col(32 + j), AL.mult, AL.add)
-            p = tile()
-            mm([A(p, 16 * q, 128 * (q // 8 + 1), 1, 0, 8) for q in range(32)],
-               [(A("lv", 8 * q, 8 * q + 8), A("ee", 128 * q, 128 * q + 128 - 16 * (q % 8))) for q in range(32)])
-            either(A("du", 0, Q, 1, 0, 8), A(p, 0, Q, 1, 0, 8))
-            p = tile()
-            narrow(A(p, 0, 32), "W8", "du", 0, Q, [(M("IC"), un)], 8)
-            act(A("pb", 64, 96), A("pb", 0, 32), AF.Identity, 2048.0)
-            tt(S(6), A(p, 0, 32), A("pb", 64, 96), AL.add)
-            tt(S(7), S(6), A("st", 32, 64), AL.min)
-            cp(A("ow", 0, 32), S(7))
-            for j in (3, 2, 1, 0):
-                cp(IND(A("kt", 0, 5120), A("ow", 8 * j, 8 * j + 8)), A(sw, seg["O"] + 128 * j, seg["O"] + 128 * j + 128))
-        B = lambda nm, i: A(nm, 32 * i, 32 * i + 32)
-        back = float(seg["P2"] - seg["On"])
-        act(S(1), kp, AF.Abs, -608.0)
-        p = tile()
-        narrow(A(p, 0, 32), "WXS", "rr", Q, 2 * Q)
-        act(S(4), A(p, 0, 32), AF.Identity, -back / 512, -1 / 512)
-        ts(B("pr", 0), S(1), 416.5, -512.0, AL.is_lt, AL.mult)
-        ts(B("pr", 1), S(1), 416.5, back, AL.is_lt, AL.mult)
-        tt(B("pr", 2), B("pr", 0), S(4), AL.mult)
-        n = 32 * ns
-        tt(A("pr", 128, 128 + n), A("pr", 0, n), A("st", 128 + 128 * t, 128 + 128 * t + n), AL.add)
-        ts(A("t4", 0, n), A("kp", 0, n), A(nw, 1, 2), BIG, AL.is_ge, AL.mult)
-        tt(A("t4", 128, 128 + n), A("t4", 0, n), A("kp", 0, n), AL.max)
-        tt(A("t4", 256, 256 + n), A("t4", 128, 128 + n), A("pr", 128, 128 + n), AL.min)
-        cp(A("of", 0, n), A("t4", 256, 256 + n))
-        nwin = A(nw, 16, 1232)
+        for i in range(3):
+            mm(B(p, i), [(M("BD"), sc), (M("NTRI"), un), (M("I"), gone)], i == 0, i == 2, [nl])
+        tt(A("t4", 128, 224), A(p, 0, 96), A("t4", 0, 96), AL.min)
+        cp(A("of", 0, 96), A("t4", 128, 224))
+        nwin = A(nw, 16, 912)
         win = lambda a: A(sw, seg[a], seg["end"])
         if t == 0:
-            for c0, c1 in zip(CUTS, CUTS[1:]):
+            for c0, c1 in spans(HASH[0]):
                 off = lambda i: A("of", 32 * i + c0 // 16, 32 * i + c1 // 16)
-                either(A("nd1", c0, c1), IND(nwin, off(0)))
-                for i, a, x in ((1, "aP", "P0"), (2, "aX", "X0"), (3, "aO", "O")):
-                    either(A("sw1", SEG[1][x] + c0, SEG[1][x] + c1), IND(win(a), off(i)))
+                ts(A("nd1", c0, c1), IND(nwin, off(0)), mkc(6), nmk(6), AL.mult, AL.add)
+                for i, a, x in ((1, "aP", "P0"), (2, "aX", "X0")):
+                    either(A("sw1", s1[x] + c0, s1[x] + c1), IND(win(a), off(i)))
+            p = tile()
+            mmx(B(p, 0), rows16("WL", "nd1", 0, Q) + [(M("IO"), gone)])
+            ts(A("oo", 0, 32), B(p, 0), -1.0, None, AL.add)
+            either(A("sw1", s1["O"], s1["On"]), IND(win("aO"), A("oo", 0, 32)))
         else:
             either(A("nd2", 0, Q), IND(nwin, B("of", 0)))
-            p = tile()
-            mm(A(p, 0, Q, 1, 0, 16), [(M("YO", 128, 16), A("nd2", 0, Q))])
-            either(A("yq", 0, Q, 1, 0, 16), A(p, 0, Q, 1, 0, 16))
-            dma("Y", "yn", A("yq", 0, Q, 1, 0, 16), "o_n", 2000)
+            for h, k in ((0, 4), (Q, 2)):
+                dma("Y", ["yn", h, h + Q], A("nd2", 0, Q, 1, k, 128, 16), "o_n", 2000)
             for j, a in ((0, "aP"), (1, "aX")):
                 for h in (0, 256):
-                    either(A("ys", j * Q + h, j * Q + h + 256), IND(win(a), A("of", 32 + 32 * j + h // 16, 48 + 32 * j + h // 16)), 0.0, 16.0)
-            for h in (0, 512, 256, 768):
-                dma("Y", ["yp", h, h + 256], A("ys", h, h + 256), "o_p", 2200)
+                    either(A("ys", j * Q + h, j * Q + h + 256), IND(win(a), A("of", 32 + 32 * j + h // 16, 48 + 32 * j + h // 16)), 0.0, 256.0)
+            for h, e in ((0, "Y"), (Q, "S")):
+                dma(e, ["yp", h, h + Q], A("ys", h, h + Q), "o_p", 2200)
 
     for t in (0, 1):
         for s in (0, 1):
-            for c0, c1 in zip(CUTS, CUTS[1:]):
+            for c0, c1 in spans(HASH[s]):
+                hashes(t, s, c0, c1)
+            for a, e in spans(KEYS[s]):
+                either(A("gk", 16 * a, 16 * e), IND(A("kt", 0, W), A("hu", a, e)), 0.0, -1.0, shy=GSHY)
+            for c0, c1 in spans(TAIL[s]):
                 step(t, s, c0, c1)
+        if t == 0:
+            places()
+        for c0, c1 in spans(SHUT):
+            close(t, c0, c1)
         finish(t)
     return ops
 
 
-def plan():
-    best = p = forward(None)
-    for _ in range(TURNS):
-        p = forward(backward(p))
-        if p[5] < best[5]:
-            best = p
-    return best
-
-
-def backward(p):
-    ops = p[0]
-    n = len(ops)
-    succ = [[] for _ in range(n)]
-    for i in range(n):
-        for j in ops[i]["all"]:
-            succ[j].append(i)
-    left = [len(s) for s in succ]
-    ready = set(i for i in range(n) if not left[i])
-    done, free = [0.0] * n, {}
-    while ready:
-        c = []
-        for i in ready:
-            o = ops[i]
-            st = max([done[j] + (0.0 if o["eng"] == ops[j]["eng"] == "P" else LAT) for j in succ[i]] + [0.0]) + o["lat"]
-            c.append((max(st, free.get(o["eng"], 0.0) if o["eng"] != "R" else 0.0), -o["t"], i))
-        t0 = min(c)[0]
-        st, _, i = min((x for x in c if x[0] <= t0 + BWIN), key=lambda x: x[1:])
-        done[i] = free[ops[i]["eng"]] = st + ops[i]["cost"]
-        ready.discard(i)
-        for j in ops[i]["all"]:
-            left[j] -= 1
-            if not left[j]:
-                ready.add(j)
-    return done
-
-
-def forward(given):
-    ops = graph()
-    n = len(ops)
+def links(ops):
     hist, group, tiles = {}, {}, {}
     for i, o in enumerate(ops):
         if o["kind"] == "dma":
@@ -632,74 +641,261 @@ def forward(given):
                         hard.update(group[ops[j]["sem"]] if ops[j]["kind"] == "dma" else [j])
             h.append((i, c0, c1, wr))
         if o["kind"] == "recv":
-            soft.add(o["args"][2])
-        o["hard"], o["soft"], o["all"] = hard, soft, hard | soft
-    opens = {v[0]: k for k, v in tiles.items()}
-    succ = [[] for _ in range(n)]
+            soft.add(o["args"][1])
+        o["hard"], o["soft"], o["all"], o["next"] = hard, soft, hard | soft, []
     for i, o in enumerate(ops):
         for j in o["all"]:
-            succ[j].append(i)
-    prio = [0.0] * n
-    chain = [i for i, o in enumerate(ops) if o["outs"] and o["outs"][0][0] == "gk"]
-    nxt = dict(zip(chain, chain[1:]))
-    for i in range(n - 1, -1, -1):
-        prio[i] = ops[i]["cost"] + ops[i]["lat"] + max([prio[j] + LAT for j in succ[i]] + [prio[nxt[i]] + STRETCH * ops[i]["cost"] if i in nxt else 0.0])
-    prio = given or prio
+            ops[j]["next"].append(i)
+    return group, tiles
+
+
+def forward(ops, tiles, prio):
+    n = len(ops)
+    opens = {v[0]: k for k, v in tiles.items()}
     left = [len(o["all"]) for o in ops]
     ready = set(i for i in range(n) if left[i] == 0)
-    fin, issue = [None] * n, [None] * n
+    fin, start, can = [None] * n, [0.0] * n, [0.0] * n
+    eng, cost = [o["eng"] for o in ops], [o["cost"][0] for o in ops]
     free = {e: 0.0 for e in "VSPGYR"}
-    bank, held = {}, [None] * 8
-    order = []
+    held, order = [None] * 8, []
     while ready:
+        cand = []
+        for b in range(8):
+            if held[b] is None:
+                cand.append((0.0, b))
+            elif all(fin[j] is not None for j in tiles[held[b]]):
+                cand.append((max(fin[j] for j in tiles[held[b]]) + LAT, b))
         best = []
-        for i in sorted(ready):
-            o = ops[i]
-            st = 0.0
-            for j in o["hard"]:
-                st = max(st, fin[j] + LAT)
-            for j in o["soft"]:
-                st = max(st, issue[j] if o["eng"] == "P" else fin[j])
-            bk = None
+        for i in ready:
+            o, st = ops[i], can[i]
             if i in opens:
-                cand = []
-                for b in range(8):
-                    if held[b] is None:
-                        cand.append((0.0, b))
-                    elif all(fin[j] is not None for j in tiles[held[b]]):
-                        cand.append((max(fin[j] for j in tiles[held[b]]) + LAT, b))
                 if not cand:
                     continue
-                tb, bk = min(cand)
-                st = max(st, tb)
+                st = max(st, min(cand)[0])
             if o["eng"] == "?":
-                best.append((max(st, free["S"]), i, bk, 0, prio[i]))
-                best.append((max(st, free["V"]) + SHY, i, bk, 1, prio[i] - LOW))
+                best.append((max(st, free["S"]) + max(0.0, -o["shy"]), i, 0, prio[i]))
+                best.append((max(st, free["V"]) + max(0.0, o["shy"]), i, 1, prio[i]))
             else:
-                best.append((max(st, free[o["eng"]]) if o["eng"] != "R" else st, i, bk, None, prio[i]))
+                best.append((max(st, free[o["eng"]]) if o["eng"] != "R" else st, i, None, prio[i]))
         t0 = min(x[0] for x in best)
-        st, i, bk, alt = max((x for x in best if x[0] <= t0 + WIN), key=lambda x: x[4])[:4]
+        st, i, alt = max((x for x in best if x[0] <= t0 + WIN), key=lambda x: (x[3], -x[1]))[:3]
         o = ops[i]
         if alt is not None:
-            o["eng"], o["kind"], o["args"], o["cost"] = o["alt"][alt]
-            o["pick"] = alt
-            st -= SHY * alt
-        if bk is not None:
-            if held[bk] is not None:
-                o["hard"] = o["hard"] | set(tiles[held[bk]])
-            held[bk] = opens[i]
-            bank[opens[i]] = bk
-        issue[i] = st + o["cost"]
-        fin[i] = issue[i] + o["lat"]
-        o["t"] = st
-        free[o["eng"]] = issue[i]
+            eng[i], cost[i] = o["alt"][alt][0], o["alt"][alt][3][0]
+            st -= max(0.0, o["shy"] if alt else -o["shy"])
+        if i in opens:
+            held[min(cand)[1]] = opens[i]
+        start[i] = st
+        free[eng[i]] = st = st + cost[i]
+        fin[i] = st + o["lat"]
         order.append(i)
         ready.discard(i)
-        for j in succ[i]:
+        for j in o["next"]:
+            can[j] = max(can[j], fin[i] + LAT if i in ops[j]["hard"] else st if ops[j]["eng"] == "P" else fin[i])
             left[j] -= 1
             if left[j] == 0:
                 ready.add(j)
     assert len(order) == n
+    return max(fin), order, start, eng, cost
+
+
+def backward(ops, p):
+    start, eng, cost = p[2:5]
+    n = len(ops)
+    left = [len(o["next"]) for o in ops]
+    ready = set(i for i in range(n) if not left[i])
+    done, can, free = [0.0] * n, [o["lat"] for o in ops], {}
+    while ready:
+        c = [(max(can[i], free.get(eng[i], 0.0) if eng[i] != "R" else 0.0), -start[i], i) for i in ready]
+        t0 = min(c)[0]
+        st, _, i = min((x for x in c if x[0] <= t0 + BWIN), key=lambda x: x[1:])
+        done[i] = free[eng[i]] = st + cost[i]
+        ready.discard(i)
+        for j in ops[i]["all"]:
+            can[j] = max(can[j], done[i] + (0.0 if eng[i] == eng[j] == "P" else LAT) + ops[j]["lat"])
+            left[j] -= 1
+            if not left[j]:
+                ready.add(j)
+    return done
+
+
+def improve(ops, tiles, p):
+    n = len(ops)
+    reach, deps = [0] * n, []
+    for i, o in enumerate(ops):
+        keep, seen = [], 0
+        for j in sorted(o["all"], reverse=True):
+            if not seen >> j & 1 or ops[j]["lat"]:
+                keep.append((j, LAT + ops[j]["lat"] if j in o["hard"] else 0.0 if o["eng"] == "P" else ops[j]["lat"]))
+            seen |= reach[j] | 1 << j
+        reach[i] = seen
+        deps.append(keep)
+    uses, opens, names = [[] for _ in range(n)], {}, sorted(tiles)
+    for k, nm in enumerate(names):
+        opens[tiles[nm][0]] = k
+        for i in set(tiles[nm]):
+            uses[i].append(k)
+    size = [len(set(tiles[nm])) for nm in names]
+    users = [[j for j in set(tiles[nm]) if not any(reach[x] >> j & 1 for x in tiles[nm])] for nm in names]
+    outs = [i for i in range(n) if not ops[i]["next"]]
+
+    def one(order, eng, cost, a, old):
+        a -= a % MARK
+        end, why = old[1][:], old[2][:]
+        free, last, left, done, who, held, bank = [x.copy() for x in old[4][a]]
+        marks = {k: v for k, v in old[4].items() if k <= a}
+        for k in range(a, n):
+            if not k % MARK:
+                marks[k] = (free[:], last[:], left[:], done[:], who[:], held[:], bank.copy())
+            i = order[k]
+            e = eng[i]
+            st, w = free[e], last[e]
+            for j, d in deps[i]:
+                if end[j] + d > st:
+                    st, w = end[j] + d, j
+            if i in opens:
+                tb, bk = 1e18, -1
+                for b in range(8):
+                    h = held[b]
+                    if h < 0:
+                        tb, bk = -1.0, b
+                        break
+                    if not left[h] and done[h] < tb:
+                        tb, bk = done[h], b
+                if bk < 0:
+                    return None
+                if tb + LAT > st and tb >= 0:
+                    st, w = tb + LAT, who[held[bk]]
+                bank[i] = (bk, held[bk])
+                held[bk] = opens[i]
+            end[i] = st = st + cost[i]
+            why[i] = w
+            if e < 5:
+                free[e], last[e] = st, i
+            for x in uses[i]:
+                left[x] -= 1
+                if st > done[x]:
+                    done[x], who[x] = st, i
+        top = max(outs, key=lambda i: end[i] + ops[i]["lat"])
+        return end[top] + ops[top]["lat"], end, why, top, marks, bank
+
+    def again(order, eng, cost, bank, a, old):
+        a -= a % MARK
+        end, why, free, last = old[1][:], old[2][:], old[4][a][0][:], old[4][a][1][:]
+        marks = {k: v for k, v in old[4].items() if k <= a}
+        for k in range(a, n):
+            if not k % MARK:
+                marks[k] = (free[:], last[:])
+            i = order[k]
+            e = eng[i]
+            st, w = free[e], last[e]
+            for j, d in deps[i]:
+                if end[j] + d > st:
+                    st, w = end[j] + d, j
+            if i in bank and bank[i][1] >= 0:
+                for j in users[bank[i][1]]:
+                    if end[j] + LAT > st:
+                        st, w = end[j] + LAT, j
+            end[i] = st = st + cost[i]
+            why[i] = w
+            if e < 5:
+                free[e], last[e] = st, i
+        top = max(outs, key=lambda i: end[i] + ops[i]["lat"])
+        return end[top] + ops[top]["lat"], end, why, top, marks
+
+    def run(order, a, old):
+        first = one(order, eng, cost[0], a, old[0])
+        if first is None:
+            return None
+        r = [first] + [again(order, eng, cost[c], first[5], a, old[c]) for c in range(1, len(CASES))]
+        return r + [sum(x[0] / c[0] for x, c in zip(r, CASES)) / len(CASES)]
+
+    def turn_over(i):
+        eng[i] = 1 - eng[i]
+        for c in range(len(CASES)):
+            cost[c][i] = ops[i]["alt"][1 - eng[i]][3][c]
+
+    rng = np.random.default_rng(SEED)
+    order, eng = p[1][:], ["VSPGYR".index(e) for e in p[3]]
+    cost = [[(o["alt"][1 - eng[i]][3] if o["eng"] == "?" else o["cost"])[c] for i, o in enumerate(ops)] for c in range(len(CASES))]
+    blank = [0, [0.0] * n, [-1] * n, 0, {0: ([0.0] * 6, [-1] * 6, size[:], [0.0] * len(size), [-1] * len(size), [-1] * 8, {})}]
+    cur = run(order, 0, [blank] * len(CASES))
+    best = (cur, order, eng[:])
+    fresh = True
+    for turn in range(MOVES):
+        if fresh:
+            pos = [0] * n
+            for k, i in enumerate(order):
+                pos[i] = k
+            pairs = []
+            for c, x in enumerate(cur[:-1]):
+                i = x[3]
+                while x[2][i] >= 0:
+                    j = x[2][i]
+                    if eng[i] == eng[j] and not reach[i] >> j & 1:
+                        pairs.append((c, j, i))
+                    i = j
+            fresh = False
+        c, j, i = pairs[rng.integers(len(pairs))]
+        how, flip = rng.random(), None
+        if 0.4 < how < 0.65:
+            end, e = cur[c][1], eng[i]
+            can = max([end[x] + d for x, d in deps[i]] + [0.0])
+            k = pos[j] - 1
+            while k >= 0 and (eng[order[k]] != e or end[order[k]] > can and not reach[i] >> order[k] & 1):
+                if eng[order[k]] == e:
+                    j = order[k]
+                    if rng.random() < 0.15:
+                        break
+                k -= 1
+        if how < FLIP and (ops[i]["eng"] == "?" or ops[j]["eng"] == "?"):
+            flip = i if ops[i]["eng"] == "?" and (ops[j]["eng"] != "?" or how < FLIP / 2) else j
+            a, new = pos[flip], order
+            turn_over(flip)
+        elif how < 0.65:
+            a, b = pos[j], pos[i]
+            mid = order[a:b]
+            new = order[:a] + [x for x in mid if reach[i] >> x & 1] + [i] + [x for x in mid if not reach[i] >> x & 1] + order[b + 1:]
+        else:
+            a = pos[j]
+            b = min(n - 1, pos[i] + int(rng.integers(3) ** 2 * rng.integers(20)))
+            mid = order[a + 1:b + 1]
+            new = order[:a] + [x for x in mid if not reach[x] >> j & 1] + [j] + [x for x in mid if reach[x] >> j & 1] + order[b + 1:]
+        r = run(new, a, cur)
+        if r is not None and r[-1] <= cur[-1] + HEAT * (1 - turn / MOVES) * rng.random():
+            cur, order, fresh = r, new, True
+            if r[-1] < best[0][-1]:
+                best = (cur, order, eng[:])
+        elif flip is not None:
+            turn_over(flip)
+    cur, order, eng = best
+    bank = {names[opens[i]]: b for i, (b, h) in cur[0][5].items()}
+    more = {i: set(tiles[names[h]]) for i, (b, h) in cur[0][5].items() if h >= 0}
+    return [x[0] for x in cur[:-1]], order, cur[0][1], ["VSPGYR"[e] for e in eng], bank, more
+
+
+def plan():
+    ops = graph()
+    group, tiles = links(ops)
+    n = len(ops)
+    prio = [0.0] * n
+    chain = [i for i, o in enumerate(ops) if o["outs"] and o["outs"][0][0] == "gk"]
+    nxt = dict(zip(chain, chain[1:]))
+    for i in range(n - 1, -1, -1):
+        o = ops[i]
+        prio[i] = o["cost"][0] + o["lat"] + max([prio[j] + LAT for j in o["next"]] + [prio[nxt[i]] + STRETCH * o["cost"][0] if i in nxt else 0.0])
+    best = p = forward(ops, tiles, prio)
+    for _ in range(TURNS):
+        p = forward(ops, tiles, backward(ops, p))
+        if p[0] < best[0]:
+            best = p
+    end, order, done, eng, bank, more = improve(ops, tiles, best)
+    for i, o in enumerate(ops):
+        if o["eng"] == "?":
+            o["eng"], o["kind"], o["args"], o["cost"] = o["alt"][eng[i] == "V"]
+        o["hard"] = o["hard"] | more.get(i, set())
+        o["cost"] = o["cost"][0]
+        o["t"] = done[i] - o["cost"]
     place = {i: k for k, i in enumerate(order)}
     needed = set()
     for o in ops:
@@ -718,13 +914,13 @@ def forward(given):
         elif o["kind"] == "recv":
             o["sig"] = (o["sem"], None)
         elif o["kind"] == "send":
-            o["sig"] = ("out%d%d" % o["args"][:2], None)
+            o["sig"] = ("out" + o["args"][0], None)
         elif i in needed:
             count[o["eng"]] += 1
             o["sig"] = ("c" + o["eng"], count[o["eng"]])
         else:
             o["sig"] = None
-    return ops, order, bank, count, group, max(fin)
+    return ops, order, bank, count, group, end[0], end
 
 
 PLAN = []
@@ -764,12 +960,12 @@ def rank_program(g, core, T, topo):
     def sig(j):
         s, v = ops[j]["sig"]
         if ops[j]["kind"] == "recv":
-            v = n_in[ops[j]["args"][0]]
+            v = n_in[int(ops[j]["args"][0][0])]
         elif ops[j]["kind"] == "send":
-            v = n_out[ops[j]["args"][0]]
+            v = n_out[int(ops[j]["args"][0][0])]
         return s, v
 
-    seen = {}
+    seen, two = {}, 0
     for i in order:
         o = ops[i]
         k, a, e = o["kind"], o["args"], o["eng"]
@@ -796,38 +992,41 @@ def rank_program(g, core, T, topo):
         elif k == "ms":
             ins = q.memset(R(a[0]), a[1])
         elif k == "scan":
-            ins = q.tensor_tensor_scan(R(a[0]), R(a[1]), R(a[2]), 0.0, AL.mult, AL.add)
+            ins = q.tensor_tensor_scan(R(a[0]), R(a[1]), R(a[2]), R(a[3]), AL.mult, AL.add)
         elif k == "act":
             ins = q.activation(R(a[0]), R(a[1]), a[2], bias=R(a[3]), scale=R(a[4]))
+        elif k == "act2":
+            q.activation(R(a[0]), R(a[1]), AF.Abs).then_inc(T.sem["c2"], 1)
+            two += 1
+            q.wait_ge(T.sem["c2"], two)
+            ins = q.activation(R(a[0]), R(a[0]), AF.Sign)
         elif k == "mm":
-            ins = q.matmul(R(a[0]), R(a[1]), R(a[2]), a[3], a[4])
+            for x in a:
+                ins = q.matmul(R(x[0]), R(x[1]), R(x[2]), x[3], x[4])
         elif k == "iota":
             if SCRATCH[a[0][0]][2] == "int32":
                 ins = q.iota(R(a[0]), a[1], a[2], a[3])
             else:
                 ins = q.iota(R(a[0]), a[1], a[2], a[3], allow_small_or_imprecise_dtypes=True)
-        elif k == "put":
-            ins = q.affine_select(R(a[0]), R(a[0]), a[1], AL.not_equal, a[3], a[2], 1)
-        elif k == "keep":
-            ins = q.affine_select(R(a[0]), R(a[1]), a[2], AL.is_ge, 0.0, 0, a[3])
+        elif k == "sel":
+            ins = q.affine_select(R(a[0]), R(a[1]), a[2], a[3], a[4], a[5], a[6])
         elif k == "dma":
             q.dma_start(R(a[0]), R(a[1])).then_inc(T.sem[o["sem"]], 16)
             continue
         else:
-            t, j = a[0], a[1]
+            w, t = a[0], int(a[0][0])
             rid, pid = topo.addr(to[t])[:2]
             mask = sum(1 << x for x in lanes(core, to[t]))
-            q.remote_dma(R(a[3]), R(a[2]), T.sem["in%d%d" % (t, j)], T.sem["out%d%d" % (t, j)], pid, rid, mask)
+            q.remote_dma(R(a[2]), R(a[1]), T.sem["in" + w], T.sem["out" + w], pid, rid, mask)
             continue
         if o["sig"] is not None:
             ins.then_inc(T.sem[o["sig"][0]], 1)
     last = {"c" + e: count[e] for e in count}
     for s in group:
         last[s] = 16 * len(group[s])
-    for t in (0, 1):
-        for j in (0, 1):
-            last["in%d%d" % (t, j)] = n_in[t]
-            last["out%d%d" % (t, j)] = n_out[t]
+    for w in WRITES:
+        last["in" + w] = n_in[int(w[0])]
+        last["out" + w] = n_out[int(w[0])]
     for s in sorted(last):
         if not any(v >= last[s] for (e, s2), v in seen.items() if s2 == s):
             g.sync.wait_ge(T.sem[s], last[s])

import numpy as np
from concourse.mybir import AluOpType, ActivationFunctionType

AL = AluOpType
AF = ActivationFunctionType
W, Q, CAP, NRANK = 4096, 512, 192, 8
HASH = [[0, 96, 320, 512], [0, 224, 416, 512]]
KEYS = [list(range(0, Q + 1, 32))] * 2
PARTS = [[0, 112, 224, 320, 416, 512]] * 2
TAIL = [[0, 224, 416, 512]] * 2
SHUT = [0, 416, 512]
SOFT = 320
CH = 32
PACKS = [[(10, 0), (6, 16)], [(9, 0), (7, 16)], [(8, 0), (5, 16), (1, 8), (2, 9), (3, 10)]]
PLAIN = [16, 15, 14, 13, 12, 11, 4]
NP, NT = len(PACKS), len(PACKS) + len(PLAIN)
TAB, EXT = 256, 4352
BIG = 8192.0
SEG = [{"aO": 0, "aP": 512, "aX": 704, "P2": 896, "P1": 1408, "X0": 1920, "P0": 1920, "O": 1920, "On": 2432, "end": 2944},
       {"aP": 0, "aX": 192, "P2": 384, "P1": 896, "X0": 1408, "P0": 1920, "O": 2432, "On": 2944, "end": 3456}]
PECY, PEFIX, LAT, FIX, SFIX = 0.5, 10.0, 120.0, 60.0, 78.0
CASES = [(1.0, 1.56, 3.8), (1.3, 1.9, 5.0), (1.3, 1.2, 2.5)]
LOAD, SEND, FLY = 1.0, 1500.0, 1.0
LEAD, STRETCH, WIN, SHY, GSHY, NSHY, TURNS, BWIN = 128, 0.5, 40.0, 600.0, 1000.0, 1e6, 3, 40.0
MOVES, HEAT, FLIP, MARK, SEED = 30000, 60.0, 0.2, 64, 2

MATS = ["I", "NI", "IM", "J", "BD", "TRI", "TRI2", "NTRI", "SEL", "TRK", "WU", "WV",
        "DJ0", "DJ1", "DJ2", "DJ3", "DQ0", "DQ1", "DQ2", "DQ3", "DQ4", "DQ5", "DQ6", "DQ7", "MK0", "MK1"]
MATS += ["K%d" % _m for _t in PACKS for _m, _r in _t if _m > 3] + ["P%d" % _i for _i in range(NP)]
EARLY = ["NL0", "K1", "K2", "K3"] + ["CW%d" % _m for _m in sorted(PLAIN)] + ["C%d" % _i for _i in range(NP)] + ["NS2", "NL1"]
LATE = ["IO", "IC", "NC", "IH", "QN", "QP", "VAL", "NDR", "WNM", "LD6", "NRS", "PLA", "SG", "WHV", "WL", "WPL"]
MOFF = {}
GMW = VMW = 0
for _n in EARLY + LATE:
    MOFF[_n] = ("gm", GMW)
    GMW += 144 if _n[0] == "W" and _n != "WNM" or _n[:2] == "CW" else 128
for _n in MATS:
    MOFF[_n] = ("vm", VMW)
    VMW += 128

SCRATCH = {}
for _d, _l in (("bfloat16", (("gm", GMW), ("vm", VMW), ("iow", 176), ("iog", 128), ("ones", Q), ("raw", W), ("kt", W + CH), ("zt", EXT + Q),
                             ("qpi", Q), ("sw0", 2944), ("sw1", 3456), ("sb0", 384), ("sb1", 384), ("gk", 16 * Q), ("ne", NT * Q),
                             ("mt", Q), ("lt", Q), ("ab", 2 * Q), ("ee", 2 * Q), ("un", 288), ("zv", 2 * Q), ("ys", 2 * Q))),
               ("float32", (("I32", 128), ("cc", 32), ("mk", 64), ("iof", Q), ("nt", TAB + W + CH), ("ft", 2560), ("ns", Q), ("ue", Q),
                            ("xf", Q), ("wn", Q), ("pk", Q), ("nw0", 912), ("nw1", 912), ("nd2", Q), ("kp", 32), ("w4", 288),
                            ("st", 288), ("dc", 128), ("sm", 32), ("t4", 256))),
               ("int32", (("pi", 8), ("nki", 768), ("wti", 8), ("qni", Q), ("xi", 2 * Q))),
               ("uint16", (("hu", Q), ("hb", 32), ("ov", 32), ("po", 32), ("ol", 32), ("ow", 32), ("of", 96), ("oo", 32))),
               ("float16", (("hs", 2 * Q), ("tm", Q), ("nd0", Q), ("nd1", Q), ("rr", 2 * Q), ("ld", Q), ("sn0", 400), ("sn1", 400),
                            ("sh", 192), ("ar0", 208), ("ar1", 208), ("pt", 128), ("xv", 32)))):
    for _n, _c in _l:
        SCRATCH[_n] = ("sbuf", [128, _c], _d)
for _b in range(8):
    SCRATCH["ps%d" % _b] = ("psum", [128, 512], "float32")
WRITES = ["00", "01", "02", "10", "11"]
SEMAPHORES = ["cV", "cS", "cP", "cG", "c2", "l_qp", "l_wt", "l_qn", "l_nk", "l_s0", "l_s1", "l_s2", "l_s3", "l_nt", "z_a", "z_b",
              "o_p", "o_n"] + ["in" + _w for _w in WRITES] + ["out" + _w for _w in WRITES]
SIZE = {"bfloat16": 2, "float16": 2, "uint16": 2, "float32": 4, "int32": 4}


def A(name, c0, c1, st=1, p0=0, p1=128, ps=1):
    return (name, c0, c1, st, p0, p1, ps)


def B(name, i, k=1):
    return A(name, 32 * i, 32 * (i + k))


def IND(win, off):
    return ("#", win, off)


def M(name, rows=128, cols=128):
    b, c = MOFF[name]
    return A(b, c, c + cols, 1, 0, rows)


def MW(name, r):
    b, c = MOFF[name]
    return A(b, c + 15 - r, c + 143 - r)


def MC(name, c):
    b, o = MOFF[name]
    return A(b, o + c, o + 128, 16)


def cols(ap):
    if ap[0] == "#":
        return 16 * cols(ap[2])
    return len(range(ap[1], ap[2], ap[3]))


def is_ap(x):
    return isinstance(x, tuple)


def width(ap):
    if ap[0][0] in "#@":
        return 4
    return SIZE[SCRATCH[ap[0]][2]]


def spans(cuts):
    return list(zip(cuts, cuts[1:]))


def graph():
    ops = []

    def add(eng, kind, outs, ins, args, cost, sem=None, lat=0.0):
        ops.append({"eng": eng, "kind": kind, "outs": outs, "ins": ins, "args": args, "cost": cost, "sem": sem, "lat": lat})

    def price(fix, n, kind=0):
        return [fix + n * c[0] * (c[kind] if kind else 1.0) for c in CASES]

    def vcost(out, in0, per, fix=FIX):
        if out[0] == "#":
            return price(fix, cols(out), 2)
        if in0[0] == "#":
            return price(fix, cols(out), 1)
        return price(fix, max(64, cols(out) * per))

    def ts(out, in0, s1, s2, op0, op1=None):
        per = 0.5 if width(out) == 2 and width(in0) == 2 else 1
        add("V", "ts", [out], [in0] + [s for s in (s1, s2) if is_ap(s)], (out, in0, s1, s2, op0, op1), vcost(out, in0, per))

    def tt(out, in0, in1, op):
        per = 1 if "@" in (in0[0][0], in1[0][0]) else 2
        add("V", "tt", [out], [in0, in1], (out, in0, in1, op), vcost(out, in0, per))

    def cp(out, in0):
        per = 0.5 if width(out) == 2 and width(in0) == 2 else 1
        add("V", "cp", [out], [in0], (out, in0), vcost(out, in0, per))

    def ms(out, val):
        add("V", "ms", [out], [], (out, val), price(FIX, max(64, cols(out) * width(out) / 4)))

    def act(out, in0, func=AF.Identity, bias=0.0, scale=1.0):
        add("S", "act", [out], [in0] + [s for s in (bias, scale) if is_ap(s)], (out, in0, func, bias, scale), vcost(out, in0, 1, SFIX))

    def either(out, in0, bias=0.0, scale=1.0, func=AF.Identity, shy=None):
        act(out, in0, func, bias, scale)
        a = ops.pop()
        if func == AF.Abs:
            a["kind"], a["cost"] = "act2", [2 * c + LAT for c in a["cost"]]
            ts(out, in0, 0.0, None, AL.not_equal)
        elif func == AF.Sign:
            ts(out, in0, bias, 0.5, AL.add, AL.is_ge)
        elif func == AF.Relu and scale == -1.0:
            ts(out, in0, -1.0, 0.0, AL.mult, AL.max)
        elif func == AF.Relu:
            ts(out, in0, bias, 0.0, AL.add, AL.max)
        elif scale != 1.0 and bias != 0.0:
            ts(out, in0, scale, bias, AL.mult, AL.add)
        elif scale != 1.0:
            ts(out, in0, scale, None, AL.mult)
        elif bias != 0.0:
            ts(out, in0, bias, None, AL.add)
        else:
            cp(out, in0)
        b = ops.pop()
        a["alt"] = [(x["eng"], x["kind"], x["args"], x["cost"]) for x in (a, b)]
        a["eng"] = "?"
        a["shy"] = SHY if shy is None else shy
        ops.append(a)

    def mm(out, terms, first=True, last=True, after=()):
        for i, (l, r) in enumerate(terms):
            o = out[i] if isinstance(out, list) else out
            c = price(PEFIX, max(min(64, cols(l)), cols(r)) * PECY * (4 if width(r) == 4 else 1))
            add("P", "mm", [o], [l, r] + list(after), [(o, l, r, first and i == 0, last and i == len(terms) - 1)], c)

    def mmx(out, terms, first=True, last=True, after=()):
        k = len(ops)
        mm(out, terms, first, last, after)
        part = ops[k:]
        del ops[k:]
        add("P", "mm", [x for o in part for x in o["outs"]], [x for o in part for x in o["ins"]], [o["args"][0] for o in part],
            [sum(c) for c in zip(*[o["cost"] for o in part])])

    def iota(out, pat, base, cm):
        add("G", "iota", [out], [], (out, pat, base, cm), price(0, 160 + 2 * cols(out)))

    def sel(out, in0, pat, cmp, fill, base, cm):
        add("G", "sel", [out], [in0], (out, in0, pat, cmp, fill, base, cm), price(0, 210 + 2 * cols(out)))

    def put(ap, pat, base, val):
        sel(ap, ap, pat, AL.not_equal, float(val), base, 1)

    def keep(out, in0, pat, cm, base=0):
        sel(out, in0, pat, AL.is_ge, 0.0, base, cm)

    def ent(name, k, c, val):
        put(MC(name, c), [[-16, 8]], -k, val)

    def entrow(name, k, val):
        put(M(name), [[-16, 8], [0, 16]], -k, val)

    def dma(eng, out, in0, sem, ns, after=(), busy=60.0):
        add(eng, "dma", [out] if is_ap(out) else [], ([in0] if is_ap(in0) else []) + list(after), (out, in0), price(busy, 0), sem, ns * LOAD)

    def send(w, src, dst, ns):
        add("G", "send", [], [src], (w, src, dst), price(SEND, 0))
        add("R", "recv", [dst], [], (w, len(ops) - 1), price(0.0, 0), "in" + w, ns * FLY)

    nps = [0]

    def tile():
        nps[0] += 1
        return "@%d" % nps[0]

    def rows16(wide, src, c0, c1):
        return [(MW(wide, r), A(src, c0 + r, c1, 16)) for r in range(16)]

    col = lambda i: A("cc", i, i + 1)
    mkc = lambda m: A("mk", m, m + 1)
    nmk = lambda m: A("mk", 32 + m, 33 + m)
    PC, KC, GB, JC, THR, LTB, TA, DUMC, LDM, IXB = [col(i) for i in range(10)]
    W0, W1 = col(14), col(15)
    I32 = A("I32", 0, 128)

    dma("Y", A("qpi", 0, Q), "qp", "l_qp", 2200)
    dma("S", A("raw", 0, 1024), ["sen", 0, 1024], "l_s0", 2600)
    dma("Y", A("wti", 0, 2), "wt", "l_wt", 2000)
    dma("S", A("raw", 1024, 2048), ["sen", 1024, 2048], "l_s1", 3300)
    dma("Y", A("raw", 2048, 3072), ["sen", 2048, 3072], "l_s2", 4000)
    dma("Y", A("raw", 3072, 4096), ["sen", 3072, 4096], "l_s3", 4700)
    dma("Y", A("nki", 0, 256), "nk", "l_nk", 3000)
    for j in range(16):
        dma("YS"[j % 2], A("qni", 0, Q, 1, j, 128, 16), "qn", "l_qn", 2200)

    iota(A("pi", 0, 1), [[0, 1]], 0, 1)
    iota(A("iow", 0, 176), [[1, 176]], -16, 0)
    iota(A("iog", 0, 128), [[16, 8], [0, 16]], 0, 0)
    iota(A("iof", 0, 32), [[1, 32]], 0, 0)
    late = MOFF[LATE[0]][1]
    ms(A("gm", 0, 512), 0.0)
    ms(A("gm", 512, late), 0.0)
    ms(A("ee", 0, 384), 0.0)
    for a in range(late, GMW, 384):
        e = min(GMW, a + 384)
        dma("Y", A("gm", a, e), A("ee", 0, e - a), "z_a", 2200, [A("raw", 1024, 1025)], 600.0)
    ms(A("ones", 0, Q), 1.0)
    ts(A("pi", 1, 2), A("pi", 0, 1), 15, None, AL.bitwise_and)
    cp(A("cc", 0, 2), A("pi", 0, 2))
    act(GB, KC, AF.Identity, PC, -1.0)
    ts(A("mk", 0, 17), A("iof", 0, 17), KC, None, AL.is_gt)
    ts(A("mk", 32, 49), A("iof", 0, 17), KC, None, AL.is_le)
    ts(M("I"), A("iow", 16, 144), PC, None, AL.is_equal)
    ts(M("BD"), A("iog", 0, 128), GB, None, AL.is_equal)
    keep(M("TRI"), M("BD"), [[1, 128]], -1)
    keep(M("TRI2"), M("BD"), [[-1, 128]], 1)
    cp(A("cc", 14, 16), A("wti", 0, 2))
    ts(M("WU"), M("TRI"), W0, 256.0, AL.mult, AL.mult)
    ts(M("WV"), M("TRI"), W1, 256.0, AL.mult, AL.mult)
    for nm, v in (("IM", -4096.0), ("NI", -1.0)):
        either(M(nm), M("I"), 0.0, v)
    for nm, v in (("IC", BIG), ("IH", -1 / 32), ("NC", -BIG), ("IO", SEG[0]["On"] / BIG)):
        put(M(nm), [[-1, 128]], 0, v)
    either(I32, M("I"))
    either(M("SEL"), M("TRI2"), 0.0, -BIG / 2)
    put(M("SEL"), [[-1, 128]], 0, BIG / 2)
    either(M("NTRI"), M("TRI2"), 0.0, -1.0)
    either(M("TRK"), M("TRI2"), 0.0, -1.0)
    put(M("TRK"), [[-1, 128]], 0, -2048.0)
    act(JC, KC, AF.Identity, GB, -1.0)
    ts(M("J"), A("iow", 1, 129), JC, None, AL.is_equal)
    run = [m for m in PLAIN if m > 7]
    b, o = MOFF["CW%d" % min(run)]
    x = A(b, o + 15, o + 144 * len(run), 16)
    iota(x, [[0, 9 * len(run)]], 1, 0)
    keep(x, x, [[0, len(run)], [-16, 9]], 1)
    keep(x, x, [[1, len(run)], [16, 9]], -1, min(run) - 1)
    for m in PLAIN:
        if m not in run:
            b, o = MOFF["CW%d" % m]
            keep(A(b, o + 15, o + 143, 16), MC("BD", 0), [[16, 8]], -1, m - 1)
    for i, t in enumerate(PACKS):
        for m, r in t:
            x = MC("C%d" % i, m - 1)
            if m < 4:
                for k in range(m):
                    ent("K%d" % m, k, r, float(32 ** k))
                put(x, [[-16, 8]], -r, 1.0)
            elif r == 16:
                either(M("K%d" % m), M("J"), 0.0, mkc(m))
                keep(x, MC("BD", 0), [[-16, 8]], 1, m - 16)
            elif r == 0:
                either(M("K%d" % m), M("I"), 0.0, mkc(m))
                keep(x, MC("BD", 0), [[16, 8]], -1, m - 1)
            else:
                ts(M("K%d" % m), A("iow", 16 - r, 144 - r), PC, mkc(m), AL.is_equal, AL.mult)
                keep(x, MC("BD", 0), [[16, 8]], -1, r + m - 1)
                keep(x, x, [[-16, 8]], 1, -r)
    entrow("NL0", 4, 1184.0)
    entrow("NL0", 9, -2.0 ** 21)
    for i0 in range(0, NP, 4):
        p, k = tile(), min(4, NP - i0)
        for i in range(k):
            mm(A(p, 128 * i, 128 * i + 128), [(M("I"), M("K%d" % m)) for m, r in PACKS[i0 + i]])
        either(M("P%d" % i0, 128, 128 * k), A(p, 0, 128 * k))
    ts(A("pi", 2, 3), A("pi", 1, 2), 1, None, AL.add)
    ts(A("pi", 3, 4), A("pi", 2, 3), 2, None, AL.arith_shift_right)
    ts(THR, A("pi", 3, 4), 0.5, None, AL.add)
    act(LTB, KC, AF.Identity, 16.0, -1.0)
    act(TA, KC, AF.Identity, -8 * BIG, BIG / 2)
    ts(col(16), KC, 7.0, mkc(10), AL.is_equal, AL.add)
    act(DUMC, mkc(1), AF.Identity, col(16), -1.0)
    act(LDM, mkc(5), AF.Identity, mkc(6), -1.0)
    act(IXB, KC, AF.Identity, -2048.0, 256.0)
    iota(A("iof", 32, Q), [[1, Q - 32]], 32, 0)
    NEWF, NEWG, NEWL = ((1, 1), (0, -1), (13, 1)), ((3, 1), (10, 1), (12, -1)), ((2, 1), (10, 1), (11, -1))
    for c, terms in ((0, NEWF), (1, NEWF), (2, NEWG), (3, NEWG)):
        for k, v in terms:
            ent("NS2", k, c, v)
    either(M("NDR"), M("NS2"))
    for k, c, v in ((15, 4, 1), (14, 5, 1), (7, 6, 1), (6, 6, -1), (7, 7, 1), (6, 7, -1)):
        ent("NS2", k, c, v)
    for k, v in NEWL:
        entrow("NL1", k, 1184.0 * v)
    entrow("NL1", 9, -2.0 ** 21)
    entrow("QN", 6, -1 / 8)
    entrow("QP", 6, 1.0)
    entrow("VAL", 15, 64.0)
    for k, v in NEWL:
        ent("NDR", k, 4, v)
    for k, v in ((7, 512.0), (6, -512.0), (8, -512.0)):
        ent("NDR", k, 6, v)
        ent("WHV", k, 15, -v)
    for k, v in ((14, 1.0), (5, 1.0), (15, 2304.0), (4, 2816.0)):
        ent("WHV", k, 15, v)
    ent("WL", 5, 15, 1.0)
    ent("WL", 6, 15, 1.0)
    for k, c in ((0, 0), (0, 1), (0, 2), (0, 3), (0, 4), (5, 5)):
        ent("NRS", k, c, 1.0)
    ent("WPL", 15, 15, 1.0)
    entrow("PLA", 15, 1.0)
    b, o = MOFF["SG"]
    SELG, SELV = A(b, o, o + 8), A(b, o + 8, o + 16)
    put(SELG, [[-16, 8]], -15, -1.0)
    put(SELV, [[-16, 8]], -15, -BIG)
    put(SELV, [[-16, 8]], -4, -BIG)
    for c in (10, 13):
        for k, v in NEWG:
            ent("WNM", k, c, v)
    for c, v in ((0, 1), (1, 1), (4, 1), (5, 1), (8, 1), (9, 1), (14, -768), (15, 2)):
        ent("WNM", 9, c, v)
    ent("LD6", 5, 14, 1.0)
    ts(A("ld", 0, Q), A("iof", 0, Q), LDM, None, AL.mult)
    one32 = A("ones", 0, Q, 1, 0, 32)
    DJ, DQ = M("DJ0", 32, Q), [M("DQ0", 32, Q), M("DQ4", 32, Q)]
    sel(DJ, one32, [[0, 16], [-1, 32]], AL.is_equal, 0.0, 0, 1)
    for e in (0, 1):
        sel(DQ[e], one32, [[-2, 16], [0, 32]], AL.is_equal, 0.0, -e, 1)
        iota(M("MK%d" % e, 32), [[0, 128]], int(BIG), 0)
        keep(M("MK%d" % e, 32), M("MK%d" % e, 32), [[0, 8], [1, 16]], -1, 16 * e)

    s0, s1 = SEG
    ts(A("sw0", s0["O"], s0["On"]), A("qpi", 0, Q), 1 / 256, None, AL.mult)
    ts(A("nd0", 0, Q), A("qni", 0, Q), mkc(5), nmk(5), AL.mult, AL.add)
    send("02", A("sw0", s0["O"], s0["On"]), A("sw0", 0, Q), 4000)

    for j in range(8):
        c0, c1 = 512 * j, 512 * j + 512
        ts(A("zt", TAB + c0, TAB + c1), A("raw", c0, c1), 1 / 4096, -1 - 7.5 / 4096, AL.mult, AL.add)
        p = tile()
        mm(A(p, 0, Q), [(M("I"), A("raw", c0, c1)), (M("IM"), A("zt", TAB + c0, TAB + c1))])
        either(A("kt", c0, c1), A(p, 0, Q), -16.0, 1 / 256)
    ms(A("zt", 0, TAB), -1.0)
    ms(A("kt", W, W + CH), 0.0)
    ms(A("nt", TAB + W, TAB + W + CH), 0.0)
    dma("Y", A("pk", 0, Q), A("iof", 0, Q), "z_b", 2500)
    either(A("nt", 0, TAB), A("ones", 0, TAB), 0.0, DUMC)
    F = lambda i: A("ft", 256 * i, 256 * i + 256)
    raw, kind, node = [A("nki", 256 * i, 256 * i + 256) for i in range(3)]
    val, quo, low, nof, nq, nl, nv, vc, ix, one = [F(i) for i in range(10)]
    ts(kind, raw, 3, None, AL.bitwise_and)
    ts(node, raw, 2, None, AL.arith_shift_right)
    ts(val, kind, 3.0, None, AL.is_equal)
    ts(quo, kind, 1.0, None, AL.is_equal)
    ts(low, kind, 2.0, None, AL.is_lt)
    cp(nof, node)
    either(ix, A("iof", 0, 256), IXB)
    iota(one, [[0, 256]], 1, 0)
    p = tile()
    mm(A(p, 0, 256), [(I32, nof)])
    mm(A(p, 256, 512), [(I32, ix)])
    for o, f in ((nq, quo), (nl, low), (nv, val)):
        tt(o, f, A(p, 0, 256), AL.mult)
    tt(vc, val, A(p, 256, 512), AL.mult)
    rows = [val, one, quo, low, one, one, quo, low, quo, one, nof, nq, nl, nv, vc, val]
    for j in (1, 4, 5, 9, 0, 15, 2, 6, 8, 3, 7, 10, 11, 12, 13, 14):
        dma("Y", A("nt", TAB, TAB + W, 1, j, 128, 16), rows[j], "l_nt", 2200, [A("raw", 1024, 1025)], 700.0)

    for i, a in enumerate((384, s0["On"] - s0["aP"], s0["On"] - s0["aX"], 384, s1["On"], s1["On"] - s1["aX"], 2 * CAP, CAP)):
        iota(B("w4", i), [[16, 32]], a, 0)
    iota(B("w4", 8), [[0, 16], [16, 2]], W - 2048, 0)
    either(B("st", 0, 9), B("w4", 0, 9), KC)
    cp(B("sh", 0, 2), B("st", 6, 2))
    ts(B("sh", 4), B("st", 7), -1.0, Q - 1.0 + CAP, AL.mult, AL.add)
    iota(B("un", 5), [[0, 32]], CAP, 0)
    iota(B("un", 6), [[0, 32]], 2, 0)

    def hashes(t, s, c0, c1):
        n, C = c1 - c0, lambda nm, o=0: A(nm, o + c0, o + c1)
        P = C("sw%d" % t, SEG[t]["P1" if s else "P0"])
        p = tile()
        mm(A(p, 0, n), [(M("WU"), P)])
        mm(A(p, 256, 256 + n), [(M("WV"), P)])
        either(C("ue"), A(p, 0, n))
        tt(C("xf"), A(p, 256, 256 + n), C("ue"), AL.mult)
        p = tile()
        mm(A(p, 0, n), [(M("NL1"), C("rr")) if s else (M("NL0"), C("nd%d" % t))], after=[C("ue")])
        tt(C("xi"), A(p, 0, n), C("xf"), AL.add)
        ts(C("xi", Q), C("xi"), 5, W - 1, AL.arith_shift_right, AL.bitwise_and)
        cp(C("hu"), C("xi", Q))
        ts(C("hs", Q if (t, s) == (0, 0) else 0), C("hu"), -2048.0, None, AL.add)

    def step(t, s, c0, c1):
        n, sw, seg, nd = c1 - c0, "sw%d" % t, SEG[t], "nd%d" % t
        q0, q1 = c0 // 16, c1 // 16
        pin = seg["P1" if s else "P0"]
        C = lambda nm, o=0: A(nm, o + c0, o + c1)
        P, X, R = C(sw, pin), C(sw, seg["X0"]), C("rr", s * Q)
        pc = tile()
        for d0, d1 in spans([c for c in PARTS[s] if c0 <= c <= c1]):
            compare(pc, A(sw, pin + d0, pin + d1), c0, c1, d0, d1, [(M("VAL"), A("rr", d0, d1))] if s else [])
        act(C("mt"), A(pc, 0, n), AF.Sign, THR, -1.0)
        p = tile()
        mm(A(p, 0, n), [(M("TRI2"), C("mt"))])
        either(C("lt"), A(p, 0, n), LTB, func=AF.Sign)
        p = tile()
        mm(A(p, 0, n), [(M("SEL"), C("mt")), (M("I"), C("hs", Q if (t, s) == (0, 0) else 0))])
        ts(C("tm"), A(p, 0, n), TA, -2050.0, AL.add, AL.max)
        p = tile()
        mmx(A(p, 0, q1 - q0), rows16("CW16", "tm", c0, c1))
        hb = A("hb", q0, q1)
        ts(hb, A(p, 0, q1 - q0), 15 * 2050.0 + 2048 + TAB, None, AL.add)
        tt(R, IND(A("nt", 0, TAB + W), hb), C("ns") if s else C(nd), AL.mult)
        tt(C("ab"), IND(A("zt", 0, TAB + W), hb), C("lt"), AL.add)
        p = tile()
        if (t, s) == (0, 0):
            mm(A(p, 0, n), [(M("NI"), C("lt")), (M("I"), P)])
        else:
            mm(A(p, 0, n), [(M("I"), X), (M("NI"), P), (M("QP"), R)], after=[C("lt")])
            either(C("ab", Q), A(p, 0, n), -7 / 8, func=AF.Relu)
            p = tile()
            mm(A(p, 0, n), [(M("NI"), C("lt")), (M("I"), P), (M("QN"), R), (M("I"), C("ab", Q))], after=[R])
        tt(C(sw, seg["P2" if s else "P1"]), A(p, 0, n), C("ab"), AL.max)
        p = tile()
        if s == 0:
            mm(A(p, 0, n), [(M("NS2"), R)])
            either(C("ns"), A(p, 0, n), nmk(7))
        else:
            mm(A(p, 0, n), [(M("NDR"), R), (M("I"), C("ld"))], after=[R])
            either(C("nw%d" % t, 400), A(p, 0, n))

    def compare(pc, P, b0, b1, c0, c1, more):
        n = c1 - c0
        K = lambda m: A("gk", 16 * c0 + m - 1, 16 * c1, 16)
        NE = lambda i, k=1: A("ne", NT * c0 + i * n, NT * c0 + (i + k) * n)
        late = 16 * max(c0, c1 - LEAD)
        pp = tile()
        mm(A(pp, 0, n), [(M("NI"), P)], after=[A("gk", late, late + 1)])
        for i, m in enumerate(PLAIN):
            tt(NE(NP + i), K(m), A(pp, 0, n), AL.not_equal)
        per = -(-NP // -(-NP * n // 512))
        per = min(per, 512 // n)
        for i in range(0, NP, per):
            p, k = tile(), min(per, NP - i)
            for j in range(k):
                mmx(A(p, j * n, j * n + n), [(M("K%d" % m), K(m)) for m, r in PACKS[i + j]] + [(M("P%d" % (i + j)), P)])
            either(NE(i, k), A(p, 0, k * n), func=AF.Abs, shy=0.0 if more and c0 >= SOFT else -NSHY)
        mm(A(pc, c0 - b0, c1 - b0), [(MW("CW%d" % m, m - 1), NE(NP + i)) for i, m in enumerate(PLAIN)] + more
           + [(M("C%d" % i), NE(i)) for i in range(NP)], c0 == b0, c1 == b1)

    def close(t, c0, c1):
        sw, seg, nw = "sw%d" % t, SEG[t], "nw%d" % t
        n, q0, q1 = c1 - c0, c0 // 16, c1 // 16
        k = q1 - q0
        N = lambda nm, o=0: A(nm, o + q0, o + q1)
        p = tile()
        mmx(A(p, 0, k), rows16("WHV", "rr", Q + c0, Q + c1))
        ts(N("un"), A(p, 0, k), 0.0, None, AL.is_le)
        cp(N("ov"), A(p, 0, k))
        either(N("un", 128), A(p, 0, k), 0.0, -1.0, AF.Relu)
        init = A("un", 31 + q0, 32 + q0) if q0 else 0.0
        add("V", "scan", [N("un", 32)], [N("ones"), N("un")] + ([init] if q0 else []), (N("un", 32), N("ones"), N("un"), init), price(FIX, 64))
        tt(N("xv"), N("un"), N("sh", 128), AL.mult)
        p = tile()
        mm(A(p, 0, k), [(M("I"), N("sh", 128)), (M("NTRI"), N("un")), (M("NI"), N("xv")), (M("BD"), N("un", 32))], after=[N("un")])
        cp(N("po"), A(p, 0, k))
        cp(IND(A("pk", 0, Q), N("po")), A(nw, 400 + c0, 400 + c1))
        zv = A("zt", EXT + c0, EXT + c1) if t == 0 else A("zv", c0, c1)
        O = A(sw, seg["O"] + c0, seg["O"] + c1)
        either(zv, IND(A("zt", 0, EXT if t == 0 else EXT + Q), N("ov")))
        p = tile()
        mm(A(p, 0, n), [(M("I"), zv), (M("I"), O)])
        act(A("zv", Q + c0, Q + c1), A(p, 0, n), AF.Sign, 1 - 15.5 / 256)
        p = tile()
        mm(A(p, 0, n), [(M("IH"), A("zv", Q + c0, Q + c1)), (M("I"), zv), (M("I"), O)])
        either(A(sw, seg["On"] + c0, seg["On"] + c1), A(p, 0, n), 1 - 1 / 32)

    def places():
        p = tile()
        mmx(A(p, 0, 32), rows16("WPL", "hs", Q, 2 * Q))
        cp(B("sh", 5), A(p, 0, 32))
        p = tile()
        mmx([A(p, r, 128, 16, 0, 32) for r in range(16)], [(A("hs", Q + r, 2 * Q, 16), SELG) for r in range(16)])
        act(A("dc", 0, 128, 1, 0, 32), A(p, 0, 128, 1, 0, 32), AF.Identity, BIG)

    def write():
        O, un = SEG[0]["O"], B("un", 0)
        p = tile()
        mm(A(p, 0, Q), [(M("WNM"), A("rr", Q, 2 * Q)), (M("LD6"), A("ld", 0, Q))])
        either(A("wn", 0, Q), A(p, 0, Q))
        p = tile()
        mmx([A(p, r, 128, 16, 0, 32) for r in range(16)], [(A("rr", Q + r, 2 * Q, 16), SELV) for r in range(16)])
        pt = A("pt", 0, 128, 1, 0, 32)
        tt(pt, A(p, 0, 128, 1, 0, 32), A("dc", 0, 128, 1, 0, 32), AL.add)
        for e in (0, 1):
            p = tile()
            mm(A(p, 0, Q), [(M("PLA"), A("hs", Q, 2 * Q)), (M("MK%d" % e, 32), DJ), (pt, DQ[e])], after=[A("hb", 30, 32)])
            either(A("ee", e * Q, e * Q + Q), A(p, 0, Q), func=AF.Abs, shy=1e6 * e)
        p = tile()
        mmx(A(p, 0, 64), rows16("CW16", "ee", 0, 2 * Q))
        either(B("un", 7, 2), A(p, 0, 64), 16 * BIG, -BIG)
        p = tile()
        mm(A(p, 0, 32), [(M("I"), B("sh", 5)), (M("IC"), un), (M("I"), B("un", 7)), (M("I"), B("un", 8))], after=[B("un", 7)])
        tt(B("sm", 0), A(p, 0, 32), B("st", 8), AL.min)
        ts(A("ow", 0, 32), B("sm", 0), 2048.0, None, AL.add)
        for a in range(Q - CH, -1, -CH):
            off = A("ow", a // 16, (a + CH) // 16)
            cp(IND(A("kt", 0, W + CH), off), A("sw0", O + a, O + a + CH))
            cp(IND(A("nt", TAB, TAB + W + CH), off), A("wn", a, a + CH))

    def finish(t):
        sw, seg, nw, sb, sn, ar = "sw%d" % t, SEG[t], "nw%d" % t, "sb%d" % t, "sn%d" % t, "ar%d" % t
        un, sc, nl, gone = B("un", 0), B("un", 1), B("un", 2), B("un", 3)
        p = tile()
        mm(A(p, 128, 144), [(M("BD"), A("un", 48, 64))])
        mm(B(p, 0), [(M("BD"), sc), (M("TRK"), un)])
        ts(A(sn, 0, 16), A(p, 128, 144), float(CAP), None, AL.min)
        either(B("kp", 0), B(p, 0), 2047.0)
        ts(A(sn, 16, 208), A("pk", 0, CAP), mkc(6), None, AL.mult)
        cp(A(sn, 208, 400), A("pk", 0, CAP))
        send("%d0" % t, A(sn, 0, 208), A(ar, 0, 208), 2500)
        p = tile()
        mmx(A(p, 0, 24), rows16("WL", sn, 16, 400))
        cp(A("ol", 0, 24), A(p, 0, 24))
        either(A(sb, 0, 192), IND(A(sw, seg["P2"], seg["P2"] + Q), A("ol", 0, 12)))
        either(A(sb, 192, 384), IND(A(sw, seg["P2"], seg["P2"] + 1536), A("ol", 12, 24)))
        send("%d1" % t, A(sb, 0, 384), A(sw, seg["aP"], seg["P2"]), 3000)
        p = tile()
        mm(A(p, 0, CAP), [(M("NRS"), A(sn, 16, 208))])
        either(A(nw, 208, 400), A(p, 0, CAP))
        if t == 0:
            write()
        ts(nl, B("kp", 0), float(CAP), None, AL.is_ge)
        p = tile()
        mm(B(p, 0), [(M("I"), B("un", 5)), (M("BD"), sc), (M("NTRI"), un), (M("IC"), nl)], True, False, [nl])
        for i in (1, 2):
            mm(B(p, i), [(M("I"), B("sh", i - 1)), (M("IC"), B("un", 6)), (M("NC"), un), (M("NC"), nl)], False, False)
        mm(B(p, 2), [(M("I"), B("un", 4))], False, True)
        tt(A("t4", 0, 96), A(p, 0, 96), B("st", 3 * t, 3), AL.min)
        cp(A(nw, 0, 208), A(ar, 0, 208))
        ts(gone, B("kp", 0), A(nw, 15, 16), BIG, AL.is_ge, AL.mult)
        p = tile()
        for i in range(3):
            mm(B(p, i), [(M("BD"), sc), (M("NTRI"), un), (M("I"), gone)], i == 0, i == 2, [nl])
        tt(A("t4", 128, 224), A(p, 0, 96), A("t4", 0, 96), AL.min)
        cp(A("of", 0, 96), A("t4", 128, 224))
        nwin = A(nw, 16, 912)
        win = lambda a: A(sw, seg[a], seg["end"])
        if t == 0:
            for c0, c1 in spans(HASH[0]):
                off = lambda i: A("of", 32 * i + c0 // 16, 32 * i + c1 // 16)
                ts(A("nd1", c0, c1), IND(nwin, off(0)), mkc(6), nmk(6), AL.mult, AL.add)
                for i, a, x in ((1, "aP", "P0"), (2, "aX", "X0")):
                    either(A("sw1", s1[x] + c0, s1[x] + c1), IND(win(a), off(i)))
            p = tile()
            mmx(B(p, 0), rows16("WL", "nd1", 0, Q) + [(M("IO"), gone)])
            ts(A("oo", 0, 32), B(p, 0), -1.0, None, AL.add)
            either(A("sw1", s1["O"], s1["On"]), IND(win("aO"), A("oo", 0, 32)))
        else:
            either(A("nd2", 0, Q), IND(nwin, B("of", 0)))
            for h, k in ((0, 4), (Q, 2)):
                dma("Y", ["yn", h, h + Q], A("nd2", 0, Q, 1, k, 128, 16), "o_n", 2000)
            for j, a in ((0, "aP"), (1, "aX")):
                for h in (0, 256):
                    either(A("ys", j * Q + h, j * Q + h + 256), IND(win(a), A("of", 32 + 32 * j + h // 16, 48 + 32 * j + h // 16)), 0.0, 256.0)
            for h, e in ((0, "Y"), (Q, "S")):
                dma(e, ["yp", h, h + Q], A("ys", h, h + Q), "o_p", 2200)

    for t in (0, 1):
        for s in (0, 1):
            for c0, c1 in spans(HASH[s]):
                hashes(t, s, c0, c1)
            for a, e in spans(KEYS[s]):
                either(A("gk", 16 * a, 16 * e), IND(A("kt", 0, W), A("hu", a, e)), 0.0, -1.0, shy=GSHY)
            for c0, c1 in spans(TAIL[s]):
                step(t, s, c0, c1)
        if t == 0:
            places()
        for c0, c1 in spans(SHUT):
            close(t, c0, c1)
        finish(t)
    return ops


def links(ops):
    hist, group, tiles = {}, {}, {}
    for i, o in enumerate(ops):
        if o["kind"] == "dma":
            group.setdefault(o["sem"], []).append(i)
    for i, o in enumerate(ops):
        hard, soft = set(), set()
        acc = [(x[1] if x[0] == "#" else x, True) for x in o["outs"]] + [(x[1] if x[0] == "#" else x, False) for x in o["ins"]]
        acc += [(x[2], False) for x in o["outs"] + o["ins"] if x[0] == "#"]
        for a, wr in acc:
            nm, c0, c1 = a[0], a[1], a[2]
            h = hist.setdefault(nm, [])
            if nm[0] == "@":
                tiles.setdefault(nm, []).append(i)
                for j, _, _, w2 in h:
                    if j == i:
                        continue
                    if ops[j]["eng"] != o["eng"] or o["eng"] == "?":
                        hard.add(j)
                    elif o["eng"] == "P":
                        soft.add(j)
                    elif wr or w2:
                        hard.add(j)
            else:
                for j, d0, d1, w2 in h:
                    if j != i and (wr or w2) and d0 < c1 and c0 < d1:
                        if ops[j]["kind"] == "dma" and o["kind"] == "dma" and ops[j]["sem"] == o["sem"]:
                            continue
                        hard.update(group[ops[j]["sem"]] if ops[j]["kind"] == "dma" else [j])
            h.append((i, c0, c1, wr))
        if o["kind"] == "recv":
            soft.add(o["args"][1])
        o["hard"], o["soft"], o["all"], o["next"] = hard, soft, hard | soft, []
    for i, o in enumerate(ops):
        for j in o["all"]:
            ops[j]["next"].append(i)
    return group, tiles


def forward(ops, tiles, prio):
    n = len(ops)
    opens = {v[0]: k for k, v in tiles.items()}
    left = [len(o["all"]) for o in ops]
    ready = set(i for i in range(n) if left[i] == 0)
    fin, start, can = [None] * n, [0.0] * n, [0.0] * n
    eng, cost = [o["eng"] for o in ops], [o["cost"][0] for o in ops]
    free = {e: 0.0 for e in "VSPGYR"}
    held, order = [None] * 8, []
    while ready:
        cand = []
        for b in range(8):
            if held[b] is None:
                cand.append((0.0, b))
            elif all(fin[j] is not None for j in tiles[held[b]]):
                cand.append((max(fin[j] for j in tiles[held[b]]) + LAT, b))
        best = []
        for i in ready:
            o, st = ops[i], can[i]
            if i in opens:
                if not cand:
                    continue
                st = max(st, min(cand)[0])
            if o["eng"] == "?":
                best.append((max(st, free["S"]) + max(0.0, -o["shy"]), i, 0, prio[i]))
                best.append((max(st, free["V"]) + max(0.0, o["shy"]), i, 1, prio[i]))
            else:
                best.append((max(st, free[o["eng"]]) if o["eng"] != "R" else st, i, None, prio[i]))
        t0 = min(x[0] for x in best)
        st, i, alt = max((x for x in best if x[0] <= t0 + WIN), key=lambda x: (x[3], -x[1]))[:3]
        o = ops[i]
        if alt is not None:
            eng[i], cost[i] = o["alt"][alt][0], o["alt"][alt][3][0]
            st -= max(0.0, o["shy"] if alt else -o["shy"])
        if i in opens:
            held[min(cand)[1]] = opens[i]
        start[i] = st
        free[eng[i]] = st = st + cost[i]
        fin[i] = st + o["lat"]
        order.append(i)
        ready.discard(i)
        for j in o["next"]:
            can[j] = max(can[j], fin[i] + LAT if i in ops[j]["hard"] else st if ops[j]["eng"] == "P" else fin[i])
            left[j] -= 1
            if left[j] == 0:
                ready.add(j)
    assert len(order) == n
    return max(fin), order, start, eng, cost


def backward(ops, p):
    start, eng, cost = p[2:5]
    n = len(ops)
    left = [len(o["next"]) for o in ops]
    ready = set(i for i in range(n) if not left[i])
    done, can, free = [0.0] * n, [o["lat"] for o in ops], {}
    while ready:
        c = [(max(can[i], free.get(eng[i], 0.0) if eng[i] != "R" else 0.0), -start[i], i) for i in ready]
        t0 = min(c)[0]
        st, _, i = min((x for x in c if x[0] <= t0 + BWIN), key=lambda x: x[1:])
        done[i] = free[eng[i]] = st + cost[i]
        ready.discard(i)
        for j in ops[i]["all"]:
            can[j] = max(can[j], done[i] + (0.0 if eng[i] == eng[j] == "P" else LAT) + ops[j]["lat"])
            left[j] -= 1
            if not left[j]:
                ready.add(j)
    return done


def improve(ops, tiles, p):
    n = len(ops)
    reach, deps = [0] * n, []
    for i, o in enumerate(ops):
        keep, seen = [], 0
        for j in sorted(o["all"], reverse=True):
            if not seen >> j & 1 or ops[j]["lat"]:
                keep.append((j, LAT + ops[j]["lat"] if j in o["hard"] else 0.0 if o["eng"] == "P" else ops[j]["lat"]))
            seen |= reach[j] | 1 << j
        reach[i] = seen
        deps.append(keep)
    uses, opens, names = [[] for _ in range(n)], {}, sorted(tiles)
    for k, nm in enumerate(names):
        opens[tiles[nm][0]] = k
        for i in set(tiles[nm]):
            uses[i].append(k)
    size = [len(set(tiles[nm])) for nm in names]
    users = [[j for j in set(tiles[nm]) if not any(reach[x] >> j & 1 for x in tiles[nm])] for nm in names]
    outs = [i for i in range(n) if not ops[i]["next"]]

    def one(order, eng, cost, a, old):
        a -= a % MARK
        end, why = old[1][:], old[2][:]
        free, last, left, done, who, held, bank = [x.copy() for x in old[4][a]]
        marks = {k: v for k, v in old[4].items() if k <= a}
        for k in range(a, n):
            if not k % MARK:
                marks[k] = (free[:], last[:], left[:], done[:], who[:], held[:], bank.copy())
            i = order[k]
            e = eng[i]
            st, w = free[e], last[e]
            for j, d in deps[i]:
                if end[j] + d > st:
                    st, w = end[j] + d, j
            if i in opens:
                tb, bk = 1e18, -1
                for b in range(8):
                    h = held[b]
                    if h < 0:
                        tb, bk = -1.0, b
                        break
                    if not left[h] and done[h] < tb:
                        tb, bk = done[h], b
                if bk < 0:
                    return None
                if tb + LAT > st and tb >= 0:
                    st, w = tb + LAT, who[held[bk]]
                bank[i] = (bk, held[bk])
                held[bk] = opens[i]
            end[i] = st = st + cost[i]
            why[i] = w
            if e < 5:
                free[e], last[e] = st, i
            for x in uses[i]:
                left[x] -= 1
                if st > done[x]:
                    done[x], who[x] = st, i
        top = max(outs, key=lambda i: end[i] + ops[i]["lat"])
        return end[top] + ops[top]["lat"], end, why, top, marks, bank

    def again(order, eng, cost, bank, a, old):
        a -= a % MARK
        end, why, free, last = old[1][:], old[2][:], old[4][a][0][:], old[4][a][1][:]
        marks = {k: v for k, v in old[4].items() if k <= a}
        for k in range(a, n):
            if not k % MARK:
                marks[k] = (free[:], last[:])
            i = order[k]
            e = eng[i]
            st, w = free[e], last[e]
            for j, d in deps[i]:
                if end[j] + d > st:
                    st, w = end[j] + d, j
            if i in bank and bank[i][1] >= 0:
                for j in users[bank[i][1]]:
                    if end[j] + LAT > st:
                        st, w = end[j] + LAT, j
            end[i] = st = st + cost[i]
            why[i] = w
            if e < 5:
                free[e], last[e] = st, i
        top = max(outs, key=lambda i: end[i] + ops[i]["lat"])
        return end[top] + ops[top]["lat"], end, why, top, marks

    def run(order, a, old):
        first = one(order, eng, cost[0], a, old[0])
        if first is None:
            return None
        r = [first] + [again(order, eng, cost[c], first[5], a, old[c]) for c in range(1, len(CASES))]
        return r + [sum(x[0] / c[0] for x, c in zip(r, CASES)) / len(CASES)]

    def turn_over(i):
        eng[i] = 1 - eng[i]
        for c in range(len(CASES)):
            cost[c][i] = ops[i]["alt"][1 - eng[i]][3][c]

    rng = np.random.default_rng(SEED)
    order, eng = p[1][:], ["VSPGYR".index(e) for e in p[3]]
    cost = [[(o["alt"][1 - eng[i]][3] if o["eng"] == "?" else o["cost"])[c] for i, o in enumerate(ops)] for c in range(len(CASES))]
    blank = [0, [0.0] * n, [-1] * n, 0, {0: ([0.0] * 6, [-1] * 6, size[:], [0.0] * len(size), [-1] * len(size), [-1] * 8, {})}]
    cur = run(order, 0, [blank] * len(CASES))
    best = (cur, order, eng[:])
    fresh = True
    for turn in range(MOVES):
        if fresh:
            pos = [0] * n
            for k, i in enumerate(order):
                pos[i] = k
            pairs = []
            for c, x in enumerate(cur[:-1]):
                i = x[3]
                while x[2][i] >= 0:
                    j = x[2][i]
                    if eng[i] == eng[j] and not reach[i] >> j & 1:
                        pairs.append((c, j, i))
                    i = j
            fresh = False
        c, j, i = pairs[rng.integers(len(pairs))]
        how, flip = rng.random(), None
        if 0.4 < how < 0.65:
            end, e = cur[c][1], eng[i]
            can = max([end[x] + d for x, d in deps[i]] + [0.0])
            k = pos[j] - 1
            while k >= 0 and (eng[order[k]] != e or end[order[k]] > can and not reach[i] >> order[k] & 1):
                if eng[order[k]] == e:
                    j = order[k]
                    if rng.random() < 0.15:
                        break
                k -= 1
        if how < FLIP and (ops[i]["eng"] == "?" or ops[j]["eng"] == "?"):
            flip = i if ops[i]["eng"] == "?" and (ops[j]["eng"] != "?" or how < FLIP / 2) else j
            a, new = pos[flip], order
            turn_over(flip)
        elif how < 0.65:
            a, b = pos[j], pos[i]
            mid = order[a:b]
            new = order[:a] + [x for x in mid if reach[i] >> x & 1] + [i] + [x for x in mid if not reach[i] >> x & 1] + order[b + 1:]
        else:
            a = pos[j]
            b = min(n - 1, pos[i] + int(rng.integers(3) ** 2 * rng.integers(20)))
            mid = order[a + 1:b + 1]
            new = order[:a] + [x for x in mid if not reach[x] >> j & 1] + [j] + [x for x in mid if reach[x] >> j & 1] + order[b + 1:]
        r = run(new, a, cur)
        if r is not None and r[-1] <= cur[-1] + HEAT * (1 - turn / MOVES) * rng.random():
            cur, order, fresh = r, new, True
            if r[-1] < best[0][-1]:
                best = (cur, order, eng[:])
        elif flip is not None:
            turn_over(flip)
    cur, order, eng = best
    bank = {names[opens[i]]: b for i, (b, h) in cur[0][5].items()}
    more = {i: set(tiles[names[h]]) for i, (b, h) in cur[0][5].items() if h >= 0}
    return [x[0] for x in cur[:-1]], order, cur[0][1], ["VSPGYR"[e] for e in eng], bank, more


def plan():
    ops = graph()
    group, tiles = links(ops)
    n = len(ops)
    prio = [0.0] * n
    chain = [i for i, o in enumerate(ops) if o["outs"] and o["outs"][0][0] == "gk"]
    nxt = dict(zip(chain, chain[1:]))
    for i in range(n - 1, -1, -1):
        o = ops[i]
        prio[i] = o["cost"][0] + o["lat"] + max([prio[j] + LAT for j in o["next"]] + [prio[nxt[i]] + STRETCH * o["cost"][0] if i in nxt else 0.0])
    best = p = forward(ops, tiles, prio)
    for _ in range(TURNS):
        p = forward(ops, tiles, backward(ops, p))
        if p[0] < best[0]:
            best = p
    end, order, done, eng, bank, more = improve(ops, tiles, best)
    for i, o in enumerate(ops):
        if o["eng"] == "?":
            o["eng"], o["kind"], o["args"], o["cost"] = o["alt"][eng[i] == "V"]
        o["hard"] = o["hard"] | more.get(i, set())
        o["cost"] = o["cost"][0]
        o["t"] = done[i] - o["cost"]
    place = {i: k for k, i in enumerate(order)}
    needed = set()
    for o in ops:
        last = {}
        for j in o["hard"]:
            e = ops[j]["eng"]
            if e not in last or place[j] > place[last[e]]:
                last[e] = j
        needed.update(last.values())
        o["hard"] = set(j for j in o["hard"] if ops[j]["kind"] in ("dma", "recv", "send") or j in last.values())
    count = {e: 0 for e in "VSPG"}
    for i in order:
        o = ops[i]
        if o["kind"] == "dma":
            o["sig"] = (o["sem"], 16 * len(group[o["sem"]]))
        elif o["kind"] == "recv":
            o["sig"] = (o["sem"], None)
        elif o["kind"] == "send":
            o["sig"] = ("out" + o["args"][0], None)
        elif i in needed:
            count[o["eng"]] += 1
            o["sig"] = ("c" + o["eng"], count[o["eng"]])
        else:
            o["sig"] = None
    return ops, order, bank, count, group, end[0], end


PLAN = []


def rank_program(g, core, T, topo):
    rank = T.rank_of(core)
    if rank is None:
        return
    if not PLAN:
        PLAN.append(plan())
    ops, order, bank, count, group = PLAN[0][:5]
    queue = {"V": g.vector, "S": g.scalar, "P": g.tensor, "G": g, "Y": g.sync}

    def lanes(src, dst):
        return topo.engines(src, dst)[:8]

    to = [T.cores[(rank + 1 + t) % NRANK] for t in (0, 1)]
    frm = [T.cores[(rank - 1 - t) % NRANK] for t in (0, 1)]
    n_out = [len(lanes(core, c)) for c in to]
    n_in = [len(lanes(c, core)) for c in frm]

    def R(x):
        if isinstance(x, str):
            return T[x][:]
        if isinstance(x, list):
            return T[x[0]][:, x[1]:x[2]]
        if not is_ap(x):
            return x
        if x[0] == "#":
            return R(x[1]).indirect(R(x[2]))
        nm = "ps%d" % bank[x[0]] if x[0][0] == "@" else x[0]
        ps = slice(x[4], x[5], x[6]) if x[6] != 1 else slice(x[4], x[5])
        cs = slice(x[1], x[2], x[3]) if x[3] != 1 else slice(x[1], x[2])
        return T[nm][ps, cs]

    def sig(j):
        s, v = ops[j]["sig"]
        if ops[j]["kind"] == "recv":
            v = n_in[int(ops[j]["args"][0][0])]
        elif ops[j]["kind"] == "send":
            v = n_out[int(ops[j]["args"][0][0])]
        return s, v

    seen, two = {}, 0
    for i in order:
        o = ops[i]
        k, a, e = o["kind"], o["args"], o["eng"]
        if k == "recv":
            continue
        q = queue[e]
        want = {}
        for j in o["hard"]:
            s, v = sig(j)
            want[s] = max(want.get(s, 0), v)
        for s in sorted(want):
            if seen.get((e, s), 0) < want[s]:
                q.wait_ge(T.sem[s], want[s])
                seen[(e, s)] = want[s]
        if k == "ts":
            if a[5] is None:
                ins = q.tensor_scalar(R(a[0]), R(a[1]), R(a[2]), None, a[4])
            else:
                ins = q.tensor_scalar(R(a[0]), R(a[1]), R(a[2]), R(a[3]), a[4], a[5])
        elif k == "tt":
            ins = q.tensor_tensor(R(a[0]), R(a[1]), R(a[2]), a[3])
        elif k == "cp":
            ins = q.tensor_copy(R(a[0]), R(a[1]))
        elif k == "ms":
            ins = q.memset(R(a[0]), a[1])
        elif k == "scan":
            ins = q.tensor_tensor_scan(R(a[0]), R(a[1]), R(a[2]), R(a[3]), AL.mult, AL.add)
        elif k == "act":
            ins = q.activation(R(a[0]), R(a[1]), a[2], bias=R(a[3]), scale=R(a[4]))
        elif k == "act2":
            q.activation(R(a[0]), R(a[1]), AF.Abs).then_inc(T.sem["c2"], 1)
            two += 1
            q.wait_ge(T.sem["c2"], two)
            ins = q.activation(R(a[0]), R(a[0]), AF.Sign)
        elif k == "mm":
            for x in a:
                ins = q.matmul(R(x[0]), R(x[1]), R(x[2]), x[3], x[4])
        elif k == "iota":
            if SCRATCH[a[0][0]][2] == "int32":
                ins = q.iota(R(a[0]), a[1], a[2], a[3])
            else:
                ins = q.iota(R(a[0]), a[1], a[2], a[3], allow_small_or_imprecise_dtypes=True)
        elif k == "sel":
            ins = q.affine_select(R(a[0]), R(a[1]), a[2], a[3], a[4], a[5], a[6])
        elif k == "dma":
            q.dma_start(R(a[0]), R(a[1])).then_inc(T.sem[o["sem"]], 16)
            continue
        else:
            w, t = a[0], int(a[0][0])
            rid, pid = topo.addr(to[t])[:2]
            mask = sum(1 << x for x in lanes(core, to[t]))
            q.remote_dma(R(a[2]), R(a[1]), T.sem["in" + w], T.sem["out" + w], pid, rid, mask)
            continue
        if o["sig"] is not None:
            ins.then_inc(T.sem[o["sig"][0]], 1)
    last = {"c" + e: count[e] for e in count}
    for s in group:
        last[s] = 16 * len(group[s])
    for w in WRITES:
        last["in" + w] = n_in[int(w[0])]
        last["out" + w] = n_out[int(w[0])]
    for s in sorted(last):
        if not any(v >= last[s] for (e, s2), v in seen.items() if s2 == s):
            g.sync.wait_ge(T.sem[s], last[s])
